import numpy as np
import ml_dtypes


def mxq(x, axis, fmt="e4m3"):
    dtype, down = {"e4m3": (ml_dtypes.float8_e4m3fn, 7), "e5m2": (ml_dtypes.float8_e5m2, 14)}[fmt]
    v = np.moveaxis(np.asarray(x, np.float32).astype(ml_dtypes.bfloat16).astype(np.float64), axis, -1)
    blocks = v.reshape(v.shape[:-1] + (-1, 32))
    amax = np.abs(blocks).max(-1, keepdims=True)
    byte = np.maximum(np.where(amax > 0, np.frexp(amax)[1] - 1 + 127, 0) - down, 1)
    scale = np.exp2(byte - 127.0)
    codes = (blocks / scale).astype(np.float32).astype(dtype).astype(np.float64)
    return np.moveaxis((codes * scale).reshape(v.shape), -1, axis)


WIDE = False


def mx_kscale(k):
    if not WIDE:
        return np.ones(k)
    levels = np.array([10, -10, 5, -5, 0])
    if k % 512:
        return np.exp2(np.random.permutation(np.resize(levels, k // 32))).repeat(32)
    a = np.empty((k // 512, 16))
    for p in range(k // 512):
        a[p, :8] = np.random.permutation(np.resize(levels, 8))
        for g in range(8):
            far = levels[np.abs(levels - a[p, g]) >= 10]
            a[p, g + 8] = far[np.random.randint(len(far))]
    return np.exp2(a.ravel()).repeat(32)


def f64(x):
    return np.asarray(x).astype(np.float64)


def striped8(idx):
    return np.concatenate([v.reshape(-1, 16).T for v in idx]).astype(np.uint16)


def unstriped8(offs):
    return np.stack([offs[16 * g:16 * g + 16].T.reshape(-1) for g in range(8)]).astype(np.int64)


E2M1 = np.array([0.0, 0.5, 1.0, 1.5, 2.0, 3.0, 4.0, 6.0, -0.0, -0.5, -1.0, -1.5, -2.0, -3.0, -4.0, -6.0])


def pack_weight(w, fmt):
    k, n = w.shape
    w = f64(np.asarray(w, np.float32).astype(ml_dtypes.bfloat16)).reshape(k // 32, 32, n)
    amax = np.abs(w).max(1)
    if fmt == "e4m3":
        byte = np.frexp(amax)[1] - 1 + 127 - 7
    else:
        mant, ex = np.frexp(amax / 6.0)
        byte = np.where(mant > 0.5, ex, ex - 1) + 127
    byte = np.clip(np.where(amax > 0, byte, 1), 1, 254)
    scaled = (w * np.exp2(127.0 - byte)[:, None, :]).reshape(k, n).astype(np.float32)
    by_word = np.ascontiguousarray(scaled.reshape(k // 512, 128, 4, n).transpose(0, 1, 3, 2))
    if fmt == "e4m3":
        words = by_word.astype(ml_dtypes.float8_e4m3fn).view(np.uint8)
    else:
        c = by_word.astype(ml_dtypes.float4_e2m1fn).view(np.uint8) & 0xF
        words = (c[..., 0::2] | (c[..., 1::2] << 4)).reshape(k // 512, 128, 2 * n)
    return np.ascontiguousarray(words), np.ascontiguousarray(byte.astype(np.uint8).reshape(k // 512, 16, n))


def unpack_weight(words, scales, fmt):
    g, _, n = scales.shape
    words = np.ascontiguousarray(words).reshape(g, 128, n, -1)
    if fmt == "e4m3":
        vals = words.view(ml_dtypes.float8_e4m3fn).astype(np.float64)
    else:
        nib = np.empty((g, 128, n, 4), np.uint8)
        nib[..., 0::2] = words & 0xF
        nib[..., 1::2] = words >> 4
        vals = E2M1[nib]
    vals = vals * np.repeat(np.exp2(scales.astype(np.float64) - 127.0), 8, axis=1)[..., None]
    return vals.transpose(0, 1, 3, 2).reshape(g * 512, n)


K, R, M, T, S = 1536, 512, 1024, 1024, 512


def setup_inputs():
    n = np.random.standard_normal
    s = mx_kscale(K)[:, None]
    u = mx_kscale(R)[:, None]
    p_w4 = pack_weight(n((K, M)) / np.sqrt(K) / s, "e2m1")
    return {
        "xT": (n((K, T)) * s).astype(np.float32),
        "w4_words": p_w4[0],
        "w4_scales": p_w4[1],
        "down": (n((K, R)) / np.sqrt(K) / s * u.T).astype(np.float32),
        "up": (0.5 * n((R, M)) / np.sqrt(R) / u).astype(np.float32),
        "wgt": np.repeat(np.random.uniform(0.5, 2.0, (8, S)), 16, axis=0).astype(np.float32),
        "offs": striped8(np.stack([np.random.permutation(T)[:S] for _ in range(8)])),
    }


def reference(xT, w4_words, w4_scales, down, up, wgt, offs):
    idx = unstriped8(offs)
    group = np.arange(K) % 512 // 64
    xg = f64(wgt)[np.arange(K) // 4 % 128] * f64(xT)[np.arange(K)[:, None], idx[group]]
    xT_ = mxq(xg, 0, "e4m3")
    w4_ = unpack_weight(w4_words, w4_scales, "e2m1")
    down_ = mxq(f64(down), 0, "e4m3")
    up_ = mxq(f64(up), 0, "e4m3")
    h_ = mxq(down_.T @ xT_, 0, "e4m3")
    y = w4_.T @ xT_ + up_.T @ h_
    return y

@@ -1,0 +1,328 @@
+from contextlib import ExitStack
+
+import concourse.mybir as mybir
+
+K, R, M, T, S = 1536, 512, 1024, 1024, 512
+FLOPS = 2 * S * (K * R + K * M + R * M)
+
+F32 = mybir.dt.float32
+BF16 = mybir.dt.bfloat16
+U32 = mybir.dt.uint32
+I32 = mybir.dt.int32
+U16 = mybir.dt.uint16
+U8 = mybir.dt.uint8
+E4M3 = mybir.dt.float8_e4m3fn_x4
+E2M1 = mybir.dt.float4_e2m1fn_x4
+MULT = mybir.AluOpType.mult
+
+P = 128
+PASSES = K // 512
+HALF = S // 2
+EARLY = 4
+U_COLS = 256
+
+
+def tile_list_hlora_none_kernel(tc, xT, w4_words, w4_scales, down, up, wgt, offs, out):
+    nc = tc.nc
+    with ExitStack() as ctx:
+        keep = ctx.enter_context(tc.tile_pool(name="keep", bufs=1))
+        psum = ctx.enter_context(tc.psum_pool(name="psum", bufs=1))
+
+        offsets = keep.tile([P, S // 16], U16, name="offsets")
+        weights = keep.tile([P, S], F32, name="weights")
+        x = [[keep.tile([P, T], F32, name=f"x{a}{t}") for t in range(4)] for a in range(PASSES)]
+        picked = [keep.tile([P, 4, S], F32, name=f"picked{a}") for a in range(PASSES)]
+        x_grouped = [keep.tile([P, S, 4], BF16, name=f"xgrouped{a}", align_bytes=64) for a in range(PASSES)]
+        x_codes = keep.tile([P, PASSES, S], U32, name="xcodes", align_bytes=64)
+        x_scales = keep.tile([P, PASSES, S], U8, name="xscales", align_bytes=64)
+        d_raw = [keep.tile([P, 4, R], F32, name=f"draw{a}") for a in range(PASSES)]
+        d_grouped = [keep.tile([P, R * 4], BF16, name=f"dgrouped{a}", align_bytes=64) for a in range(PASSES)]
+        d_codes = keep.tile([P, PASSES, R], U32, name="dcodes", align_bytes=64)
+        d_scales = keep.tile([P, PASSES, R], U8, name="dscales", align_bytes=64)
+        u_raw = [keep.tile([P, 4, U_COLS], F32, name=f"uraw{c}") for c in range(M // U_COLS)]
+        u_grouped = {c: keep.tile([P, U_COLS, 4], BF16, name=f"ugrouped{c}", align_bytes=64) for c in [0,1]}
+        u_codes = keep.tile([P, M], U32, name="ucodes", align_bytes=64)
+        u_scales = keep.tile([P, M], U8, name="uscales", align_bytes=64)
+        w_codes = keep.tile([P, PASSES, 2 * M], U8, name="wcodes", align_bytes=64)
+        w_scales = keep.tile([P, PASSES, M], U8, name="wscales", align_bytes=64)
+        h_flat = keep.tile([P, 4, S], BF16, name="hflat", align_bytes=64)
+        h_grouped = keep.tile([P, S, 4], BF16, name="hgrouped", align_bytes=64)
+        h_codes = keep.tile([P, S], U32, name="hcodes", align_bytes=64)
+        h_scales = keep.tile([P, S], U8, name="hscales", align_bytes=64)
+        staged = [keep.tile([P, S], F32, name=f"staged{n}") for n in range(8)]
+
+        nc.sync.dma_start(offsets[:], offs)
+        nc.sync.dma_start(weights[:, 0:HALF], wgt[:, 0:HALF])
+        nc.gpsimd.memset(w_scales[:].bitcast(I32), 0)
+        for q in range(4):
+            nc.gpsimd.dma_start(
+                out=w_scales[32 * q : 32 * q + 4].bitcast(I32),
+                in_=w4_scales[:, 4 * q : 4 * q + 4, :].bitcast(I32).rearrange("a q c -> q a c"),
+            )
+
+        def load_x(a, t):
+            nc.sync.dma_start(out=x[a][t][:], in_=xT[512 * a : 512 * a + 512, :].rearrange("(p t) c -> p t c", t=4)[:, t, :])
+
+        def load_d(a):
+            nc.sync.dma_start(out=d_raw[a][:], in_=down[512 * a : 512 * a + 512, :].rearrange("(p t) r -> p t r", t=4))
+
+        def load_w(a0, a1, n0, n1):
+            nc.sync.dma_start(
+                out=w_codes[:].bitcast(I32)[:, a0:a1, 64 * n0 : 64 * n1],
+                in_=w4_words.bitcast(I32).rearrange("a p c -> p a c")[:, a0:a1, 64 * n0 : 64 * n1],
+            )
+
+        def load_u(c):
+            nc.sync.dma_start(out=u_raw[c][:], in_=up.rearrange("(p t) n -> p t n", t=4)[:, :, U_COLS * c : U_COLS * c + U_COLS])
+
+        load_x(0, 0)
+        nc.sync.dma_start(weights[:, HALF:S], wgt[:, HALF:S])
+        load_x(0, 1)
+        load_x(0, 2)
+        load_x(0, 3)
+        load_x(1, 0)
+        load_x(1, 1)
+        load_x(1, 2)
+        load_x(1, 3)
+        load_x(2, 0)
+        load_d(0)
+        load_x(2, 1)
+        load_x(2, 2)
+        load_d(1)
+        load_x(2, 3)
+        load_d(2)
+        load_w(0, 1, 0, EARLY)
+        load_u(0)
+        load_w(1, 2, 0, EARLY)
+        load_w(0, 3, EARLY, 8)
+        load_w(2, 3, 0, EARLY)
+        load_u(1)
+        load_u(2)
+        load_u(3)
+
+        def gather(a, t, h):
+            cols = slice(h * HALF, (h + 1) * HALF)
+            nc.vector.tensor_tensor(
+                picked[a][:, t, cols],
+                x[a][t][:].indirect(offsets[:, h * HALF // 16 : (h + 1) * HALF // 16]),
+                weights[:, cols],
+                MULT,
+            )
+
+        def copy_on(engine):
+            return nc.scalar.copy if engine == "S" else nc.vector.tensor_copy
+
+        def group_x(a, c0, c1, engine):
+            copy_on(engine)(
+                out=x_grouped[a][:, c0:c1, :].rearrange("p (c i) t -> p c t i", i=4),
+                in_=picked[a][:, :, c0:c1].rearrange("p t (c i) -> p c t i", i=4),
+            )
+
+        def quantize_x(a):
+            nc.vector.quantize_mx(
+                out=x_codes[:, a, :].bitcast(E4M3), scales=x_scales[:, a, :], in_=x_grouped[a][:].rearrange("p c t -> p (c t)")
+            )
+
+        def group_d(a, m0, m1, engine):
+            copy_on(engine)(
+                out=d_grouped[a][:].rearrange("p (t m j) -> p m t j", t=4, j=4)[:, m0:m1],
+                in_=d_raw[a][:].rearrange("p j (m t) -> p m t j", t=4)[:, m0:m1],
+            )
+
+        def quantize_d(a):
+            nc.vector.quantize_mx(out=d_codes[:, a, :].bitcast(E4M3), scales=d_scales[:, a, :], in_=d_grouped[a][:])
+
+        def group_u(c, c0, c1, engine):
+            copy_on(engine)(
+                out=u_grouped[c][:, c0:c1, :].rearrange("p (c i) t -> p c t i", i=4),
+                in_=u_raw[c][:, :, c0:c1].rearrange("p t (c i) -> p c t i", i=4),
+            )
+
+        def quantize_u(c):
+            cols = slice(U_COLS * c, U_COLS * c + U_COLS)
+            nc.vector.quantize_mx(
+                out=u_codes[:, cols].bitcast(E4M3), scales=u_scales[:, cols], in_=u_grouped[c][:].rearrange("p c t -> p (c t)")
+            )
+
+        acc = {}
+
+        def base(n, a):
+            if a == 0:
+                acc[n] = psum.tile([P, S], F32, name=f"acc{n}" if n < EARLY else f"bank{n - 4}")
+            nc.tensor.matmul_mx(
+                out=acc[n][:],
+                lhsT=w_codes[:, a, 256 * n : 256 * n + 256].bitcast(E2M1),
+                lhsT_scale=w_scales[:, a, 128 * n : 128 * n + 128],
+                rhs=x_codes[:, a, :].bitcast(E4M3),
+                rhs_scale=x_scales[:, a, :],
+                start=(a == 0),
+                stop=False,
+            )
+
+        h_bank = {}
+
+        def low_rank(t, a):
+            if a == 0:
+                h_bank[t] = psum.tile([P, S], F32, name=f"bank{t}")
+            nc.tensor.matmul_mx(
+                out=h_bank[t][:],
+                lhsT=d_codes[:, a, 128 * t : 128 * t + 128].bitcast(E4M3),
+                lhsT_scale=d_scales[:, a, 128 * t : 128 * t + 128],
+                rhs=x_codes[:, a, :].bitcast(E4M3),
+                rhs_scale=x_scales[:, a, :],
+                start=(a == 0),
+                stop=(a == PASSES - 1),
+            )
+
+        def empty_h(t, engine):
+            copy_on(engine)(out=h_flat[:, t, :], in_=h_bank[t][:])
+
+        def group_h(c0, c1, engine):
+            copy_on(engine)(
+                out=h_grouped[:, c0:c1, :].rearrange("p (c i) t -> p c t i", i=4),
+                in_=h_flat[:, :, c0:c1].rearrange("p t (c i) -> p c t i", i=4),
+            )
+
+        def quantize_h():
+            nc.vector.quantize_mx(out=h_codes[:].bitcast(E4M3), scales=h_scales[:], in_=h_grouped[:].rearrange("p c t -> p (c t)"))
+
+        def finish(n):
+            nc.tensor.matmul_mx(
+                out=acc[n][:],
+                lhsT=u_codes[:, 128 * n : 128 * n + 128].bitcast(E4M3),
+                lhsT_scale=u_scales[:, 128 * n : 128 * n + 128],
+                rhs=h_codes[:].bitcast(E4M3),
+                rhs_scale=h_scales[:],
+                start=False,
+                stop=True,
+            )
+
+        def empty_out(n, c0, c1, engine):
+            copy_on(engine)(out=staged[n][:, c0:c1], in_=acc[n][:, c0:c1])
+
+        def store(n):
+            nc.sync.dma_start(out=out[128 * n : 128 * n + 128, :], in_=staged[n][:])
+
+        gather(0, 0, 0)
+        gather(0, 0, 1)
+        gather(0, 1, 0)
+        gather(0, 1, 1)
+        gather(0, 2, 1)
+        gather(0, 2, 0)
+        gather(0, 3, 1)
+        gather(0, 3, 0)
+        group_x(0, HALF, S, "S")
+        gather(1, 0, 0)
+        gather(1, 0, 1)
+        group_x(0, 0, HALF, "S")
+        gather(1, 1, 0)
+        gather(1, 2, 0)
+        gather(1, 2, 1)
+        gather(1, 3, 1)
+        gather(1, 1, 1)
+        gather(2, 0, 0)
+        group_x(1, HALF, S, "S")
+        gather(2, 0, 1)
+        quantize_x(0)
+        group_d(0, 0, 96, "S")
+        group_d(0, 96, 128, "V")
+        gather(1, 3, 0)
+        gather(2, 1, 0)
+        gather(2, 1, 1)
+        group_x(1, 0, HALF, "S")
+        gather(2, 2, 0)
+        gather(2, 2, 1)
+        quantize_x(1)
+        quantize_d(0)
+        group_d(1, 0, 96, "S")
+        group_d(1, 96, 128, "V")
+        low_rank(0, 0)
+        low_rank(2, 0)
+        gather(2, 3, 0)
+        low_rank(1, 0)
+        low_rank(3, 0)
+        gather(2, 3, 1)
+        group_x(2, 0, HALF, "S")
+        quantize_d(1)
+        group_x(2, HALF, S, "V")
+        low_rank(1, 1)
+        group_d(2, 0, 64, "S")
+        low_rank(3, 1)
+        group_d(2, 64, 128, "V")
+        low_rank(0, 1)
+        low_rank(2, 1)
+        quantize_x(2)
+        base(1, 0)
+        base(2, 0)
+        group_u(0, 0, 192, "S")
+        base(3, 0)
+        quantize_d(2)
+        base(0, 0)
+        base(2, 1)
+        group_u(0, 192, 256, "V")
+        base(1, 1)
+        low_rank(1, 2)
+        quantize_u(0)
+        low_rank(3, 2)
+        empty_h(1, "V")
+        low_rank(2, 2)
+        empty_h(3, "S")
+        low_rank(0, 2)
+        base(3, 1)
+        empty_h(2, "V")
+        base(0, 1)
+        empty_h(0, "S")
+        base(2, 2)
+        group_u(1, 64, 256, "V")
+        base(7, 0)
+        base(6, 0)
+        group_u(1, 0, 64, "S")
+        base(7, 1)
+        group_h(128, 512, "V")
+        group_h(0, 128, "S")
+        base(4, 0)
+        base(0, 2)
+        base(3, 2)
+        quantize_u(1)
+        base(1, 2)
+        held = keep.tile([P, 2, U_COLS, 4], BF16, name="hflat", align_bytes=64)
+        u_grouped[2] = held[:, 0]
+        u_grouped[3] = held[:, 1]
+        group_u(2, 0, 256, "S")
+        quantize_h()
+        base(5, 0)
+        base(6, 1)
+        base(5, 1)
+        group_u(3, 0, 256, "V")
+        finish(0)
+        finish(1)
+        empty_out(0, HALF, S, "V")
+        empty_out(0, 0, HALF, "S")
+        store(0)
+        finish(3)
+        base(5, 2)
+        quantize_u(2)
+        empty_out(1, 0, S, "S")
+        store(1)
+        finish(2)
+        empty_out(3, 0, S, "V")
+        store(3)
+        base(6, 2)
+        finish(5)
+        empty_out(2, 0, S, "S")
+        store(2)
+        quantize_u(3)
+        base(7, 2)
+        base(4, 1)
+        empty_out(5, 0, S, "V")
+        store(5)
+        finish(7)
+        finish(6)
+        empty_out(7, 0, S, "V")
+        store(7)
+        base(4, 2)
+        empty_out(6, 0, S, "S")
+        store(6)
+        finish(4)
+        empty_out(4, 0, S, "V")
+        store(4)

@@ -17,9 +17,14 @@ MULT = mybir.AluOpType.mult
 
 P = 128
 PASSES = K // 512
-HALF = S // 2
+TILES = M // P
 EARLY = 4
-U_COLS = 256
+CHUNK = 128
+CHUNKS = S // CHUNK
+U_COLS = 512
+X_SPLIT = 176
+D_SPLIT = 56
+U_SPLIT = 256
 
 
 def tile_list_hlora_none_kernel(tc, xT, w4_words, w4_scales, down, up, wgt, offs, out):
@@ -33,26 +38,24 @@ def tile_list_hlora_none_kernel(tc, xT, w4_words, w4_scales, down, up, wgt, offs
         x = [[keep.tile([P, T], F32, name=f"x{a}{t}") for t in range(4)] for a in range(PASSES)]
         picked = [keep.tile([P, 4, S], F32, name=f"picked{a}") for a in range(PASSES)]
         x_grouped = [keep.tile([P, S, 4], BF16, name=f"xgrouped{a}", align_bytes=64) for a in range(PASSES)]
-        x_codes = keep.tile([P, PASSES, S], U32, name="xcodes", align_bytes=64)
-        x_scales = keep.tile([P, PASSES, S], U8, name="xscales", align_bytes=64)
+        x_codes = [keep.tile([P, S], U32, name=f"xcodes{a}", align_bytes=64) for a in range(PASSES)]
+        x_scales = [keep.tile([P, S], U8, name=f"xscales{a}", align_bytes=64) for a in range(PASSES)]
         d_raw = [keep.tile([P, 4, R], F32, name=f"draw{a}") for a in range(PASSES)]
         d_grouped = [keep.tile([P, R * 4], BF16, name=f"dgrouped{a}", align_bytes=64) for a in range(PASSES)]
-        d_codes = keep.tile([P, PASSES, R], U32, name="dcodes", align_bytes=64)
-        d_scales = keep.tile([P, PASSES, R], U8, name="dscales", align_bytes=64)
+        d_codes = [keep.tile([P, R], U32, name=f"dcodes{a}", align_bytes=64) for a in range(PASSES)]
+        d_scales = [keep.tile([P, R], U8, name=f"dscales{a}", align_bytes=64) for a in range(PASSES)]
         u_raw = [keep.tile([P, 4, U_COLS], F32, name=f"uraw{c}") for c in range(M // U_COLS)]
-        u_grouped = {c: keep.tile([P, U_COLS, 4], BF16, name=f"ugrouped{c}", align_bytes=64) for c in [0,1]}
-        u_codes = keep.tile([P, M], U32, name="ucodes", align_bytes=64)
-        u_scales = keep.tile([P, M], U8, name="uscales", align_bytes=64)
-        w_codes = keep.tile([P, PASSES, 2 * M], U8, name="wcodes", align_bytes=64)
+        u_grouped = [keep.tile([P, U_COLS, 4], BF16, name=f"ugrouped{c}", align_bytes=64) for c in range(M // U_COLS)]
+        u_codes = [keep.tile([P, U_COLS], U32, name=f"ucodes{c}", align_bytes=64) for c in range(M // U_COLS)]
+        u_scales = [keep.tile([P, U_COLS], U8, name=f"uscales{c}", align_bytes=64) for c in range(M // U_COLS)]
+        w_codes = [keep.tile([P, PASSES, 2 * P * EARLY], U8, name=f"wcodes{g}", align_bytes=64) for g in range(2)]
         w_scales = keep.tile([P, PASSES, M], U8, name="wscales", align_bytes=64)
-        h_flat = keep.tile([P, 4, S], BF16, name="hflat", align_bytes=64)
         h_grouped = keep.tile([P, S, 4], BF16, name="hgrouped", align_bytes=64)
         h_codes = keep.tile([P, S], U32, name="hcodes", align_bytes=64)
         h_scales = keep.tile([P, S], U8, name="hscales", align_bytes=64)
-        staged = [keep.tile([P, S], F32, name=f"staged{n}") for n in range(8)]
+        staged = [keep.tile([P, S], F32, name=f"staged{n}") for n in range(TILES)]
 
         nc.sync.dma_start(offsets[:], offs)
-        nc.sync.dma_start(weights[:, 0:HALF], wgt[:, 0:HALF])
         nc.gpsimd.memset(w_scales[:].bitcast(I32), 0)
         for q in range(4):
             nc.gpsimd.dma_start(
@@ -66,62 +69,46 @@ def tile_list_hlora_none_kernel(tc, xT, w4_words, w4_scales, down, up, wgt, offs
         def load_d(a):
             nc.sync.dma_start(out=d_raw[a][:], in_=down[512 * a : 512 * a + 512, :].rearrange("(p t) r -> p t r", t=4))
 
-        def load_w(a0, a1, n0, n1):
+        def load_w(g):
             nc.sync.dma_start(
-                out=w_codes[:].bitcast(I32)[:, a0:a1, 64 * n0 : 64 * n1],
-                in_=w4_words.bitcast(I32).rearrange("a p c -> p a c")[:, a0:a1, 64 * n0 : 64 * n1],
+                out=w_codes[g][:].bitcast(I32),
+                in_=w4_words.bitcast(I32).rearrange("a p c -> p a c")[:, :, 64 * EARLY * g : 64 * EARLY * (g + 1)],
             )
 
         def load_u(c):
             nc.sync.dma_start(out=u_raw[c][:], in_=up.rearrange("(p t) n -> p t n", t=4)[:, :, U_COLS * c : U_COLS * c + U_COLS])
 
-        load_x(0, 0)
-        nc.sync.dma_start(weights[:, HALF:S], wgt[:, HALF:S])
-        load_x(0, 1)
-        load_x(0, 2)
-        load_x(0, 3)
-        load_x(1, 0)
-        load_x(1, 1)
-        load_x(1, 2)
-        load_x(1, 3)
-        load_x(2, 0)
-        load_d(0)
-        load_x(2, 1)
-        load_x(2, 2)
-        load_d(1)
-        load_x(2, 3)
-        load_d(2)
-        load_w(0, 1, 0, EARLY)
+        for a in range(PASSES):
+            for t in range(4):
+                if a > 0 and t == 2:
+                    load_d(a - 1)
+                if (a, t) == (PASSES - 1, 3):
+                    load_w(0)
+                load_x(a, t)
+                if (a, t) == (0, 0):
+                    nc.sync.dma_start(weights[:], wgt)
+        load_d(PASSES - 1)
         load_u(0)
-        load_w(1, 2, 0, EARLY)
-        load_w(0, 3, EARLY, 8)
-        load_w(2, 3, 0, EARLY)
+        load_w(1)
         load_u(1)
-        load_u(2)
-        load_u(3)
 
-        def gather(a, t, h):
-            cols = slice(h * HALF, (h + 1) * HALF)
-            nc.vector.tensor_tensor(
-                picked[a][:, t, cols],
-                x[a][t][:].indirect(offsets[:, h * HALF // 16 : (h + 1) * HALF // 16]),
-                weights[:, cols],
-                MULT,
-            )
+        def gather(a, t):
+            nc.vector.tensor_tensor(picked[a][:, t, :], x[a][t][:].indirect(offsets[:]), weights[:], MULT)
 
         def copy_on(engine):
             return nc.scalar.copy if engine == "S" else nc.vector.tensor_copy
 
-        def group_x(a, c0, c1, engine):
+        def interleave(dst, src, c0, c1, engine):
             copy_on(engine)(
-                out=x_grouped[a][:, c0:c1, :].rearrange("p (c i) t -> p c t i", i=4),
-                in_=picked[a][:, :, c0:c1].rearrange("p t (c i) -> p c t i", i=4),
+                out=dst[:, c0:c1, :].rearrange("p (c i) t -> p c t i", i=4),
+                in_=src[:, :, c0:c1].rearrange("p t (c i) -> p c t i", i=4),
             )
 
+        def quantize(codes, scales, grouped):
+            nc.vector.quantize_mx(out=codes.bitcast(E4M3), scales=scales, in_=grouped)
+
         def quantize_x(a):
-            nc.vector.quantize_mx(
-                out=x_codes[:, a, :].bitcast(E4M3), scales=x_scales[:, a, :], in_=x_grouped[a][:].rearrange("p c t -> p (c t)")
-            )
+            quantize(x_codes[a][:], x_scales[a][:], x_grouped[a][:].rearrange("p c t -> p (c t)"))
 
         def group_d(a, m0, m1, engine):
             copy_on(engine)(
@@ -130,199 +117,101 @@ def tile_list_hlora_none_kernel(tc, xT, w4_words, w4_scales, down, up, wgt, offs
             )
 
         def quantize_d(a):
-            nc.vector.quantize_mx(out=d_codes[:, a, :].bitcast(E4M3), scales=d_scales[:, a, :], in_=d_grouped[a][:])
-
-        def group_u(c, c0, c1, engine):
-            copy_on(engine)(
-                out=u_grouped[c][:, c0:c1, :].rearrange("p (c i) t -> p c t i", i=4),
-                in_=u_raw[c][:, :, c0:c1].rearrange("p t (c i) -> p c t i", i=4),
-            )
+            quantize(d_codes[a][:], d_scales[a][:], d_grouped[a][:])
 
         def quantize_u(c):
-            cols = slice(U_COLS * c, U_COLS * c + U_COLS)
-            nc.vector.quantize_mx(
-                out=u_codes[:, cols].bitcast(E4M3), scales=u_scales[:, cols], in_=u_grouped[c][:].rearrange("p c t -> p (c t)")
-            )
+            quantize(u_codes[c][:], u_scales[c][:], u_grouped[c][:].rearrange("p c t -> p (c t)"))
 
         acc = {}
 
         def base(n, a):
             if a == 0:
-                acc[n] = psum.tile([P, S], F32, name=f"acc{n}" if n < EARLY else f"bank{n - 4}")
+                acc[n] = psum.tile([P, S], F32, name=f"acc{n}" if n < EARLY else f"bank{n - EARLY}")
+            g, m = divmod(n, EARLY)
             nc.tensor.matmul_mx(
                 out=acc[n][:],
-                lhsT=w_codes[:, a, 256 * n : 256 * n + 256].bitcast(E2M1),
+                lhsT=w_codes[g][:, a, 256 * m : 256 * m + 256].bitcast(E2M1),
                 lhsT_scale=w_scales[:, a, 128 * n : 128 * n + 128],
-                rhs=x_codes[:, a, :].bitcast(E4M3),
-                rhs_scale=x_scales[:, a, :],
+                rhs=x_codes[a][:].bitcast(E4M3),
+                rhs_scale=x_scales[a][:],
                 start=(a == 0),
                 stop=False,
             )
 
-        h_bank = {}
+        h_bank = [psum.tile([P, 4, CHUNK], F32, name=f"bank{q}") for q in range(CHUNKS)]
 
-        def low_rank(t, a):
-            if a == 0:
-                h_bank[t] = psum.tile([P, S], F32, name=f"bank{t}")
-            nc.tensor.matmul_mx(
-                out=h_bank[t][:],
-                lhsT=d_codes[:, a, 128 * t : 128 * t + 128].bitcast(E4M3),
-                lhsT_scale=d_scales[:, a, 128 * t : 128 * t + 128],
-                rhs=x_codes[:, a, :].bitcast(E4M3),
-                rhs_scale=x_scales[:, a, :],
-                start=(a == 0),
-                stop=(a == PASSES - 1),
-            )
+        def low_rank(q, a):
+            cols = slice(CHUNK * q, CHUNK * q + CHUNK)
+            for t in range(4):
+                nc.tensor.matmul_mx(
+                    out=h_bank[q][:, t, :],
+                    lhsT=d_codes[a][:, 128 * t : 128 * t + 128].bitcast(E4M3),
+                    lhsT_scale=d_scales[a][:, 128 * t : 128 * t + 128],
+                    rhs=x_codes[a][:, cols].bitcast(E4M3),
+                    rhs_scale=x_scales[a][:, cols],
+                    start=(a == 0 and t == 0),
+                    stop=(a == PASSES - 1 and t == 3),
+                )
 
-        def empty_h(t, engine):
-            copy_on(engine)(out=h_flat[:, t, :], in_=h_bank[t][:])
+        def empty_h(q, engine):
+            copy_on(engine)(out=h_grouped[:, CHUNK * q : CHUNK * q + CHUNK, :], in_=h_bank[q][:].rearrange("p t c -> p c t"))
 
-        def group_h(c0, c1, engine):
-            copy_on(engine)(
-                out=h_grouped[:, c0:c1, :].rearrange("p (c i) t -> p c t i", i=4),
-                in_=h_flat[:, :, c0:c1].rearrange("p t (c i) -> p c t i", i=4),
-            )
+        def quantize_h(half):
+            cols = slice(256 * half, 256 * half + 256)
+            quantize(h_codes[:, cols], h_scales[:, cols], h_grouped[:, cols, :].rearrange("p c t -> p (c t)"))
 
-        def quantize_h():
-            nc.vector.quantize_mx(out=h_codes[:].bitcast(E4M3), scales=h_scales[:], in_=h_grouped[:].rearrange("p c t -> p (c t)"))
-
-        def finish(n):
+        def finish(n, engine):
+            c, m = divmod(128 * n, U_COLS)
             nc.tensor.matmul_mx(
                 out=acc[n][:],
-                lhsT=u_codes[:, 128 * n : 128 * n + 128].bitcast(E4M3),
-                lhsT_scale=u_scales[:, 128 * n : 128 * n + 128],
+                lhsT=u_codes[c][:, m : m + 128].bitcast(E4M3),
+                lhsT_scale=u_scales[c][:, m : m + 128],
                 rhs=h_codes[:].bitcast(E4M3),
                 rhs_scale=h_scales[:],
                 start=False,
                 stop=True,
             )
-
-        def empty_out(n, c0, c1, engine):
-            copy_on(engine)(out=staged[n][:, c0:c1], in_=acc[n][:, c0:c1])
-
-        def store(n):
+            copy_on(engine)(out=staged[n][:], in_=acc[n][:])
             nc.sync.dma_start(out=out[128 * n : 128 * n + 128, :], in_=staged[n][:])
 
-        gather(0, 0, 0)
-        gather(0, 0, 1)
-        gather(0, 1, 0)
-        gather(0, 1, 1)
-        gather(0, 2, 1)
-        gather(0, 2, 0)
-        gather(0, 3, 1)
-        gather(0, 3, 0)
-        group_x(0, HALF, S, "S")
-        gather(1, 0, 0)
-        gather(1, 0, 1)
-        group_x(0, 0, HALF, "S")
-        gather(1, 1, 0)
-        gather(1, 2, 0)
-        gather(1, 2, 1)
-        gather(1, 3, 1)
-        gather(1, 1, 1)
-        gather(2, 0, 0)
-        group_x(1, HALF, S, "S")
-        gather(2, 0, 1)
-        quantize_x(0)
-        group_d(0, 0, 96, "S")
-        group_d(0, 96, 128, "V")
-        gather(1, 3, 0)
-        gather(2, 1, 0)
-        gather(2, 1, 1)
-        group_x(1, 0, HALF, "S")
-        gather(2, 2, 0)
-        gather(2, 2, 1)
-        quantize_x(1)
-        quantize_d(0)
-        group_d(1, 0, 96, "S")
-        group_d(1, 96, 128, "V")
-        low_rank(0, 0)
-        low_rank(2, 0)
-        gather(2, 3, 0)
-        low_rank(1, 0)
-        low_rank(3, 0)
-        gather(2, 3, 1)
-        group_x(2, 0, HALF, "S")
-        quantize_d(1)
-        group_x(2, HALF, S, "V")
-        low_rank(1, 1)
-        group_d(2, 0, 64, "S")
-        low_rank(3, 1)
-        group_d(2, 64, 128, "V")
-        low_rank(0, 1)
-        low_rank(2, 1)
-        quantize_x(2)
-        base(1, 0)
-        base(2, 0)
-        group_u(0, 0, 192, "S")
-        base(3, 0)
-        quantize_d(2)
-        base(0, 0)
-        base(2, 1)
-        group_u(0, 192, 256, "V")
-        base(1, 1)
-        low_rank(1, 2)
+        for a in range(PASSES - 1):
+            for t in range(4):
+                gather(a, t)
+            interleave(x_grouped[a], picked[a], 0, S, "S")
+            quantize_x(a)
+            group_d(a, 0, 128, "S")
+            quantize_d(a)
+            for q in range(CHUNKS):
+                low_rank(q, a)
+        last = PASSES - 1
+        for t in range(4):
+            gather(last, t)
+        interleave(x_grouped[last], picked[last], 0, X_SPLIT, "S")
+        interleave(x_grouped[last], picked[last], X_SPLIT, S, "V")
+        quantize_x(last)
+        group_d(last, 0, D_SPLIT, "S")
+        group_d(last, D_SPLIT, 128, "V")
+        quantize_d(last)
+        for a in range(PASSES - 1):
+            for n in range(EARLY):
+                base(n, a)
+        for q in range(CHUNKS):
+            low_rank(q, last)
+            empty_h(q, "SV"[q % 2])
+            if q % 2 == 1:
+                quantize_h(q // 2)
+        for n in range(EARLY):
+            base(n, last)
+        interleave(u_grouped[0], u_raw[0], 0, U_SPLIT, "S")
+        interleave(u_grouped[0], u_raw[0], U_SPLIT, U_COLS, "V")
         quantize_u(0)
-        low_rank(3, 2)
-        empty_h(1, "V")
-        low_rank(2, 2)
-        empty_h(3, "S")
-        low_rank(0, 2)
-        base(3, 1)
-        empty_h(2, "V")
-        base(0, 1)
-        empty_h(0, "S")
-        base(2, 2)
-        group_u(1, 64, 256, "V")
-        base(7, 0)
-        base(6, 0)
-        group_u(1, 0, 64, "S")
-        base(7, 1)
-        group_h(128, 512, "V")
-        group_h(0, 128, "S")
-        base(4, 0)
-        base(0, 2)
-        base(3, 2)
+        for n in range(EARLY):
+            finish(n, "SV"[n % 2])
+        interleave(u_grouped[1], u_raw[1], 0, U_SPLIT, "S")
+        interleave(u_grouped[1], u_raw[1], U_SPLIT, U_COLS, "V")
         quantize_u(1)
-        base(1, 2)
-        held = keep.tile([P, 2, U_COLS, 4], BF16, name="hflat", align_bytes=64)
-        u_grouped[2] = held[:, 0]
-        u_grouped[3] = held[:, 1]
-        group_u(2, 0, 256, "S")
-        quantize_h()
-        base(5, 0)
-        base(6, 1)
-        base(5, 1)
-        group_u(3, 0, 256, "V")
-        finish(0)
-        finish(1)
-        empty_out(0, HALF, S, "V")
-        empty_out(0, 0, HALF, "S")
-        store(0)
-        finish(3)
-        base(5, 2)
-        quantize_u(2)
-        empty_out(1, 0, S, "S")
-        store(1)
-        finish(2)
-        empty_out(3, 0, S, "V")
-        store(3)
-        base(6, 2)
-        finish(5)
-        empty_out(2, 0, S, "S")
-        store(2)
-        quantize_u(3)
-        base(7, 2)
-        base(4, 1)
-        empty_out(5, 0, S, "V")
-        store(5)
-        finish(7)
-        finish(6)
-        empty_out(7, 0, S, "V")
-        store(7)
-        base(4, 2)
-        empty_out(6, 0, S, "S")
-        store(6)
-        finish(4)
-        empty_out(4, 0, S, "V")
-        store(4)
+        for n in range(EARLY, TILES):
+            for a in range(PASSES):
+                base(n, a)
+        for n in range(EARLY, TILES):
+            finish(n, "SV"[n % 2])

@@ -21,10 +21,13 @@ TILES = M // P
 EARLY = 4
 CHUNK = 128
 CHUNKS = S // CHUNK
-U_COLS = 512
-X_SPLIT = 176
-D_SPLIT = 56
-U_SPLIT = 256
+U_COLS = 256
+HOLD = 2
+UBUF = 1
+PU = 1
+EV = "SSSSSVSV"
+D_SPLIT = (96, 72, 52)
+U_SPLIT = (256, 256, 0, 0)
 
 
 def tile_list_hlora_none_kernel(tc, xT, w4_words, w4_scales, down, up, wgt, offs, out):
@@ -35,33 +38,36 @@ def tile_list_hlora_none_kernel(tc, xT, w4_words, w4_scales, down, up, wgt, offs
 
         offsets = keep.tile([P, S // 16], U16, name="offsets")
         weights = keep.tile([P, S], F32, name="weights")
-        x = [[keep.tile([P, T], F32, name=f"x{a}{t}") for t in range(4)] for a in range(PASSES)]
+        x = [[keep.tile([P, T], F32, name=f"x{a}{t}", align_bytes=64) for t in range(4)] for a in range(PASSES)]
         picked = [keep.tile([P, 4, S], F32, name=f"picked{a}") for a in range(PASSES)]
         x_grouped = [keep.tile([P, S, 4], BF16, name=f"xgrouped{a}", align_bytes=64) for a in range(PASSES)]
-        x_codes = [keep.tile([P, S], U32, name=f"xcodes{a}", align_bytes=64) for a in range(PASSES)]
+        x_codes = {}
         x_scales = [keep.tile([P, S], U8, name=f"xscales{a}", align_bytes=64) for a in range(PASSES)]
         d_raw = [keep.tile([P, 4, R], F32, name=f"draw{a}") for a in range(PASSES)]
         d_grouped = [keep.tile([P, R * 4], BF16, name=f"dgrouped{a}", align_bytes=64) for a in range(PASSES)]
         d_codes = [keep.tile([P, R], U32, name=f"dcodes{a}", align_bytes=64) for a in range(PASSES)]
         d_scales = [keep.tile([P, R], U8, name=f"dscales{a}", align_bytes=64) for a in range(PASSES)]
         u_raw = [keep.tile([P, 4, U_COLS], F32, name=f"uraw{c}") for c in range(M // U_COLS)]
-        u_grouped = [keep.tile([P, U_COLS, 4], BF16, name=f"ugrouped{c}", align_bytes=64) for c in range(M // U_COLS)]
+        u_grouped = {}
         u_codes = [keep.tile([P, U_COLS], U32, name=f"ucodes{c}", align_bytes=64) for c in range(M // U_COLS)]
         u_scales = [keep.tile([P, U_COLS], U8, name=f"uscales{c}", align_bytes=64) for c in range(M // U_COLS)]
         w_codes = [keep.tile([P, PASSES, 2 * P * EARLY], U8, name=f"wcodes{g}", align_bytes=64) for g in range(2)]
-        w_scales = keep.tile([P, PASSES, M], U8, name="wscales", align_bytes=64)
+        w_scales = [keep.tile([P, PASSES, P * EARLY], U8, name=f"wscales{g}", align_bytes=64) for g in range(2)]
         h_grouped = keep.tile([P, S, 4], BF16, name="hgrouped", align_bytes=64)
         h_codes = keep.tile([P, S], U32, name="hcodes", align_bytes=64)
         h_scales = keep.tile([P, S], U8, name="hscales", align_bytes=64)
         staged = [keep.tile([P, S], F32, name=f"staged{n}") for n in range(TILES)]
 
         nc.sync.dma_start(offsets[:], offs)
-        nc.gpsimd.memset(w_scales[:].bitcast(I32), 0)
-        for q in range(4):
-            nc.gpsimd.dma_start(
-                out=w_scales[32 * q : 32 * q + 4].bitcast(I32),
-                in_=w4_scales[:, 4 * q : 4 * q + 4, :].bitcast(I32).rearrange("a q c -> q a c"),
-            )
+        for g in range(2):
+            nc.gpsimd.memset(w_scales[g][:].bitcast(I32), 0)
+
+        def load_scales(g, engine):
+            for q in range(4):
+                engine.dma_start(
+                    out=w_scales[g][32 * q : 32 * q + 4].bitcast(I32),
+                    in_=w4_scales.bitcast(I32)[:, 4 * q : 4 * q + 4, 32 * EARLY * g : 32 * EARLY * (g + 1)].rearrange("a q c -> q a c"),
+                )
 
         def load_x(a, t):
             nc.sync.dma_start(out=x[a][t][:], in_=xT[512 * a : 512 * a + 512, :].rearrange("(p t) c -> p t c", t=4)[:, t, :])
@@ -78,19 +84,20 @@ def tile_list_hlora_none_kernel(tc, xT, w4_words, w4_scales, down, up, wgt, offs
         def load_u(c):
             nc.sync.dma_start(out=u_raw[c][:], in_=up.rearrange("(p t) n -> p t n", t=4)[:, :, U_COLS * c : U_COLS * c + U_COLS])
 
+        load_scales(0, nc.gpsimd)
         for a in range(PASSES):
             for t in range(4):
-                if a > 0 and t == 2:
-                    load_d(a - 1)
-                if (a, t) == (PASSES - 1, 3):
-                    load_w(0)
                 load_x(a, t)
                 if (a, t) == (0, 0):
                     nc.sync.dma_start(weights[:], wgt)
-        load_d(PASSES - 1)
+        load_w(0)
+        for a in range(PASSES):
+            load_d(a)
         load_u(0)
         load_w(1)
-        load_u(1)
+        load_scales(1, nc.sync)
+        for c in range(1, M // U_COLS):
+            load_u(c)
 
         def gather(a, t):
             nc.vector.tensor_tensor(picked[a][:, t, :], x[a][t][:].indirect(offsets[:]), weights[:], MULT)
@@ -108,6 +115,7 @@ def tile_list_hlora_none_kernel(tc, xT, w4_words, w4_scales, down, up, wgt, offs
             nc.vector.quantize_mx(out=codes.bitcast(E4M3), scales=scales, in_=grouped)
 
         def quantize_x(a):
+            x_codes[a] = keep.tile([P, S], U32, name=f"x{a + 1}{HOLD}" if a + 1 < PASSES else "xcodes", align_bytes=64)
             quantize(x_codes[a][:], x_scales[a][:], x_grouped[a][:].rearrange("p c t -> p (c t)"))
 
         def group_d(a, m0, m1, engine):
@@ -131,7 +139,7 @@ def tile_list_hlora_none_kernel(tc, xT, w4_words, w4_scales, down, up, wgt, offs
             nc.tensor.matmul_mx(
                 out=acc[n][:],
                 lhsT=w_codes[g][:, a, 256 * m : 256 * m + 256].bitcast(E2M1),
-                lhsT_scale=w_scales[:, a, 128 * n : 128 * n + 128],
+                lhsT_scale=w_scales[g][:, a, 128 * m : 128 * m + 128],
                 rhs=x_codes[a][:].bitcast(E4M3),
                 rhs_scale=x_scales[a][:],
                 start=(a == 0),
@@ -174,44 +182,41 @@ def tile_list_hlora_none_kernel(tc, xT, w4_words, w4_scales, down, up, wgt, offs
             copy_on(engine)(out=staged[n][:], in_=acc[n][:])
             nc.sync.dma_start(out=out[128 * n : 128 * n + 128, :], in_=staged[n][:])
 
-        for a in range(PASSES - 1):
+        def prepare_u(c):
+            u_grouped[c] = keep.tile([P, U_COLS, 4], BF16, name=f"ugrouped{c % UBUF}", align_bytes=64)
+            if U_SPLIT[c] > 0:
+                interleave(u_grouped[c], u_raw[c], 0, U_SPLIT[c], "S")
+            if U_SPLIT[c] < U_COLS:
+                interleave(u_grouped[c], u_raw[c], U_SPLIT[c], U_COLS, "V")
+            quantize_u(c)
+
+        last = PASSES - 1
+        for a in range(PASSES):
             for t in range(4):
                 gather(a, t)
-            interleave(x_grouped[a], picked[a], 0, S, "S")
-            quantize_x(a)
-            group_d(a, 0, 128, "S")
+                if a > 0 and t == HOLD:
+                    quantize_x(a - 1)
+            interleave(x_grouped[a], picked[a], 0, S, "V" if a == last else "S")
+        quantize_x(last)
+        for a in range(PASSES):
+            group_d(a, 0, D_SPLIT[a], "S")
+            group_d(a, D_SPLIT[a], 128, "V")
             quantize_d(a)
+            if a == last:
+                prepare_u(0)
             for q in range(CHUNKS):
                 low_rank(q, a)
-        last = PASSES - 1
-        for t in range(4):
-            gather(last, t)
-        interleave(x_grouped[last], picked[last], 0, X_SPLIT, "S")
-        interleave(x_grouped[last], picked[last], X_SPLIT, S, "V")
-        quantize_x(last)
-        group_d(last, 0, D_SPLIT, "S")
-        group_d(last, D_SPLIT, 128, "V")
-        quantize_d(last)
-        for a in range(PASSES - 1):
+                if a == last:
+                    empty_h(q, "SV"[q % 2])
+        quantize_h(0)
+        quantize_h(1)
+        for a in range(PASSES):
             for n in range(EARLY):
                 base(n, a)
-        for q in range(CHUNKS):
-            low_rank(q, last)
-            empty_h(q, "SV"[q % 2])
-            if q % 2 == 1:
-                quantize_h(q // 2)
-        for n in range(EARLY):
-            base(n, last)
-        interleave(u_grouped[0], u_raw[0], 0, U_SPLIT, "S")
-        interleave(u_grouped[0], u_raw[0], U_SPLIT, U_COLS, "V")
-        quantize_u(0)
-        for n in range(EARLY):
-            finish(n, "SV"[n % 2])
-        interleave(u_grouped[1], u_raw[1], 0, U_SPLIT, "S")
-        interleave(u_grouped[1], u_raw[1], U_SPLIT, U_COLS, "V")
-        quantize_u(1)
-        for n in range(EARLY, TILES):
-            for a in range(PASSES):
-                base(n, a)
-        for n in range(EARLY, TILES):
-            finish(n, "SV"[n % 2])
+        for n in range(TILES):
+            if n % 2 == PU and n // 2 + 1 < 4:
+                prepare_u(n // 2 + 1)
+            if n >= EARLY:
+                for a in range(PASSES):
+                    base(n, a)
+            finish(n, EV[n])

@@ -23,11 +23,11 @@ CHUNK = 128
 CHUNKS = S // CHUNK
 U_COLS = 256
 HOLD = 2
-UBUF = 1
+UBUF = 3
 PU = 1
 EV = "SSSSSVSV"
 D_SPLIT = (96, 72, 52)
-U_SPLIT = (256, 256, 0, 0)
+U_SPLIT = (256, 0, 0, 0)
 
 
 def tile_list_hlora_none_kernel(tc, xT, w4_words, w4_scales, down, up, wgt, offs, out):
@@ -52,22 +52,19 @@ def tile_list_hlora_none_kernel(tc, xT, w4_words, w4_scales, down, up, wgt, offs
         u_codes = [keep.tile([P, U_COLS], U32, name=f"ucodes{c}", align_bytes=64) for c in range(M // U_COLS)]
         u_scales = [keep.tile([P, U_COLS], U8, name=f"uscales{c}", align_bytes=64) for c in range(M // U_COLS)]
         w_codes = [keep.tile([P, PASSES, 2 * P * EARLY], U8, name=f"wcodes{g}", align_bytes=64) for g in range(2)]
-        w_scales = [keep.tile([P, PASSES, P * EARLY], U8, name=f"wscales{g}", align_bytes=64) for g in range(2)]
+        w_scales = keep.tile([P, PASSES, M], U8, name="wscales", align_bytes=64)
         h_grouped = keep.tile([P, S, 4], BF16, name="hgrouped", align_bytes=64)
         h_codes = keep.tile([P, S], U32, name="hcodes", align_bytes=64)
         h_scales = keep.tile([P, S], U8, name="hscales", align_bytes=64)
         staged = [keep.tile([P, S], F32, name=f"staged{n}") for n in range(TILES)]
 
         nc.sync.dma_start(offsets[:], offs)
-        for g in range(2):
-            nc.gpsimd.memset(w_scales[g][:].bitcast(I32), 0)
-
-        def load_scales(g, engine):
-            for q in range(4):
-                engine.dma_start(
-                    out=w_scales[g][32 * q : 32 * q + 4].bitcast(I32),
-                    in_=w4_scales.bitcast(I32)[:, 4 * q : 4 * q + 4, 32 * EARLY * g : 32 * EARLY * (g + 1)].rearrange("a q c -> q a c"),
-                )
+        nc.gpsimd.memset(w_scales[:].bitcast(I32), 0)
+        for q in range(4):
+            nc.gpsimd.dma_start(
+                out=w_scales[32 * q : 32 * q + 4].bitcast(I32),
+                in_=w4_scales[:, 4 * q : 4 * q + 4, :].bitcast(I32).rearrange("a q c -> q a c"),
+            )
 
         def load_x(a, t):
             nc.sync.dma_start(out=x[a][t][:], in_=xT[512 * a : 512 * a + 512, :].rearrange("(p t) c -> p t c", t=4)[:, t, :])
@@ -84,7 +81,6 @@ def tile_list_hlora_none_kernel(tc, xT, w4_words, w4_scales, down, up, wgt, offs
         def load_u(c):
             nc.sync.dma_start(out=u_raw[c][:], in_=up.rearrange("(p t) n -> p t n", t=4)[:, :, U_COLS * c : U_COLS * c + U_COLS])
 
-        load_scales(0, nc.gpsimd)
         for a in range(PASSES):
             for t in range(4):
                 load_x(a, t)
@@ -95,7 +91,6 @@ def tile_list_hlora_none_kernel(tc, xT, w4_words, w4_scales, down, up, wgt, offs
             load_d(a)
         load_u(0)
         load_w(1)
-        load_scales(1, nc.sync)
         for c in range(1, M // U_COLS):
             load_u(c)
 
@@ -139,7 +134,7 @@ def tile_list_hlora_none_kernel(tc, xT, w4_words, w4_scales, down, up, wgt, offs
             nc.tensor.matmul_mx(
                 out=acc[n][:],
                 lhsT=w_codes[g][:, a, 256 * m : 256 * m + 256].bitcast(E2M1),
-                lhsT_scale=w_scales[g][:, a, 128 * m : 128 * m + 128],
+                lhsT_scale=w_scales[:, a, 128 * n : 128 * n + 128],
                 rhs=x_codes[a][:].bitcast(E4M3),
                 rhs_scale=x_scales[a][:],
                 start=(a == 0),
@@ -183,7 +178,7 @@ def tile_list_hlora_none_kernel(tc, xT, w4_words, w4_scales, down, up, wgt, offs
             nc.sync.dma_start(out=out[128 * n : 128 * n + 128, :], in_=staged[n][:])
 
         def prepare_u(c):
-            u_grouped[c] = keep.tile([P, U_COLS, 4], BF16, name=f"ugrouped{c % UBUF}", align_bytes=64)
+            u_grouped[c] = keep.tile([P, U_COLS, 4], BF16, name="hgrouped" if 0 < c <= UBUF else f"ugrouped{c}", align_bytes=64)
             if U_SPLIT[c] > 0:
                 interleave(u_grouped[c], u_raw[c], 0, U_SPLIT[c], "S")
             if U_SPLIT[c] < U_COLS:

@@ -23,11 +23,12 @@ CHUNK = 128
 CHUNKS = S // CHUNK
 U_COLS = 256
 HOLD = 2
-UBUF = 3
+X_SPLIT = 192
+UTAG = ("ugrouped0", "dcodes2", "hgrouped", "hgrouped")
 PU = 1
 EV = "SSSSSVSV"
-D_SPLIT = (96, 72, 52)
-U_SPLIT = (256, 0, 0, 0)
+D_SPLIT = (160, 144, 96)
+U_SPLIT = (192, 256, 0, 0)
 
 
 def tile_list_hlora_none_kernel(tc, xT, w4_words, w4_scales, down, up, wgt, offs, out):
@@ -113,14 +114,23 @@ def tile_list_hlora_none_kernel(tc, xT, w4_words, w4_scales, down, up, wgt, offs
             x_codes[a] = keep.tile([P, S], U32, name=f"x{a + 1}{HOLD}" if a + 1 < PASSES else "xcodes", align_bytes=64)
             quantize(x_codes[a][:], x_scales[a][:], x_grouped[a][:].rearrange("p c t -> p (c t)"))
 
-        def group_d(a, m0, m1, engine):
+        def group_d(a, m0, m1, t0, engine):
             copy_on(engine)(
-                out=d_grouped[a][:].rearrange("p (t m j) -> p m t j", t=4, j=4)[:, m0:m1],
-                in_=d_raw[a][:].rearrange("p j (m t) -> p m t j", t=4)[:, m0:m1],
+                out=d_grouped[a][:].rearrange("p (t m j) -> p m j t", t=4, j=4)[:, m0:m1, :, t0 : t0 + 2],
+                in_=d_raw[a][:].rearrange("p j (m t) -> p m j t", t=4)[:, m0:m1, :, t0 : t0 + 2],
             )
 
-        def quantize_d(a):
-            quantize(d_codes[a][:], d_scales[a][:], d_grouped[a][:])
+        def prepare_d(a):
+            upper, lower = min(D_SPLIT[a], P), max(D_SPLIT[a] - P, 0)
+            group_d(a, 0, upper, 2, "S")
+            if lower > 0:
+                group_d(a, 0, lower, 0, "S")
+            group_d(a, lower, P, 0, "V")
+            if upper < P:
+                group_d(a, upper, P, 2, "V")
+
+        def quantize_d(a, t0=0, t1=4):
+            quantize(d_codes[a][:, 128 * t0 : 128 * t1], d_scales[a][:, 128 * t0 : 128 * t1], d_grouped[a][:, 512 * t0 : 512 * t1])
 
         def quantize_u(c):
             quantize(u_codes[c][:], u_scales[c][:], u_grouped[c][:].rearrange("p c t -> p (c t)"))
@@ -143,9 +153,9 @@ def tile_list_hlora_none_kernel(tc, xT, w4_words, w4_scales, down, up, wgt, offs
 
         h_bank = [psum.tile([P, 4, CHUNK], F32, name=f"bank{q}") for q in range(CHUNKS)]
 
-        def low_rank(q, a):
+        def low_rank(q, a, t0=0, t1=4):
             cols = slice(CHUNK * q, CHUNK * q + CHUNK)
-            for t in range(4):
+            for t in range(t0, t1):
                 nc.tensor.matmul_mx(
                     out=h_bank[q][:, t, :],
                     lhsT=d_codes[a][:, 128 * t : 128 * t + 128].bitcast(E4M3),
@@ -178,7 +188,7 @@ def tile_list_hlora_none_kernel(tc, xT, w4_words, w4_scales, down, up, wgt, offs
             nc.sync.dma_start(out=out[128 * n : 128 * n + 128, :], in_=staged[n][:])
 
         def prepare_u(c):
-            u_grouped[c] = keep.tile([P, U_COLS, 4], BF16, name="hgrouped" if 0 < c <= UBUF else f"ugrouped{c}", align_bytes=64)
+            u_grouped[c] = keep.tile([P, U_COLS, 4], BF16, name=UTAG[c], align_bytes=64)
             if U_SPLIT[c] > 0:
                 interleave(u_grouped[c], u_raw[c], 0, U_SPLIT[c], "S")
             if U_SPLIT[c] < U_COLS:
@@ -191,18 +201,26 @@ def tile_list_hlora_none_kernel(tc, xT, w4_words, w4_scales, down, up, wgt, offs
                 gather(a, t)
                 if a > 0 and t == HOLD:
                     quantize_x(a - 1)
-            interleave(x_grouped[a], picked[a], 0, S, "V" if a == last else "S")
+            split = X_SPLIT if a == last else S
+            if split > 0:
+                interleave(x_grouped[a], picked[a], 0, split, "S")
+            if split < S:
+                interleave(x_grouped[a], picked[a], split, S, "V")
         quantize_x(last)
-        for a in range(PASSES):
-            group_d(a, 0, D_SPLIT[a], "S")
-            group_d(a, D_SPLIT[a], 128, "V")
+        for a in range(last):
+            prepare_d(a)
             quantize_d(a)
-            if a == last:
-                prepare_u(0)
             for q in range(CHUNKS):
                 low_rank(q, a)
-                if a == last:
-                    empty_h(q, "SV"[q % 2])
+        prepare_d(last)
+        quantize_d(last, 0, 2)
+        quantize_d(last, 2, 4)
+        prepare_u(0)
+        for q in range(CHUNKS):
+            low_rank(q, last, 0, 2)
+        for q in range(CHUNKS):
+            low_rank(q, last, 2, 4)
+            empty_h(q, "SV"[q % 2])
         quantize_h(0)
         quantize_h(1)
         for a in range(PASSES):

@@ -23,6 +23,12 @@ CHUNK = 128
 CHUNKS = S // CHUNK
 U_COLS = 256
 HOLD = 2
+LEAD = 2
+HE = "SVSV"
+HALVES = (7,)
+W_AT = 10
+W2_AT = 13
+D_AT = 11
 X_SPLIT = 192
 UTAG = ("ugrouped0", "dcodes2", "hgrouped", "hgrouped")
 PU = 1
@@ -73,24 +79,38 @@ def tile_list_hlora_none_kernel(tc, xT, w4_words, w4_scales, down, up, wgt, offs
         def load_d(a):
             nc.sync.dma_start(out=d_raw[a][:], in_=down[512 * a : 512 * a + 512, :].rearrange("(p t) r -> p t r", t=4))
 
-        def load_w(g):
+        def load_w(g, a0=0, a1=PASSES):
             nc.sync.dma_start(
-                out=w_codes[g][:].bitcast(I32),
-                in_=w4_words.bitcast(I32).rearrange("a p c -> p a c")[:, :, 64 * EARLY * g : 64 * EARLY * (g + 1)],
+                out=w_codes[g][:].bitcast(I32)[:, a0:a1],
+                in_=w4_words.bitcast(I32).rearrange("a p c -> p a c")[:, a0:a1, 64 * EARLY * g : 64 * EARLY * (g + 1)],
             )
 
         def load_u(c):
             nc.sync.dma_start(out=u_raw[c][:], in_=up.rearrange("(p t) n -> p t n", t=4)[:, :, U_COLS * c : U_COLS * c + U_COLS])
 
+        def extra(k):
+            if k == W_AT and k == W2_AT:
+                load_w(0)
+            elif k == W_AT:
+                load_w(0, 0, 2)
+            elif k == W2_AT:
+                load_w(0, 2, 3)
+            if k == D_AT:
+                load_d(0)
+
         for a in range(PASSES):
             for t in range(4):
+                extra(4 * a + t)
                 load_x(a, t)
                 if (a, t) == (0, 0):
                     nc.sync.dma_start(weights[:], wgt)
-        load_w(0)
-        for a in range(PASSES):
-            load_d(a)
+        extra(12)
+        load_d(1)
+        extra(13)
+        load_d(2)
+        extra(14)
         load_u(0)
+        extra(15)
         load_w(1)
         for c in range(1, M // U_COLS):
             load_u(c)
@@ -125,7 +145,8 @@ def tile_list_hlora_none_kernel(tc, xT, w4_words, w4_scales, down, up, wgt, offs
             group_d(a, 0, upper, 2, "S")
             if lower > 0:
                 group_d(a, 0, lower, 0, "S")
-            group_d(a, lower, P, 0, "V")
+            if lower < P:
+                group_d(a, lower, P, 0, "V")
             if upper < P:
                 group_d(a, upper, P, 2, "V")
 
@@ -184,8 +205,10 @@ def tile_list_hlora_none_kernel(tc, xT, w4_words, w4_scales, down, up, wgt, offs
                 start=False,
                 stop=True,
             )
-            copy_on(engine)(out=staged[n][:], in_=acc[n][:])
-            nc.sync.dma_start(out=out[128 * n : 128 * n + 128, :], in_=staged[n][:])
+            width = S // 2 if n in HALVES else S
+            for c0 in range(0, S, width):
+                copy_on(engine)(out=staged[n][:, c0 : c0 + width], in_=acc[n][:, c0 : c0 + width])
+                nc.sync.dma_start(out=out[128 * n : 128 * n + 128, c0 : c0 + width], in_=staged[n][:, c0 : c0 + width])
 
         def prepare_u(c):
             u_grouped[c] = keep.tile([P, U_COLS, 4], BF16, name=UTAG[c], align_bytes=64)
@@ -216,11 +239,11 @@ def tile_list_hlora_none_kernel(tc, xT, w4_words, w4_scales, down, up, wgt, offs
         quantize_d(last, 0, 2)
         quantize_d(last, 2, 4)
         prepare_u(0)
-        for q in range(CHUNKS):
+        for q in range(LEAD):
             low_rank(q, last, 0, 2)
         for q in range(CHUNKS):
-            low_rank(q, last, 2, 4)
-            empty_h(q, "SV"[q % 2])
+            low_rank(q, last, 2 if q < LEAD else 0, 4)
+            empty_h(q, HE[q])
         quantize_h(0)
         quantize_h(1)
         for a in range(PASSES):

@@ -22,19 +22,22 @@ EARLY = 4
 CHUNK = 128
 CHUNKS = S // CHUNK
 U_COLS = 256
-HOLD = 2
+HOLD = (2, 2)
 LEAD = 2
-HE = "SVSV"
+D_CUT = 64
+FIRST = 256
+HE = "VSVS"
 HALVES = (7,)
 W_AT = 10
 W2_AT = 13
 D_AT = 11
-X_SPLIT = 192
-UTAG = ("ugrouped0", "dcodes2", "hgrouped", "hgrouped")
-PU = 1
+X_SPLIT = 160
+UTAG = ("ugrouped0", "", "hsecond", "hsecond")
+AHEAD = 0
+FIRST_V = 5
 EV = "SSSSSVSV"
-D_SPLIT = (160, 144, 96)
-U_SPLIT = (192, 256, 0, 0)
+D_SPLIT = (128, 160, 128)
+U_SPLIT = (192, 0, 0, 0)
 
 
 def tile_list_hlora_none_kernel(tc, xT, w4_words, w4_scales, down, up, wgt, offs, out):
@@ -50,7 +53,11 @@ def tile_list_hlora_none_kernel(tc, xT, w4_words, w4_scales, down, up, wgt, offs
         x_grouped = [keep.tile([P, S, 4], BF16, name=f"xgrouped{a}", align_bytes=64) for a in range(PASSES)]
         x_codes = {}
         x_scales = [keep.tile([P, S], U8, name=f"xscales{a}", align_bytes=64) for a in range(PASSES)]
-        d_raw = [keep.tile([P, 4, R], F32, name=f"draw{a}") for a in range(PASSES)]
+        d_cuts = [(0, P), (0, P), (0, D_CUT, P) if D_CUT < P else (0, P)]
+        d_raw = {}
+        for a in range(PASSES):
+            for m0, m1 in zip(d_cuts[a], d_cuts[a][1:]):
+                d_raw[a, m0] = keep.tile([P, 4, 4 * (m1 - m0)], F32, name=f"draw{a}{m0}")
         d_grouped = [keep.tile([P, R * 4], BF16, name=f"dgrouped{a}", align_bytes=64) for a in range(PASSES)]
         d_codes = [keep.tile([P, R], U32, name=f"dcodes{a}", align_bytes=64) for a in range(PASSES)]
         d_scales = [keep.tile([P, R], U8, name=f"dscales{a}", align_bytes=64) for a in range(PASSES)]
@@ -58,12 +65,12 @@ def tile_list_hlora_none_kernel(tc, xT, w4_words, w4_scales, down, up, wgt, offs
         u_grouped = {}
         u_codes = [keep.tile([P, U_COLS], U32, name=f"ucodes{c}", align_bytes=64) for c in range(M // U_COLS)]
         u_scales = [keep.tile([P, U_COLS], U8, name=f"uscales{c}", align_bytes=64) for c in range(M // U_COLS)]
-        w_codes = [keep.tile([P, PASSES, 2 * P * EARLY], U8, name=f"wcodes{g}", align_bytes=64) for g in range(2)]
+        w_codes = {}
         w_scales = keep.tile([P, PASSES, M], U8, name="wscales", align_bytes=64)
-        h_grouped = keep.tile([P, S, 4], BF16, name="hgrouped", align_bytes=64)
+        h_grouped = [keep.tile([P, S // 2, 4], BF16, name=name, align_bytes=64) for name in ("hfirst", "hsecond")]
         h_codes = keep.tile([P, S], U32, name="hcodes", align_bytes=64)
         h_scales = keep.tile([P, S], U8, name="hscales", align_bytes=64)
-        staged = [keep.tile([P, S], F32, name=f"staged{n}") for n in range(TILES)]
+        staged = {}
 
         nc.sync.dma_start(offsets[:], offs)
         nc.gpsimd.memset(w_scales[:].bitcast(I32), 0)
@@ -77,11 +84,16 @@ def tile_list_hlora_none_kernel(tc, xT, w4_words, w4_scales, down, up, wgt, offs
             nc.sync.dma_start(out=x[a][t][:], in_=xT[512 * a : 512 * a + 512, :].rearrange("(p t) c -> p t c", t=4)[:, t, :])
 
         def load_d(a):
-            nc.sync.dma_start(out=d_raw[a][:], in_=down[512 * a : 512 * a + 512, :].rearrange("(p t) r -> p t r", t=4))
+            for m0, m1 in zip(d_cuts[a], d_cuts[a][1:]):
+                rows = down[512 * a : 512 * a + 512, 4 * m0 : 4 * m1]
+                nc.sync.dma_start(out=d_raw[a, m0][:], in_=rows.rearrange("(p t) r -> p t r", t=4))
 
         def load_w(g, a0=0, a1=PASSES):
+            piece = keep.tile([P, a1 - a0, 2 * P * EARLY], U8, name=f"wcodes{g}{a0}", align_bytes=64)
+            for a in range(a0, a1):
+                w_codes[g, a] = piece[:, a - a0, :]
             nc.sync.dma_start(
-                out=w_codes[g][:].bitcast(I32)[:, a0:a1],
+                out=piece[:].bitcast(I32),
                 in_=w4_words.bitcast(I32).rearrange("a p c -> p a c")[:, a0:a1, 64 * EARLY * g : 64 * EARLY * (g + 1)],
             )
 
@@ -103,7 +115,8 @@ def tile_list_hlora_none_kernel(tc, xT, w4_words, w4_scales, down, up, wgt, offs
                 extra(4 * a + t)
                 load_x(a, t)
                 if (a, t) == (0, 0):
-                    nc.sync.dma_start(weights[:], wgt)
+                    for c0 in range(0, S, FIRST):
+                        nc.sync.dma_start(weights[:, c0 : c0 + FIRST], wgt[:, c0 : c0 + FIRST])
         extra(12)
         load_d(1)
         extra(13)
@@ -111,12 +124,19 @@ def tile_list_hlora_none_kernel(tc, xT, w4_words, w4_scales, down, up, wgt, offs
         extra(14)
         load_u(0)
         extra(15)
-        load_w(1)
-        for c in range(1, M // U_COLS):
+        load_w(1, 0, 1)
+        load_u(1)
+        load_w(1, 1, PASSES)
+        for c in range(2, M // U_COLS):
             load_u(c)
 
         def gather(a, t):
-            nc.vector.tensor_tensor(picked[a][:, t, :], x[a][t][:].indirect(offsets[:]), weights[:], MULT)
+            width = FIRST if (a, t) == (0, 0) else S
+            for c0 in range(0, S, width):
+                cols = slice(c0, c0 + width)
+                nc.vector.tensor_tensor(
+                    picked[a][:, t, cols], x[a][t][:].indirect(offsets[:, c0 // 16 : (c0 + width) // 16]), weights[:, cols], MULT
+                )
 
         def copy_on(engine):
             return nc.scalar.copy if engine == "S" else nc.vector.tensor_copy
@@ -131,24 +151,27 @@ def tile_list_hlora_none_kernel(tc, xT, w4_words, w4_scales, down, up, wgt, offs
             nc.vector.quantize_mx(out=codes.bitcast(E4M3), scales=scales, in_=grouped)
 
         def quantize_x(a):
-            x_codes[a] = keep.tile([P, S], U32, name=f"x{a + 1}{HOLD}" if a + 1 < PASSES else "xcodes", align_bytes=64)
+            x_codes[a] = keep.tile([P, S], U32, name=f"x{a + 1}{HOLD[a]}" if a + 1 < PASSES else "xcodes", align_bytes=64)
             quantize(x_codes[a][:], x_scales[a][:], x_grouped[a][:].rearrange("p c t -> p (c t)"))
 
-        def group_d(a, m0, m1, t0, engine):
+        def group_d(a, first, m0, m1, t0, engine):
             copy_on(engine)(
-                out=d_grouped[a][:].rearrange("p (t m j) -> p m j t", t=4, j=4)[:, m0:m1, :, t0 : t0 + 2],
-                in_=d_raw[a][:].rearrange("p j (m t) -> p m j t", t=4)[:, m0:m1, :, t0 : t0 + 2],
+                out=d_grouped[a][:].rearrange("p (t m j) -> p m j t", t=4, j=4)[:, first + m0 : first + m1, :, t0 : t0 + 2],
+                in_=d_raw[a, first][:].rearrange("p j (m t) -> p m j t", t=4)[:, m0:m1, :, t0 : t0 + 2],
             )
 
         def prepare_d(a):
-            upper, lower = min(D_SPLIT[a], P), max(D_SPLIT[a] - P, 0)
-            group_d(a, 0, upper, 2, "S")
-            if lower > 0:
-                group_d(a, 0, lower, 0, "S")
-            if lower < P:
-                group_d(a, lower, P, 0, "V")
-            if upper < P:
-                group_d(a, upper, P, 2, "V")
+            for first, end in zip(d_cuts[a], d_cuts[a][1:]):
+                width = end - first
+                share = D_SPLIT[a] * width // P // 2 * 2
+                upper, lower = min(share, width), max(share - width, 0)
+                group_d(a, first, 0, upper, 2, "S")
+                if lower > 0:
+                    group_d(a, first, 0, lower, 0, "S")
+                if lower < width:
+                    group_d(a, first, lower, width, 0, "V")
+                if upper < width:
+                    group_d(a, first, upper, width, 2, "V")
 
         def quantize_d(a, t0=0, t1=4):
             quantize(d_codes[a][:, 128 * t0 : 128 * t1], d_scales[a][:, 128 * t0 : 128 * t1], d_grouped[a][:, 512 * t0 : 512 * t1])
@@ -164,7 +187,7 @@ def tile_list_hlora_none_kernel(tc, xT, w4_words, w4_scales, down, up, wgt, offs
             g, m = divmod(n, EARLY)
             nc.tensor.matmul_mx(
                 out=acc[n][:],
-                lhsT=w_codes[g][:, a, 256 * m : 256 * m + 256].bitcast(E2M1),
+                lhsT=w_codes[g, a][:, 256 * m : 256 * m + 256].bitcast(E2M1),
                 lhsT_scale=w_scales[:, a, 128 * n : 128 * n + 128],
                 rhs=x_codes[a][:].bitcast(E4M3),
                 rhs_scale=x_scales[a][:],
@@ -188,11 +211,11 @@ def tile_list_hlora_none_kernel(tc, xT, w4_words, w4_scales, down, up, wgt, offs
                 )
 
         def empty_h(q, engine):
-            copy_on(engine)(out=h_grouped[:, CHUNK * q : CHUNK * q + CHUNK, :], in_=h_bank[q][:].rearrange("p t c -> p c t"))
+            copy_on(engine)(out=h_grouped[q // 2][:, CHUNK * (q % 2) : CHUNK * (q % 2) + CHUNK, :], in_=h_bank[q][:].rearrange("p t c -> p c t"))
 
         def quantize_h(half):
             cols = slice(256 * half, 256 * half + 256)
-            quantize(h_codes[:, cols], h_scales[:, cols], h_grouped[:, cols, :].rearrange("p c t -> p (c t)"))
+            quantize(h_codes[:, cols], h_scales[:, cols], h_grouped[half][:].rearrange("p c t -> p (c t)"))
 
         def finish(n, engine):
             c, m = divmod(128 * n, U_COLS)
@@ -205,6 +228,7 @@ def tile_list_hlora_none_kernel(tc, xT, w4_words, w4_scales, down, up, wgt, offs
                 start=False,
                 stop=True,
             )
+            staged[n] = keep.tile([P, S], F32, name="hsecond" if n == FIRST_V else f"staged{n}", align_bytes=64)
             width = S // 2 if n in HALVES else S
             for c0 in range(0, S, width):
                 copy_on(engine)(out=staged[n][:, c0 : c0 + width], in_=acc[n][:, c0 : c0 + width])
@@ -216,13 +240,12 @@ def tile_list_hlora_none_kernel(tc, xT, w4_words, w4_scales, down, up, wgt, offs
                 interleave(u_grouped[c], u_raw[c], 0, U_SPLIT[c], "S")
             if U_SPLIT[c] < U_COLS:
                 interleave(u_grouped[c], u_raw[c], U_SPLIT[c], U_COLS, "V")
-            quantize_u(c)
 
         last = PASSES - 1
         for a in range(PASSES):
             for t in range(4):
                 gather(a, t)
-                if a > 0 and t == HOLD:
+                if a > 0 and t == HOLD[a - 1]:
                     quantize_x(a - 1)
             split = X_SPLIT if a == last else S
             if split > 0:
@@ -239,6 +262,9 @@ def tile_list_hlora_none_kernel(tc, xT, w4_words, w4_scales, down, up, wgt, offs
         quantize_d(last, 0, 2)
         quantize_d(last, 2, 4)
         prepare_u(0)
+        quantize_u(0)
+        u_first = keep.tile([P, P, 4], BF16, name="ufirst", align_bytes=64)
+        interleave(u_first, u_raw[1], 0, P, "S")
         for q in range(LEAD):
             low_rank(q, last, 0, 2)
         for q in range(CHUNKS):
@@ -249,10 +275,22 @@ def tile_list_hlora_none_kernel(tc, xT, w4_words, w4_scales, down, up, wgt, offs
         for a in range(PASSES):
             for n in range(EARLY):
                 base(n, a)
+        u_second = keep.tile([P, P, 4], BF16, name="dcodes2", align_bytes=64)
+        interleave(u_second, u_raw[1][:, :, P : 2 * P], 0, P, "S")
+        prepare_u(2)
+        u_codes_1 = keep.tile([P, U_COLS], U32, name="hfirst", align_bytes=64)
+        u_codes[1] = u_codes_1
+        quantize(u_codes[1][:, 0:P], u_scales[1][:, 0:P], u_first[:].rearrange("p c t -> p (c t)"))
+        quantize(u_codes[1][:, P : 2 * P], u_scales[1][:, P : 2 * P], u_second[:].rearrange("p c t -> p (c t)"))
+        quantize_u(2)
+        prepare_u(3)
+        quantize_u(3)
         for n in range(TILES):
-            if n % 2 == PU and n // 2 + 1 < 4:
-                prepare_u(n // 2 + 1)
-            if n >= EARLY:
-                for a in range(PASSES):
-                    base(n, a)
+            ahead = [EARLY, EARLY + 1] if n == EARLY else [n + 1]
+            if AHEAD == 0:
+                ahead = [n]
+            for k in ahead:
+                if n >= EARLY and k < TILES:
+                    for a in range(PASSES):
+                        base(k, a)
             finish(n, EV[n])

@@ -23,7 +23,7 @@ CHUNK = 128
 CHUNKS = S // CHUNK
 U_COLS = 256
 HOLD = (2, 2)
-LEAD = 2
+LEAD = 0
 D_CUT = 64
 FIRST = 256
 HE = "VSVS"
@@ -31,13 +31,18 @@ HALVES = (7,)
 W_AT = 10
 W2_AT = 13
 D_AT = 11
-X_SPLIT = 160
-UTAG = ("ugrouped0", "", "hsecond", "hsecond")
+X_SPLIT = 128
+UTAG = ("ugrouped0", "dcodes2", "hsecond", "dcodes2")
 AHEAD = 0
-FIRST_V = 5
-EV = "SSSSSVSV"
-D_SPLIT = (128, 160, 128)
-U_SPLIT = (192, 0, 0, 0)
+POST = "u0 w02 u1 u2 u3 w23"
+H0 = "hfirst"
+B7 = "acc1"
+ORDER = 0
+BANKS = ("acc0", "acc1", "acc2", "acc3", "bank0", "bank1", "bank2")
+FIRST_V = 9
+EV = "SSSSVSVS"
+D_SPLIT = (208, 176, 160)
+U_SPLIT = (256, 256, 0, 0)
 
 
 def tile_list_hlora_none_kernel(tc, xT, w4_words, w4_scales, down, up, wgt, offs, out):
@@ -67,7 +72,6 @@ def tile_list_hlora_none_kernel(tc, xT, w4_words, w4_scales, down, up, wgt, offs
         u_scales = [keep.tile([P, U_COLS], U8, name=f"uscales{c}", align_bytes=64) for c in range(M // U_COLS)]
         w_codes = {}
         w_scales = keep.tile([P, PASSES, M], U8, name="wscales", align_bytes=64)
-        h_grouped = [keep.tile([P, S // 2, 4], BF16, name=name, align_bytes=64) for name in ("hfirst", "hsecond")]
         h_codes = keep.tile([P, S], U32, name="hcodes", align_bytes=64)
         h_scales = keep.tile([P, S], U8, name="hscales", align_bytes=64)
         staged = {}
@@ -121,14 +125,11 @@ def tile_list_hlora_none_kernel(tc, xT, w4_words, w4_scales, down, up, wgt, offs
         load_d(1)
         extra(13)
         load_d(2)
-        extra(14)
-        load_u(0)
-        extra(15)
-        load_w(1, 0, 1)
-        load_u(1)
-        load_w(1, 1, PASSES)
-        for c in range(2, M // U_COLS):
-            load_u(c)
+        for item in POST.split():
+            if item[0] == "u":
+                load_u(int(item[1]))
+            else:
+                load_w(1, int(item[1]), int(item[2]))
 
         def gather(a, t):
             width = FIRST if (a, t) == (0, 0) else S
@@ -183,7 +184,7 @@ def tile_list_hlora_none_kernel(tc, xT, w4_words, w4_scales, down, up, wgt, offs
 
         def base(n, a):
             if a == 0:
-                acc[n] = psum.tile([P, S], F32, name=f"acc{n}" if n < EARLY else f"bank{n - EARLY}")
+                acc[n] = psum.tile([P, S], F32, name=(BANKS + (B7,))[n])
             g, m = divmod(n, EARLY)
             nc.tensor.matmul_mx(
                 out=acc[n][:],
@@ -263,8 +264,7 @@ def tile_list_hlora_none_kernel(tc, xT, w4_words, w4_scales, down, up, wgt, offs
         quantize_d(last, 2, 4)
         prepare_u(0)
         quantize_u(0)
-        u_first = keep.tile([P, P, 4], BF16, name="ufirst", align_bytes=64)
-        interleave(u_first, u_raw[1], 0, P, "S")
+        h_grouped = [keep.tile([P, S // 2, 4], BF16, name=name, align_bytes=64) for name in (H0, "hsecond")]
         for q in range(LEAD):
             low_rank(q, last, 0, 2)
         for q in range(CHUNKS):
@@ -275,15 +275,15 @@ def tile_list_hlora_none_kernel(tc, xT, w4_words, w4_scales, down, up, wgt, offs
         for a in range(PASSES):
             for n in range(EARLY):
                 base(n, a)
-        u_second = keep.tile([P, P, 4], BF16, name="dcodes2", align_bytes=64)
-        interleave(u_second, u_raw[1][:, :, P : 2 * P], 0, P, "S")
+        prepare_u(1)
         prepare_u(2)
-        u_codes_1 = keep.tile([P, U_COLS], U32, name="hfirst", align_bytes=64)
-        u_codes[1] = u_codes_1
-        quantize(u_codes[1][:, 0:P], u_scales[1][:, 0:P], u_first[:].rearrange("p c t -> p (c t)"))
-        quantize(u_codes[1][:, P : 2 * P], u_scales[1][:, P : 2 * P], u_second[:].rearrange("p c t -> p (c t)"))
-        quantize_u(2)
-        prepare_u(3)
+        quantize_u(1)
+        if ORDER == 0:
+            quantize_u(2)
+            prepare_u(3)
+        else:
+            prepare_u(3)
+            quantize_u(2)
         quantize_u(3)
         for n in range(TILES):
             ahead = [EARLY, EARLY + 1] if n == EARLY else [n + 1]

@@ -17,64 +17,49 @@ MULT = mybir.AluOpType.mult
 
 P = 128
 PASSES = K // 512
+LAST = PASSES - 1
 TILES = M // P
 EARLY = 4
 CHUNK = 128
 CHUNKS = S // CHUNK
+HALF = S // 2
 U_COLS = 256
-HOLD = (2, 2)
-LEAD = 0
-D_CUT = 64
-FIRST = 256
-HE = "VSVS"
-HALVES = (7,)
-W_AT = 10
-W2_AT = 13
-D_AT = 11
-X_SPLIT = 128
-UTAG = ("ugrouped0", "dcodes2", "hsecond", "dcodes2")
-AHEAD = 0
-POST = "u0 w02 u1 u2 u3 w23"
-H0 = "hfirst"
-B7 = "acc1"
-ORDER = 0
-BANKS = ("acc0", "acc1", "acc2", "acc3", "bank0", "bank1", "bank2")
-FIRST_V = 9
-EV = "SSSSVSVS"
-D_SPLIT = (208, 176, 160)
-U_SPLIT = (256, 256, 0, 0)
+QUARTERS = M // U_COLS
+
+X_ON_SCALAR = 128
+D_ON_SCALAR = (80, 48, 32)
 
 
 def tile_list_hlora_none_kernel(tc, xT, w4_words, w4_scales, down, up, wgt, offs, out):
     nc = tc.nc
+    on_scalar, on_vector = nc.scalar.copy, nc.vector.tensor_copy
     with ExitStack() as ctx:
         keep = ctx.enter_context(tc.tile_pool(name="keep", bufs=1))
         psum = ctx.enter_context(tc.psum_pool(name="psum", bufs=1))
 
         offsets = keep.tile([P, S // 16], U16, name="offsets")
         weights = keep.tile([P, S], F32, name="weights")
-        x = [[keep.tile([P, T], F32, name=f"x{a}{t}", align_bytes=64) for t in range(4)] for a in range(PASSES)]
+        x_plane = [[keep.tile([P, T], F32, name=f"x{a}{i}", align_bytes=64) for i in range(4)] for a in range(PASSES)]
         picked = [keep.tile([P, 4, S], F32, name=f"picked{a}") for a in range(PASSES)]
         x_grouped = [keep.tile([P, S, 4], BF16, name=f"xgrouped{a}", align_bytes=64) for a in range(PASSES)]
         x_codes = {}
         x_scales = [keep.tile([P, S], U8, name=f"xscales{a}", align_bytes=64) for a in range(PASSES)]
-        d_cuts = [(0, P), (0, P), (0, D_CUT, P) if D_CUT < P else (0, P)]
+        d_pieces = [[(0, P)], [(0, P)], [(0, P // 2), (P // 2, P)]]
         d_raw = {}
         for a in range(PASSES):
-            for m0, m1 in zip(d_cuts[a], d_cuts[a][1:]):
+            for m0, m1 in d_pieces[a]:
                 d_raw[a, m0] = keep.tile([P, 4, 4 * (m1 - m0)], F32, name=f"draw{a}{m0}")
         d_grouped = [keep.tile([P, R * 4], BF16, name=f"dgrouped{a}", align_bytes=64) for a in range(PASSES)]
         d_codes = [keep.tile([P, R], U32, name=f"dcodes{a}", align_bytes=64) for a in range(PASSES)]
         d_scales = [keep.tile([P, R], U8, name=f"dscales{a}", align_bytes=64) for a in range(PASSES)]
-        u_raw = [keep.tile([P, 4, U_COLS], F32, name=f"uraw{c}") for c in range(M // U_COLS)]
+        u_raw = [keep.tile([P, 4, U_COLS], F32, name=f"uraw{c}") for c in range(QUARTERS)]
         u_grouped = {}
-        u_codes = [keep.tile([P, U_COLS], U32, name=f"ucodes{c}", align_bytes=64) for c in range(M // U_COLS)]
-        u_scales = [keep.tile([P, U_COLS], U8, name=f"uscales{c}", align_bytes=64) for c in range(M // U_COLS)]
+        u_codes = [keep.tile([P, U_COLS], U32, name=f"ucodes{c}", align_bytes=64) for c in range(QUARTERS)]
+        u_scales = [keep.tile([P, U_COLS], U8, name=f"uscales{c}", align_bytes=64) for c in range(QUARTERS)]
         w_codes = {}
         w_scales = keep.tile([P, PASSES, M], U8, name="wscales", align_bytes=64)
         h_codes = keep.tile([P, S], U32, name="hcodes", align_bytes=64)
         h_scales = keep.tile([P, S], U8, name="hscales", align_bytes=64)
-        staged = {}
 
         nc.sync.dma_start(offsets[:], offs)
         nc.gpsimd.memset(w_scales[:].bitcast(I32), 0)
@@ -84,213 +69,176 @@ def tile_list_hlora_none_kernel(tc, xT, w4_words, w4_scales, down, up, wgt, offs
                 in_=w4_scales[:, 4 * q : 4 * q + 4, :].bitcast(I32).rearrange("a q c -> q a c"),
             )
 
-        def load_x(a, t):
-            nc.sync.dma_start(out=x[a][t][:], in_=xT[512 * a : 512 * a + 512, :].rearrange("(p t) c -> p t c", t=4)[:, t, :])
+        def load_x(a, i):
+            rows = xT[512 * a : 512 * a + 512, :].rearrange("(p i) c -> p i c", i=4)
+            nc.sync.dma_start(out=x_plane[a][i][:], in_=rows[:, i, :])
 
         def load_d(a):
-            for m0, m1 in zip(d_cuts[a], d_cuts[a][1:]):
+            for m0, m1 in d_pieces[a]:
                 rows = down[512 * a : 512 * a + 512, 4 * m0 : 4 * m1]
-                nc.sync.dma_start(out=d_raw[a, m0][:], in_=rows.rearrange("(p t) r -> p t r", t=4))
+                nc.sync.dma_start(out=d_raw[a, m0][:], in_=rows.rearrange("(p i) r -> p i r", i=4))
 
-        def load_w(g, a0=0, a1=PASSES):
-            piece = keep.tile([P, a1 - a0, 2 * P * EARLY], U8, name=f"wcodes{g}{a0}", align_bytes=64)
+        def load_w(group, a0, a1):
+            piece = keep.tile([P, a1 - a0, 2 * P * EARLY], U8, name=f"wcodes{group}{a0}", align_bytes=64)
             for a in range(a0, a1):
-                w_codes[g, a] = piece[:, a - a0, :]
-            nc.sync.dma_start(
-                out=piece[:].bitcast(I32),
-                in_=w4_words.bitcast(I32).rearrange("a p c -> p a c")[:, a0:a1, 64 * EARLY * g : 64 * EARLY * (g + 1)],
-            )
+                w_codes[group, a] = piece[:, a - a0, :]
+            per_group = 2 * P * EARLY // 4
+            words = w4_words.bitcast(I32).rearrange("a p c -> p a c")
+            nc.sync.dma_start(out=piece[:].bitcast(I32), in_=words[:, a0:a1, per_group * group : per_group * (group + 1)])
 
         def load_u(c):
-            nc.sync.dma_start(out=u_raw[c][:], in_=up.rearrange("(p t) n -> p t n", t=4)[:, :, U_COLS * c : U_COLS * c + U_COLS])
+            rows = up.rearrange("(p i) n -> p i n", i=4)
+            nc.sync.dma_start(out=u_raw[c][:], in_=rows[:, :, U_COLS * c : U_COLS * c + U_COLS])
 
-        def extra(k):
-            if k == W_AT and k == W2_AT:
-                load_w(0)
-            elif k == W_AT:
-                load_w(0, 0, 2)
-            elif k == W2_AT:
-                load_w(0, 2, 3)
-            if k == D_AT:
-                load_d(0)
-
-        for a in range(PASSES):
-            for t in range(4):
-                extra(4 * a + t)
-                load_x(a, t)
-                if (a, t) == (0, 0):
-                    for c0 in range(0, S, FIRST):
-                        nc.sync.dma_start(weights[:, c0 : c0 + FIRST], wgt[:, c0 : c0 + FIRST])
-        extra(12)
+        load_x(0, 0)
+        for c0 in (0, HALF):
+            nc.sync.dma_start(weights[:, c0 : c0 + HALF], wgt[:, c0 : c0 + HALF])
+        for a, i in [(a, i) for a in range(PASSES) for i in range(4)][1:-2]:
+            load_x(a, i)
+        load_w(0, 0, LAST)
+        load_x(LAST, 2)
+        load_d(0)
+        load_x(LAST, 3)
         load_d(1)
-        extra(13)
-        load_d(2)
-        for item in POST.split():
-            if item[0] == "u":
-                load_u(int(item[1]))
-            else:
-                load_w(1, int(item[1]), int(item[2]))
+        load_w(0, LAST, PASSES)
+        load_d(LAST)
+        load_u(0)
+        load_w(1, 0, LAST)
+        for c in range(1, QUARTERS):
+            load_u(c)
+        load_w(1, LAST, PASSES)
 
-        def gather(a, t):
-            width = FIRST if (a, t) == (0, 0) else S
-            for c0 in range(0, S, width):
-                cols = slice(c0, c0 + width)
-                nc.vector.tensor_tensor(
-                    picked[a][:, t, cols], x[a][t][:].indirect(offsets[:, c0 // 16 : (c0 + width) // 16]), weights[:, cols], MULT
-                )
+        def gather(a, i, c0, c1):
+            window = x_plane[a][i][:].indirect(offsets[:, c0 // 16 : c1 // 16])
+            nc.vector.tensor_tensor(picked[a][:, i, c0:c1], window, weights[:, c0:c1], MULT)
 
-        def copy_on(engine):
-            return nc.scalar.copy if engine == "S" else nc.vector.tensor_copy
-
-        def interleave(dst, src, c0, c1, engine):
-            copy_on(engine)(
-                out=dst[:, c0:c1, :].rearrange("p (c i) t -> p c t i", i=4),
-                in_=src[:, :, c0:c1].rearrange("p t (c i) -> p c t i", i=4),
+        def interleave(copy, grouped, planes, c0, c1):
+            copy(
+                out=grouped[:, c0:c1, :].rearrange("p (c e) i -> p c i e", e=4),
+                in_=planes[:, :, c0:c1].rearrange("p i (c e) -> p c i e", e=4),
             )
 
         def quantize(codes, scales, grouped):
             nc.vector.quantize_mx(out=codes.bitcast(E4M3), scales=scales, in_=grouped)
 
-        def quantize_x(a):
-            x_codes[a] = keep.tile([P, S], U32, name=f"x{a + 1}{HOLD[a]}" if a + 1 < PASSES else "xcodes", align_bytes=64)
-            quantize(x_codes[a][:], x_scales[a][:], x_grouped[a][:].rearrange("p c t -> p (c t)"))
+        def quantize_x(a, buffer):
+            x_codes[a] = keep.tile([P, S], U32, name=buffer, align_bytes=64)
+            quantize(x_codes[a][:], x_scales[a][:], x_grouped[a][:].rearrange("p c i -> p (c i)"))
 
-        def group_d(a, first, m0, m1, t0, engine):
-            copy_on(engine)(
-                out=d_grouped[a][:].rearrange("p (t m j) -> p m j t", t=4, j=4)[:, first + m0 : first + m1, :, t0 : t0 + 2],
-                in_=d_raw[a, first][:].rearrange("p j (m t) -> p m j t", t=4)[:, m0:m1, :, t0 : t0 + 2],
-            )
+        def interleave_d(a):
+            for m0, m1 in d_pieces[a]:
+                target = d_grouped[a][:].rearrange("p (t m i) -> p m i t", t=4, i=4)[:, m0:m1]
+                source = d_raw[a, m0][:].rearrange("p i (m t) -> p m i t", t=4)
+                cut = D_ON_SCALAR[a] * (m1 - m0) // P
+                for copy, first, end, t0 in ((on_scalar, 0, m1 - m0, 2), (on_scalar, 0, cut, 0), (on_vector, cut, m1 - m0, 0)):
+                    copy(out=target[:, first:end, :, t0 : t0 + 2], in_=source[:, first:end, :, t0 : t0 + 2])
 
-        def prepare_d(a):
-            for first, end in zip(d_cuts[a], d_cuts[a][1:]):
-                width = end - first
-                share = D_SPLIT[a] * width // P // 2 * 2
-                upper, lower = min(share, width), max(share - width, 0)
-                group_d(a, first, 0, upper, 2, "S")
-                if lower > 0:
-                    group_d(a, first, 0, lower, 0, "S")
-                if lower < width:
-                    group_d(a, first, lower, width, 0, "V")
-                if upper < width:
-                    group_d(a, first, upper, width, 2, "V")
+        def quantize_d(a, t0, t1):
+            cols = slice(P * t0, P * t1)
+            quantize(d_codes[a][:, cols], d_scales[a][:, cols], d_grouped[a][:, 4 * P * t0 : 4 * P * t1])
 
-        def quantize_d(a, t0=0, t1=4):
-            quantize(d_codes[a][:, 128 * t0 : 128 * t1], d_scales[a][:, 128 * t0 : 128 * t1], d_grouped[a][:, 512 * t0 : 512 * t1])
+        def interleave_u(c, copy, buffer):
+            u_grouped[c] = keep.tile([P, U_COLS, 4], BF16, name=buffer, align_bytes=64)
+            interleave(copy, u_grouped[c], u_raw[c], 0, U_COLS)
 
         def quantize_u(c):
-            quantize(u_codes[c][:], u_scales[c][:], u_grouped[c][:].rearrange("p c t -> p (c t)"))
+            quantize(u_codes[c][:], u_scales[c][:], u_grouped[c][:].rearrange("p c i -> p (c i)"))
 
+        h_bank = [psum.tile([P, 4, CHUNK], F32, name=f"bank{q}") for q in range(CHUNKS)]
+
+        def multiply_down(q, a):
+            cols = slice(CHUNK * q, CHUNK * q + CHUNK)
+            for t in range(4):
+                nc.tensor.matmul_mx(
+                    out=h_bank[q][:, t, :],
+                    lhsT=d_codes[a][:, P * t : P * t + P].bitcast(E4M3),
+                    lhsT_scale=d_scales[a][:, P * t : P * t + P],
+                    rhs=x_codes[a][:, cols].bitcast(E4M3),
+                    rhs_scale=x_scales[a][:, cols],
+                    start=(a == 0 and t == 0),
+                    stop=(a == LAST and t == 3),
+                )
+
+        out_bank = [f"acc{n}" for n in range(EARLY)] + [f"bank{q}" for q in range(TILES - EARLY - 1)] + [f"acc{EARLY - 1}"]
         acc = {}
 
-        def base(n, a):
+        def multiply_w4(n, a):
             if a == 0:
-                acc[n] = psum.tile([P, S], F32, name=(BANKS + (B7,))[n])
-            g, m = divmod(n, EARLY)
+                acc[n] = psum.tile([P, S], F32, name=out_bank[n])
+            group, m = divmod(n, EARLY)
             nc.tensor.matmul_mx(
                 out=acc[n][:],
-                lhsT=w_codes[g, a][:, 256 * m : 256 * m + 256].bitcast(E2M1),
-                lhsT_scale=w_scales[:, a, 128 * n : 128 * n + 128],
+                lhsT=w_codes[group, a][:, 2 * P * m : 2 * P * (m + 1)].bitcast(E2M1),
+                lhsT_scale=w_scales[:, a, P * n : P * n + P],
                 rhs=x_codes[a][:].bitcast(E4M3),
                 rhs_scale=x_scales[a][:],
                 start=(a == 0),
                 stop=False,
             )
 
-        h_bank = [psum.tile([P, 4, CHUNK], F32, name=f"bank{q}") for q in range(CHUNKS)]
-
-        def low_rank(q, a, t0=0, t1=4):
-            cols = slice(CHUNK * q, CHUNK * q + CHUNK)
-            for t in range(t0, t1):
-                nc.tensor.matmul_mx(
-                    out=h_bank[q][:, t, :],
-                    lhsT=d_codes[a][:, 128 * t : 128 * t + 128].bitcast(E4M3),
-                    lhsT_scale=d_scales[a][:, 128 * t : 128 * t + 128],
-                    rhs=x_codes[a][:, cols].bitcast(E4M3),
-                    rhs_scale=x_scales[a][:, cols],
-                    start=(a == 0 and t == 0),
-                    stop=(a == PASSES - 1 and t == 3),
-                )
-
-        def empty_h(q, engine):
-            copy_on(engine)(out=h_grouped[q // 2][:, CHUNK * (q % 2) : CHUNK * (q % 2) + CHUNK, :], in_=h_bank[q][:].rearrange("p t c -> p c t"))
-
-        def quantize_h(half):
-            cols = slice(256 * half, 256 * half + 256)
-            quantize(h_codes[:, cols], h_scales[:, cols], h_grouped[half][:].rearrange("p c t -> p (c t)"))
-
-        def finish(n, engine):
-            c, m = divmod(128 * n, U_COLS)
+        def close_and_store(n, copy, width):
+            c, first = divmod(P * n, U_COLS)
             nc.tensor.matmul_mx(
                 out=acc[n][:],
-                lhsT=u_codes[c][:, m : m + 128].bitcast(E4M3),
-                lhsT_scale=u_scales[c][:, m : m + 128],
+                lhsT=u_codes[c][:, first : first + P].bitcast(E4M3),
+                lhsT_scale=u_scales[c][:, first : first + P],
                 rhs=h_codes[:].bitcast(E4M3),
                 rhs_scale=h_scales[:],
                 start=False,
                 stop=True,
             )
-            staged[n] = keep.tile([P, S], F32, name="hsecond" if n == FIRST_V else f"staged{n}", align_bytes=64)
-            width = S // 2 if n in HALVES else S
+            staged = keep.tile([P, S], F32, name=f"staged{n}", align_bytes=64)
             for c0 in range(0, S, width):
-                copy_on(engine)(out=staged[n][:, c0 : c0 + width], in_=acc[n][:, c0 : c0 + width])
-                nc.sync.dma_start(out=out[128 * n : 128 * n + 128, c0 : c0 + width], in_=staged[n][:, c0 : c0 + width])
+                copy(out=staged[:, c0 : c0 + width], in_=acc[n][:, c0 : c0 + width])
+                nc.sync.dma_start(out=out[P * n : P * n + P, c0 : c0 + width], in_=staged[:, c0 : c0 + width])
 
-        def prepare_u(c):
-            u_grouped[c] = keep.tile([P, U_COLS, 4], BF16, name=UTAG[c], align_bytes=64)
-            if U_SPLIT[c] > 0:
-                interleave(u_grouped[c], u_raw[c], 0, U_SPLIT[c], "S")
-            if U_SPLIT[c] < U_COLS:
-                interleave(u_grouped[c], u_raw[c], U_SPLIT[c], U_COLS, "V")
-
-        last = PASSES - 1
         for a in range(PASSES):
-            for t in range(4):
-                gather(a, t)
-                if a > 0 and t == HOLD[a - 1]:
-                    quantize_x(a - 1)
-            split = X_SPLIT if a == last else S
-            if split > 0:
-                interleave(x_grouped[a], picked[a], 0, split, "S")
-            if split < S:
-                interleave(x_grouped[a], picked[a], split, S, "V")
-        quantize_x(last)
-        for a in range(last):
-            prepare_d(a)
-            quantize_d(a)
+            for i in range(4):
+                if (a, i) == (0, 0):
+                    gather(a, i, 0, HALF)
+                    gather(a, i, HALF, S)
+                else:
+                    gather(a, i, 0, S)
+                if a > 0 and i == 2:
+                    quantize_x(a - 1, f"x{a}{i}")
+            if a < LAST:
+                interleave(on_scalar, x_grouped[a], picked[a], 0, S)
+        interleave(on_scalar, x_grouped[LAST], picked[LAST], 0, X_ON_SCALAR)
+        interleave(on_vector, x_grouped[LAST], picked[LAST], X_ON_SCALAR, S)
+        quantize_x(LAST, "xcodes")
+
+        for a in range(LAST):
+            interleave_d(a)
+            quantize_d(a, 0, 4)
             for q in range(CHUNKS):
-                low_rank(q, a)
-        prepare_d(last)
-        quantize_d(last, 0, 2)
-        quantize_d(last, 2, 4)
-        prepare_u(0)
+                multiply_down(q, a)
+        interleave_d(LAST)
+        quantize_d(LAST, 0, 2)
+        quantize_d(LAST, 2, 4)
+        interleave_u(0, on_scalar, "ugrouped")
         quantize_u(0)
-        h_grouped = [keep.tile([P, S // 2, 4], BF16, name=name, align_bytes=64) for name in (H0, "hsecond")]
-        for q in range(LEAD):
-            low_rank(q, last, 0, 2)
+        h_grouped = [keep.tile([P, HALF, 4], BF16, name=f"hgrouped{half}", align_bytes=64) for half in range(2)]
         for q in range(CHUNKS):
-            low_rank(q, last, 2 if q < LEAD else 0, 4)
-            empty_h(q, HE[q])
-        quantize_h(0)
-        quantize_h(1)
+            multiply_down(q, LAST)
+            half, first = divmod(CHUNK * q, HALF)
+            copy = on_scalar if q % 2 else on_vector
+            copy(out=h_grouped[half][:, first : first + CHUNK, :], in_=h_bank[q][:].rearrange("p t c -> p c t"))
+        for half in range(2):
+            cols = slice(HALF * half, HALF * half + HALF)
+            quantize(h_codes[:, cols], h_scales[:, cols], h_grouped[half][:].rearrange("p c t -> p (c t)"))
+
         for a in range(PASSES):
             for n in range(EARLY):
-                base(n, a)
-        prepare_u(1)
-        prepare_u(2)
+                multiply_w4(n, a)
+        interleave_u(1, on_scalar, f"dcodes{LAST}")
+        interleave_u(2, on_vector, "hgrouped1")
         quantize_u(1)
-        if ORDER == 0:
-            quantize_u(2)
-            prepare_u(3)
-        else:
-            prepare_u(3)
-            quantize_u(2)
+        quantize_u(2)
+        interleave_u(3, on_vector, f"dcodes{LAST}")
         quantize_u(3)
         for n in range(TILES):
-            ahead = [EARLY, EARLY + 1] if n == EARLY else [n + 1]
-            if AHEAD == 0:
-                ahead = [n]
-            for k in ahead:
-                if n >= EARLY and k < TILES:
-                    for a in range(PASSES):
-                        base(k, a)
-            finish(n, EV[n])
+            if n >= EARLY:
+                for a in range(PASSES):
+                    multiply_w4(n, a)
+            copy = on_vector if n >= EARLY and n % 2 == 0 else on_scalar
+            close_and_store(n, copy, HALF if n == TILES - 1 else S)

@@ -27,7 +27,7 @@ U_COLS = 256
 QUARTERS = M // U_COLS
 
 X_ON_SCALAR = 128
-D_ON_SCALAR = (80, 48, 32)
+D_ON_SCALAR = (80, 64, 32)
 
 
 def tile_list_hlora_none_kernel(tc, xT, w4_words, w4_scales, down, up, wgt, offs, out):
@@ -215,7 +215,9 @@ def tile_list_hlora_none_kernel(tc, xT, w4_words, w4_scales, down, up, wgt, offs
         interleave_d(LAST)
         quantize_d(LAST, 0, 2)
         quantize_d(LAST, 2, 4)
-        interleave_u(0, on_scalar, "ugrouped")
+        u_grouped[0] = keep.tile([P, U_COLS, 4], BF16, name="ugrouped", align_bytes=64)
+        interleave(on_scalar, u_grouped[0], u_raw[0], 0, P)
+        interleave(on_vector, u_grouped[0], u_raw[0], P, U_COLS)
         quantize_u(0)
         h_grouped = [keep.tile([P, HALF, 4], BF16, name=f"hgrouped{half}", align_bytes=64) for half in range(2)]
         for q in range(CHUNKS):

@@ -26,8 +26,16 @@ HALF = S // 2
 U_COLS = 256
 QUARTERS = M // U_COLS
 
-X_ON_SCALAR = 128
-D_ON_SCALAR = (80, 64, 32)
+X_ON_SCALAR = 192
+D_ON_SCALAR = (80, 32, 16)
+ORDER = "x00 ga gb x01 x02 x03 x10 x11 x12 x13 x20 x21 d0 x22 e01 x23 d1 e2 d2a d2b u0 l01 u1 u2 u3 l2"
+SPLIT3 = (1, 1, 1)
+HOLD = (-1, -1)
+D0_FIRST = 0
+D0_HOLD = 0
+T0_HALF = 0
+U0S = 128
+QSPLIT = 0
 
 
 def tile_list_hlora_none_kernel(tc, xT, w4_words, w4_scales, down, up, wgt, offs, out):
@@ -41,10 +49,10 @@ def tile_list_hlora_none_kernel(tc, xT, w4_words, w4_scales, down, up, wgt, offs
         weights = keep.tile([P, S], F32, name="weights")
         x_plane = [[keep.tile([P, T], F32, name=f"x{a}{i}", align_bytes=64) for i in range(4)] for a in range(PASSES)]
         picked = [keep.tile([P, 4, S], F32, name=f"picked{a}") for a in range(PASSES)]
-        x_grouped = [keep.tile([P, S, 4], BF16, name=f"xgrouped{a}", align_bytes=64) for a in range(PASSES)]
+        x_grouped = [keep.tile([P, S, 4], BF16, name=f"xgrouped{a}", align_bytes=64) for a in range(LAST)]
         x_codes = {}
         x_scales = [keep.tile([P, S], U8, name=f"xscales{a}", align_bytes=64) for a in range(PASSES)]
-        d_pieces = [[(0, P)], [(0, P)], [(0, P // 2), (P // 2, P)]]
+        d_pieces = [[(0, P)] if f"d{a}" in ORDER.split() else [(0, P // 2), (P // 2, P)] for a in range(PASSES)]
         d_raw = {}
         for a in range(PASSES):
             for m0, m1 in d_pieces[a]:
@@ -73,8 +81,8 @@ def tile_list_hlora_none_kernel(tc, xT, w4_words, w4_scales, down, up, wgt, offs
             rows = xT[512 * a : 512 * a + 512, :].rearrange("(p i) c -> p i c", i=4)
             nc.sync.dma_start(out=x_plane[a][i][:], in_=rows[:, i, :])
 
-        def load_d(a):
-            for m0, m1 in d_pieces[a]:
+        def load_d(a, pieces):
+            for m0, m1 in pieces:
                 rows = down[512 * a : 512 * a + 512, 4 * m0 : 4 * m1]
                 nc.sync.dma_start(out=d_raw[a, m0][:], in_=rows.rearrange("(p i) r -> p i r", i=4))
 
@@ -90,23 +98,21 @@ def tile_list_hlora_none_kernel(tc, xT, w4_words, w4_scales, down, up, wgt, offs
             rows = up.rearrange("(p i) n -> p i n", i=4)
             nc.sync.dma_start(out=u_raw[c][:], in_=rows[:, :, U_COLS * c : U_COLS * c + U_COLS])
 
-        load_x(0, 0)
-        for c0 in (0, HALF):
-            nc.sync.dma_start(weights[:, c0 : c0 + HALF], wgt[:, c0 : c0 + HALF])
-        for a, i in [(a, i) for a in range(PASSES) for i in range(4)][1:-2]:
-            load_x(a, i)
-        load_w(0, 0, LAST)
-        load_x(LAST, 2)
-        load_d(0)
-        load_x(LAST, 3)
-        load_d(1)
-        load_w(0, LAST, PASSES)
-        load_d(LAST)
-        load_u(0)
-        load_w(1, 0, LAST)
-        for c in range(1, QUARTERS):
-            load_u(c)
-        load_w(1, LAST, PASSES)
+        for w in ORDER.split():
+            if w[0] == "x":
+                load_x(int(w[1]), int(w[2]))
+            elif w == "g":
+                nc.sync.dma_start(weights[:], wgt)
+            elif w[0] == "g":
+                c0 = HALF * (w[1] == "b")
+                nc.sync.dma_start(weights[:, c0 : c0 + HALF], wgt[:, c0 : c0 + HALF])
+            elif w[0] == "d":
+                a = int(w[1])
+                load_d(a, d_pieces[a] if len(w) == 2 else [d_pieces[a][w[2] == "b"]])
+            elif w[0] == "u":
+                load_u(int(w[1]))
+            else:
+                load_w(int(w[0] == "l"), int(w[1]), int(w[-1]) + 1)
 
         def gather(a, i, c0, c1):
             window = x_plane[a][i][:].indirect(offsets[:, c0 // 16 : c1 // 16])
@@ -131,7 +137,8 @@ def tile_list_hlora_none_kernel(tc, xT, w4_words, w4_scales, down, up, wgt, offs
                 source = d_raw[a, m0][:].rearrange("p i (m t) -> p m i t", t=4)
                 cut = D_ON_SCALAR[a] * (m1 - m0) // P
                 for copy, first, end, t0 in ((on_scalar, 0, m1 - m0, 2), (on_scalar, 0, cut, 0), (on_vector, cut, m1 - m0, 0)):
-                    copy(out=target[:, first:end, :, t0 : t0 + 2], in_=source[:, first:end, :, t0 : t0 + 2])
+                    if first < end:
+                        copy(out=target[:, first:end, :, t0 : t0 + 2], in_=source[:, first:end, :, t0 : t0 + 2])
 
         def quantize_d(a, t0, t1):
             cols = slice(P * t0, P * t1)
@@ -192,32 +199,48 @@ def tile_list_hlora_none_kernel(tc, xT, w4_words, w4_scales, down, up, wgt, offs
                 copy(out=staged[:, c0 : c0 + width], in_=acc[n][:, c0 : c0 + width])
                 nc.sync.dma_start(out=out[P * n : P * n + P, c0 : c0 + width], in_=staged[:, c0 : c0 + width])
 
-        for a in range(PASSES):
-            for i in range(4):
-                if (a, i) == (0, 0):
-                    gather(a, i, 0, HALF)
-                    gather(a, i, HALF, S)
-                else:
-                    gather(a, i, 0, S)
-                if a > 0 and i == 2:
-                    quantize_x(a - 1, f"x{a}{i}")
-            if a < LAST:
-                interleave(on_scalar, x_grouped[a], picked[a], 0, S)
-        interleave(on_scalar, x_grouped[LAST], picked[LAST], 0, X_ON_SCALAR)
-        interleave(on_vector, x_grouped[LAST], picked[LAST], X_ON_SCALAR, S)
-        quantize_x(LAST, "xcodes")
-
-        for a in range(LAST):
+        def d_pass(a):
             interleave_d(a)
             quantize_d(a, 0, 4)
             for q in range(CHUNKS):
                 multiply_down(q, a)
+
+        for a in range(PASSES):
+            for i in range(4):
+                if ((a, i) == (0, 0) and "ga" in ORDER) or (i == 3 and SPLIT3[a]):
+                    gather(a, i, 0, HALF)
+                    gather(a, i, HALF, S)
+                else:
+                    gather(a, i, 0, S)
+                if a > 0 and i == max(HOLD[a - 1], 0):
+                    quantize_x(a - 1, f"x{a}{i}" if HOLD[a - 1] >= 0 else f"xc{a}")
+            if a < LAST:
+                if SPLIT3[a]:
+                    interleave(on_scalar, x_grouped[a], picked[a], 0, HALF)
+                    interleave(on_scalar, x_grouped[a], picked[a], HALF, S)
+                else:
+                    interleave(on_scalar, x_grouped[a], picked[a], 0, S)
+        if D0_FIRST:
+            d_pass(0)
+        x_grouped.append(keep.tile([P, S, 4], BF16, name="dgrouped0" if D0_HOLD else "xgrouped2", align_bytes=64))
+        interleave(on_scalar, x_grouped[LAST], picked[LAST], 0, X_ON_SCALAR)
+        if SPLIT3[LAST] and X_ON_SCALAR < HALF:
+            interleave(on_vector, x_grouped[LAST], picked[LAST], X_ON_SCALAR, HALF)
+            interleave(on_vector, x_grouped[LAST], picked[LAST], HALF, S)
+        else:
+            interleave(on_vector, x_grouped[LAST], picked[LAST], X_ON_SCALAR, S)
+        quantize_x(LAST, "xcodes")
+
+        for a in range(1 if D0_FIRST else 0, LAST):
+            d_pass(a)
         interleave_d(LAST)
         quantize_d(LAST, 0, 2)
         quantize_d(LAST, 2, 4)
         u_grouped[0] = keep.tile([P, U_COLS, 4], BF16, name="ugrouped", align_bytes=64)
-        interleave(on_scalar, u_grouped[0], u_raw[0], 0, P)
-        interleave(on_vector, u_grouped[0], u_raw[0], P, U_COLS)
+        if U0S:
+            interleave(on_scalar, u_grouped[0], u_raw[0], 0, U0S)
+        if U0S < U_COLS:
+            interleave(on_vector, u_grouped[0], u_raw[0], U0S, U_COLS)
         quantize_u(0)
         h_grouped = [keep.tile([P, HALF, 4], BF16, name=f"hgrouped{half}", align_bytes=64) for half in range(2)]
         for q in range(CHUNKS):
@@ -243,4 +266,4 @@ def tile_list_hlora_none_kernel(tc, xT, w4_words, w4_scales, down, up, wgt, offs
                 for a in range(PASSES):
                     multiply_w4(n, a)
             copy = on_vector if n >= EARLY and n % 2 == 0 else on_scalar
-            close_and_store(n, copy, HALF if n == TILES - 1 else S)
+            close_and_store(n, copy, HALF if n == TILES - 1 or (n == 0 and T0_HALF) else S)

@@ -25,6 +25,7 @@ CHUNKS = S // CHUNK
 HALF = S // 2
 U_COLS = 256
 QUARTERS = M // U_COLS
+ALIGN = 256
 
 X_ON_SCALAR = 192
 D_ON_SCALAR = (80, 32, 16)
@@ -46,28 +47,28 @@ def tile_list_hlora_none_kernel(tc, xT, w4_words, w4_scales, down, up, wgt, offs
         psum = ctx.enter_context(tc.psum_pool(name="psum", bufs=1))
 
         offsets = keep.tile([P, S // 16], U16, name="offsets")
-        weights = keep.tile([P, S], F32, name="weights")
-        x_plane = [[keep.tile([P, T], F32, name=f"x{a}{i}", align_bytes=64) for i in range(4)] for a in range(PASSES)]
-        picked = [keep.tile([P, 4, S], F32, name=f"picked{a}") for a in range(PASSES)]
-        x_grouped = [keep.tile([P, S, 4], BF16, name=f"xgrouped{a}", align_bytes=64) for a in range(LAST)]
+        weights = keep.tile([P, S], F32, name="weights", align_bytes=ALIGN)
+        x_plane = [[keep.tile([P, T], F32, name=f"x{a}{i}", align_bytes=ALIGN) for i in range(4)] for a in range(PASSES)]
+        picked = [keep.tile([P, 4, S], F32, name=f"picked{a}", align_bytes=ALIGN) for a in range(PASSES)]
+        x_grouped = [keep.tile([P, S, 4], BF16, name=f"xgrouped{a}", align_bytes=ALIGN) for a in range(LAST)]
         x_codes = {}
-        x_scales = [keep.tile([P, S], U8, name=f"xscales{a}", align_bytes=64) for a in range(PASSES)]
+        x_scales = [keep.tile([P, S], U8, name=f"xscales{a}", align_bytes=ALIGN) for a in range(PASSES)]
         d_pieces = [[(0, P)] if f"d{a}" in ORDER.split() else [(0, P // 2), (P // 2, P)] for a in range(PASSES)]
         d_raw = {}
         for a in range(PASSES):
             for m0, m1 in d_pieces[a]:
-                d_raw[a, m0] = keep.tile([P, 4, 4 * (m1 - m0)], F32, name=f"draw{a}{m0}")
-        d_grouped = [keep.tile([P, R * 4], BF16, name=f"dgrouped{a}", align_bytes=64) for a in range(PASSES)]
-        d_codes = [keep.tile([P, R], U32, name=f"dcodes{a}", align_bytes=64) for a in range(PASSES)]
-        d_scales = [keep.tile([P, R], U8, name=f"dscales{a}", align_bytes=64) for a in range(PASSES)]
-        u_raw = [keep.tile([P, 4, U_COLS], F32, name=f"uraw{c}") for c in range(QUARTERS)]
+                d_raw[a, m0] = keep.tile([P, 4, 4 * (m1 - m0)], F32, name=f"draw{a}{m0}", align_bytes=ALIGN)
+        d_grouped = [keep.tile([P, R * 4], BF16, name=f"dgrouped{a}", align_bytes=ALIGN) for a in range(PASSES)]
+        d_codes = [keep.tile([P, R], U32, name=f"dcodes{a}", align_bytes=ALIGN) for a in range(PASSES)]
+        d_scales = [keep.tile([P, R], U8, name=f"dscales{a}", align_bytes=ALIGN) for a in range(PASSES)]
+        u_raw = [keep.tile([P, 4, U_COLS], F32, name=f"uraw{c}", align_bytes=ALIGN) for c in range(QUARTERS)]
         u_grouped = {}
-        u_codes = [keep.tile([P, U_COLS], U32, name=f"ucodes{c}", align_bytes=64) for c in range(QUARTERS)]
-        u_scales = [keep.tile([P, U_COLS], U8, name=f"uscales{c}", align_bytes=64) for c in range(QUARTERS)]
+        u_codes = [keep.tile([P, U_COLS], U32, name=f"ucodes{c}", align_bytes=ALIGN) for c in range(QUARTERS)]
+        u_scales = [keep.tile([P, U_COLS], U8, name=f"uscales{c}", align_bytes=ALIGN) for c in range(QUARTERS)]
         w_codes = {}
-        w_scales = keep.tile([P, PASSES, M], U8, name="wscales", align_bytes=64)
-        h_codes = keep.tile([P, S], U32, name="hcodes", align_bytes=64)
-        h_scales = keep.tile([P, S], U8, name="hscales", align_bytes=64)
+        w_scales = keep.tile([P, PASSES, M], U8, name="wscales", align_bytes=ALIGN)
+        h_codes = keep.tile([P, S], U32, name="hcodes", align_bytes=ALIGN)
+        h_scales = keep.tile([P, S], U8, name="hscales", align_bytes=ALIGN)
 
         nc.sync.dma_start(offsets[:], offs)
         nc.gpsimd.memset(w_scales[:].bitcast(I32), 0)
@@ -87,7 +88,7 @@ def tile_list_hlora_none_kernel(tc, xT, w4_words, w4_scales, down, up, wgt, offs
                 nc.sync.dma_start(out=d_raw[a, m0][:], in_=rows.rearrange("(p i) r -> p i r", i=4))
 
         def load_w(group, a0, a1):
-            piece = keep.tile([P, a1 - a0, 2 * P * EARLY], U8, name=f"wcodes{group}{a0}", align_bytes=64)
+            piece = keep.tile([P, a1 - a0, 2 * P * EARLY], U8, name=f"wcodes{group}{a0}", align_bytes=ALIGN)
             for a in range(a0, a1):
                 w_codes[group, a] = piece[:, a - a0, :]
             per_group = 2 * P * EARLY // 4
@@ -128,7 +129,7 @@ def tile_list_hlora_none_kernel(tc, xT, w4_words, w4_scales, down, up, wgt, offs
             nc.vector.quantize_mx(out=codes.bitcast(E4M3), scales=scales, in_=grouped)
 
         def quantize_x(a, buffer):
-            x_codes[a] = keep.tile([P, S], U32, name=buffer, align_bytes=64)
+            x_codes[a] = keep.tile([P, S], U32, name=buffer, align_bytes=ALIGN)
             quantize(x_codes[a][:], x_scales[a][:], x_grouped[a][:].rearrange("p c i -> p (c i)"))
 
         def interleave_d(a):
@@ -145,7 +146,7 @@ def tile_list_hlora_none_kernel(tc, xT, w4_words, w4_scales, down, up, wgt, offs
             quantize(d_codes[a][:, cols], d_scales[a][:, cols], d_grouped[a][:, 4 * P * t0 : 4 * P * t1])
 
         def interleave_u(c, copy, buffer):
-            u_grouped[c] = keep.tile([P, U_COLS, 4], BF16, name=buffer, align_bytes=64)
+            u_grouped[c] = keep.tile([P, U_COLS, 4], BF16, name=buffer, align_bytes=ALIGN)
             interleave(copy, u_grouped[c], u_raw[c], 0, U_COLS)
 
         def quantize_u(c):
@@ -194,7 +195,7 @@ def tile_list_hlora_none_kernel(tc, xT, w4_words, w4_scales, down, up, wgt, offs
                 start=False,
                 stop=True,
             )
-            staged = keep.tile([P, S], F32, name=f"staged{n}", align_bytes=64)
+            staged = keep.tile([P, S], F32, name=f"staged{n}", align_bytes=ALIGN)
             for c0 in range(0, S, width):
                 copy(out=staged[:, c0 : c0 + width], in_=acc[n][:, c0 : c0 + width])
                 nc.sync.dma_start(out=out[P * n : P * n + P, c0 : c0 + width], in_=staged[:, c0 : c0 + width])
@@ -222,7 +223,7 @@ def tile_list_hlora_none_kernel(tc, xT, w4_words, w4_scales, down, up, wgt, offs
                     interleave(on_scalar, x_grouped[a], picked[a], 0, S)
         if D0_FIRST:
             d_pass(0)
-        x_grouped.append(keep.tile([P, S, 4], BF16, name="dgrouped0" if D0_HOLD else "xgrouped2", align_bytes=64))
+        x_grouped.append(keep.tile([P, S, 4], BF16, name="dgrouped0" if D0_HOLD else "xgrouped2", align_bytes=ALIGN))
         interleave(on_scalar, x_grouped[LAST], picked[LAST], 0, X_ON_SCALAR)
         if SPLIT3[LAST] and X_ON_SCALAR < HALF:
             interleave(on_vector, x_grouped[LAST], picked[LAST], X_ON_SCALAR, HALF)
@@ -236,13 +237,13 @@ def tile_list_hlora_none_kernel(tc, xT, w4_words, w4_scales, down, up, wgt, offs
         interleave_d(LAST)
         quantize_d(LAST, 0, 2)
         quantize_d(LAST, 2, 4)
-        u_grouped[0] = keep.tile([P, U_COLS, 4], BF16, name="ugrouped", align_bytes=64)
+        u_grouped[0] = keep.tile([P, U_COLS, 4], BF16, name="ugrouped", align_bytes=ALIGN)
         if U0S:
             interleave(on_scalar, u_grouped[0], u_raw[0], 0, U0S)
         if U0S < U_COLS:
             interleave(on_vector, u_grouped[0], u_raw[0], U0S, U_COLS)
         quantize_u(0)
-        h_grouped = [keep.tile([P, HALF, 4], BF16, name=f"hgrouped{half}", align_bytes=64) for half in range(2)]
+        h_grouped = [keep.tile([P, HALF, 4], BF16, name=f"hgrouped{half}", align_bytes=ALIGN) for half in range(2)]
         for q in range(CHUNKS):
             multiply_down(q, LAST)
             half, first = divmod(CHUNK * q, HALF)

@@ -28,15 +28,7 @@ QUARTERS = M // U_COLS
 ALIGN = 256
 
 X_ON_SCALAR = 192
-D_ON_SCALAR = (80, 32, 16)
-ORDER = "x00 ga gb x01 x02 x03 x10 x11 x12 x13 x20 x21 d0 x22 e01 x23 d1 e2 d2a d2b u0 l01 u1 u2 u3 l2"
-SPLIT3 = (1, 1, 1)
-HOLD = (-1, -1)
-D0_FIRST = 0
-D0_HOLD = 0
-T0_HALF = 0
-U0S = 128
-QSPLIT = 0
+D_ON_SCALAR = (80, 48, 32)
 
 
 def tile_list_hlora_none_kernel(tc, xT, w4_words, w4_scales, down, up, wgt, offs, out):
@@ -53,7 +45,8 @@ def tile_list_hlora_none_kernel(tc, xT, w4_words, w4_scales, down, up, wgt, offs
         x_grouped = [keep.tile([P, S, 4], BF16, name=f"xgrouped{a}", align_bytes=ALIGN) for a in range(LAST)]
         x_codes = {}
         x_scales = [keep.tile([P, S], U8, name=f"xscales{a}", align_bytes=ALIGN) for a in range(PASSES)]
-        d_pieces = [[(0, P)] if f"d{a}" in ORDER.split() else [(0, P // 2), (P // 2, P)] for a in range(PASSES)]
+        whole, halves = [(0, P)], [(0, P // 2), (P // 2, P)]
+        d_pieces = [whole] * LAST + [halves]
         d_raw = {}
         for a in range(PASSES):
             for m0, m1 in d_pieces[a]:
@@ -78,11 +71,12 @@ def tile_list_hlora_none_kernel(tc, xT, w4_words, w4_scales, down, up, wgt, offs
                 in_=w4_scales[:, 4 * q : 4 * q + 4, :].bitcast(I32).rearrange("a q c -> q a c"),
             )
 
-        def load_x(a, i):
+        def load_x(a, *planes):
             rows = xT[512 * a : 512 * a + 512, :].rearrange("(p i) c -> p i c", i=4)
-            nc.sync.dma_start(out=x_plane[a][i][:], in_=rows[:, i, :])
+            for i in planes:
+                nc.sync.dma_start(out=x_plane[a][i][:], in_=rows[:, i, :])
 
-        def load_d(a, pieces):
+        def load_d(a, *pieces):
             for m0, m1 in pieces:
                 rows = down[512 * a : 512 * a + 512, 4 * m0 : 4 * m1]
                 nc.sync.dma_start(out=d_raw[a, m0][:], in_=rows.rearrange("(p i) r -> p i r", i=4))
@@ -95,25 +89,28 @@ def tile_list_hlora_none_kernel(tc, xT, w4_words, w4_scales, down, up, wgt, offs
             words = w4_words.bitcast(I32).rearrange("a p c -> p a c")
             nc.sync.dma_start(out=piece[:].bitcast(I32), in_=words[:, a0:a1, per_group * group : per_group * (group + 1)])
 
-        def load_u(c):
+        def load_u(*quarters):
             rows = up.rearrange("(p i) n -> p i n", i=4)
-            nc.sync.dma_start(out=u_raw[c][:], in_=rows[:, :, U_COLS * c : U_COLS * c + U_COLS])
+            for c in quarters:
+                nc.sync.dma_start(out=u_raw[c][:], in_=rows[:, :, U_COLS * c : U_COLS * c + U_COLS])
 
-        for w in ORDER.split():
-            if w[0] == "x":
-                load_x(int(w[1]), int(w[2]))
-            elif w == "g":
-                nc.sync.dma_start(weights[:], wgt)
-            elif w[0] == "g":
-                c0 = HALF * (w[1] == "b")
-                nc.sync.dma_start(weights[:, c0 : c0 + HALF], wgt[:, c0 : c0 + HALF])
-            elif w[0] == "d":
-                a = int(w[1])
-                load_d(a, d_pieces[a] if len(w) == 2 else [d_pieces[a][w[2] == "b"]])
-            elif w[0] == "u":
-                load_u(int(w[1]))
-            else:
-                load_w(int(w[0] == "l"), int(w[1]), int(w[-1]) + 1)
+        load_x(0, 0)
+        for c0 in (0, HALF):
+            nc.sync.dma_start(weights[:, c0 : c0 + HALF], wgt[:, c0 : c0 + HALF])
+        load_x(0, 1, 2, 3)
+        load_x(1, 0, 1, 2, 3)
+        load_x(LAST, 0, 1)
+        load_d(0, *whole)
+        load_x(LAST, 2)
+        load_w(0, 0, LAST)
+        load_x(LAST, 3)
+        load_d(1, *whole)
+        load_w(0, LAST, PASSES)
+        load_d(LAST, *halves)
+        load_u(0)
+        load_w(1, 0, LAST)
+        load_u(1, 2, 3)
+        load_w(1, LAST, PASSES)
 
         def gather(a, i, c0, c1):
             window = x_plane[a][i][:].indirect(offsets[:, c0 // 16 : c1 // 16])
@@ -128,8 +125,8 @@ def tile_list_hlora_none_kernel(tc, xT, w4_words, w4_scales, down, up, wgt, offs
         def quantize(codes, scales, grouped):
             nc.vector.quantize_mx(out=codes.bitcast(E4M3), scales=scales, in_=grouped)
 
-        def quantize_x(a, buffer):
-            x_codes[a] = keep.tile([P, S], U32, name=buffer, align_bytes=ALIGN)
+        def quantize_x(a):
+            x_codes[a] = keep.tile([P, S], U32, name=f"xcodes{a}", align_bytes=ALIGN)
             quantize(x_codes[a][:], x_scales[a][:], x_grouped[a][:].rearrange("p c i -> p (c i)"))
 
         def interleave_d(a):
@@ -138,8 +135,7 @@ def tile_list_hlora_none_kernel(tc, xT, w4_words, w4_scales, down, up, wgt, offs
                 source = d_raw[a, m0][:].rearrange("p i (m t) -> p m i t", t=4)
                 cut = D_ON_SCALAR[a] * (m1 - m0) // P
                 for copy, first, end, t0 in ((on_scalar, 0, m1 - m0, 2), (on_scalar, 0, cut, 0), (on_vector, cut, m1 - m0, 0)):
-                    if first < end:
-                        copy(out=target[:, first:end, :, t0 : t0 + 2], in_=source[:, first:end, :, t0 : t0 + 2])
+                    copy(out=target[:, first:end, :, t0 : t0 + 2], in_=source[:, first:end, :, t0 : t0 + 2])
 
         def quantize_d(a, t0, t1):
             cols = slice(P * t0, P * t1)
@@ -200,48 +196,33 @@ def tile_list_hlora_none_kernel(tc, xT, w4_words, w4_scales, down, up, wgt, offs
                 copy(out=staged[:, c0 : c0 + width], in_=acc[n][:, c0 : c0 + width])
                 nc.sync.dma_start(out=out[P * n : P * n + P, c0 : c0 + width], in_=staged[:, c0 : c0 + width])
 
-        def d_pass(a):
+        for a in range(PASSES):
+            for i in range(4):
+                width = HALF if (a, i) == (0, 0) or i == 3 else S
+                for c0 in range(0, S, width):
+                    gather(a, i, c0, c0 + width)
+                if a > 0 and i == 0:
+                    quantize_x(a - 1)
+            if a < LAST:
+                for c0 in (0, HALF):
+                    interleave(on_scalar, x_grouped[a], picked[a], c0, c0 + HALF)
+        x_grouped.append(keep.tile([P, S, 4], BF16, name=f"xgrouped{LAST}", align_bytes=ALIGN))
+        interleave(on_scalar, x_grouped[LAST], picked[LAST], 0, X_ON_SCALAR)
+        interleave(on_vector, x_grouped[LAST], picked[LAST], X_ON_SCALAR, HALF)
+        interleave(on_vector, x_grouped[LAST], picked[LAST], HALF, S)
+        quantize_x(LAST)
+
+        for a in range(LAST):
             interleave_d(a)
             quantize_d(a, 0, 4)
             for q in range(CHUNKS):
                 multiply_down(q, a)
-
-        for a in range(PASSES):
-            for i in range(4):
-                if ((a, i) == (0, 0) and "ga" in ORDER) or (i == 3 and SPLIT3[a]):
-                    gather(a, i, 0, HALF)
-                    gather(a, i, HALF, S)
-                else:
-                    gather(a, i, 0, S)
-                if a > 0 and i == max(HOLD[a - 1], 0):
-                    quantize_x(a - 1, f"x{a}{i}" if HOLD[a - 1] >= 0 else f"xc{a}")
-            if a < LAST:
-                if SPLIT3[a]:
-                    interleave(on_scalar, x_grouped[a], picked[a], 0, HALF)
-                    interleave(on_scalar, x_grouped[a], picked[a], HALF, S)
-                else:
-                    interleave(on_scalar, x_grouped[a], picked[a], 0, S)
-        if D0_FIRST:
-            d_pass(0)
-        x_grouped.append(keep.tile([P, S, 4], BF16, name="dgrouped0" if D0_HOLD else "xgrouped2", align_bytes=ALIGN))
-        interleave(on_scalar, x_grouped[LAST], picked[LAST], 0, X_ON_SCALAR)
-        if SPLIT3[LAST] and X_ON_SCALAR < HALF:
-            interleave(on_vector, x_grouped[LAST], picked[LAST], X_ON_SCALAR, HALF)
-            interleave(on_vector, x_grouped[LAST], picked[LAST], HALF, S)
-        else:
-            interleave(on_vector, x_grouped[LAST], picked[LAST], X_ON_SCALAR, S)
-        quantize_x(LAST, "xcodes")
-
-        for a in range(1 if D0_FIRST else 0, LAST):
-            d_pass(a)
         interleave_d(LAST)
         quantize_d(LAST, 0, 2)
         quantize_d(LAST, 2, 4)
         u_grouped[0] = keep.tile([P, U_COLS, 4], BF16, name="ugrouped", align_bytes=ALIGN)
-        if U0S:
-            interleave(on_scalar, u_grouped[0], u_raw[0], 0, U0S)
-        if U0S < U_COLS:
-            interleave(on_vector, u_grouped[0], u_raw[0], U0S, U_COLS)
+        interleave(on_scalar, u_grouped[0], u_raw[0], 0, P)
+        interleave(on_vector, u_grouped[0], u_raw[0], P, U_COLS)
         quantize_u(0)
         h_grouped = [keep.tile([P, HALF, 4], BF16, name=f"hgrouped{half}", align_bytes=ALIGN) for half in range(2)]
         for q in range(CHUNKS):
@@ -267,4 +248,4 @@ def tile_list_hlora_none_kernel(tc, xT, w4_words, w4_scales, down, up, wgt, offs
                 for a in range(PASSES):
                     multiply_w4(n, a)
             copy = on_vector if n >= EARLY and n % 2 == 0 else on_scalar
-            close_and_store(n, copy, HALF if n == TILES - 1 or (n == 0 and T0_HALF) else S)
+            close_and_store(n, copy, HALF if n == TILES - 1 else S)

@@ -38,38 +38,36 @@ def tile_list_hlora_none_kernel(tc, xT, w4_words, w4_scales, down, up, wgt, offs
         keep = ctx.enter_context(tc.tile_pool(name="keep", bufs=1))
         psum = ctx.enter_context(tc.psum_pool(name="psum", bufs=1))
 
+        def sbuf(shape, dtype, name):
+            return keep.tile(shape, dtype, name=name, align_bytes=ALIGN)
+
         offsets = keep.tile([P, S // 16], U16, name="offsets")
-        weights = keep.tile([P, S], F32, name="weights", align_bytes=ALIGN)
-        x_plane = [[keep.tile([P, T], F32, name=f"x{a}{i}", align_bytes=ALIGN) for i in range(4)] for a in range(PASSES)]
-        picked = [keep.tile([P, 4, S], F32, name=f"picked{a}", align_bytes=ALIGN) for a in range(PASSES)]
-        x_grouped = [keep.tile([P, S, 4], BF16, name=f"xgrouped{a}", align_bytes=ALIGN) for a in range(LAST)]
-        x_codes = {}
-        x_scales = [keep.tile([P, S], U8, name=f"xscales{a}", align_bytes=ALIGN) for a in range(PASSES)]
+        weights = sbuf([P, S], F32, "weights")
+        x_plane = [[sbuf([P, T], F32, f"x{a}{i}") for i in range(4)] for a in range(PASSES)]
+        picked = [sbuf([P, 4, S], F32, f"picked{a}") for a in range(PASSES)]
+        x_grouped = [sbuf([P, S, 4], BF16, f"xgrouped{a}") for a in range(PASSES)]
+        x_codes = [sbuf([P, S], U32, f"xcodes{a}") for a in range(PASSES)]
+        x_scales = [sbuf([P, S], U8, f"xscales{a}") for a in range(PASSES)]
         whole, halves = [(0, P)], [(0, P // 2), (P // 2, P)]
         d_pieces = [whole] * LAST + [halves]
-        d_raw = {}
-        for a in range(PASSES):
-            for m0, m1 in d_pieces[a]:
-                d_raw[a, m0] = keep.tile([P, 4, 4 * (m1 - m0)], F32, name=f"draw{a}{m0}", align_bytes=ALIGN)
-        d_grouped = [keep.tile([P, R * 4], BF16, name=f"dgrouped{a}", align_bytes=ALIGN) for a in range(PASSES)]
-        d_codes = [keep.tile([P, R], U32, name=f"dcodes{a}", align_bytes=ALIGN) for a in range(PASSES)]
-        d_scales = [keep.tile([P, R], U8, name=f"dscales{a}", align_bytes=ALIGN) for a in range(PASSES)]
-        u_raw = [keep.tile([P, 4, U_COLS], F32, name=f"uraw{c}", align_bytes=ALIGN) for c in range(QUARTERS)]
+        d_raw = {(a, m0): sbuf([P, 4, 4 * (m1 - m0)], F32, f"draw{a}{m0}") for a in range(PASSES) for m0, m1 in d_pieces[a]}
+        d_grouped = [sbuf([P, R * 4], BF16, f"dgrouped{a}") for a in range(PASSES)]
+        d_codes = [sbuf([P, R], U32, f"dcodes{a}") for a in range(PASSES)]
+        d_scales = [sbuf([P, R], U8, f"dscales{a}") for a in range(PASSES)]
+        u_raw = [sbuf([P, 4, U_COLS], F32, f"uraw{c}") for c in range(QUARTERS)]
         u_grouped = {}
-        u_codes = [keep.tile([P, U_COLS], U32, name=f"ucodes{c}", align_bytes=ALIGN) for c in range(QUARTERS)]
-        u_scales = [keep.tile([P, U_COLS], U8, name=f"uscales{c}", align_bytes=ALIGN) for c in range(QUARTERS)]
+        u_codes = [sbuf([P, U_COLS], U32, f"ucodes{c}") for c in range(QUARTERS)]
+        u_scales = [sbuf([P, U_COLS], U8, f"uscales{c}") for c in range(QUARTERS)]
         w_codes = {}
-        w_scales = keep.tile([P, PASSES, M], U8, name="wscales", align_bytes=ALIGN)
-        h_codes = keep.tile([P, S], U32, name="hcodes", align_bytes=ALIGN)
-        h_scales = keep.tile([P, S], U8, name="hscales", align_bytes=ALIGN)
+        w_scales = sbuf([P, PASSES, M], U8, "wscales")
+        h_grouped = [sbuf([P, HALF, 4], BF16, f"hgrouped{half}") for half in range(2)]
+        h_codes = sbuf([P, S], U32, "hcodes")
+        h_scales = sbuf([P, S], U8, "hscales")
 
-        nc.sync.dma_start(offsets[:], offs)
-        nc.gpsimd.memset(w_scales[:].bitcast(I32), 0)
-        for q in range(4):
-            nc.gpsimd.dma_start(
-                out=w_scales[32 * q : 32 * q + 4].bitcast(I32),
-                in_=w4_scales[:, 4 * q : 4 * q + 4, :].bitcast(I32).rearrange("a q c -> q a c"),
-            )
+        def load_scales():
+            rows = w4_scales.bitcast(I32).rearrange("a q c -> q a c")
+            for q in range(4):
+                nc.gpsimd.dma_start(out=w_scales[32 * q : 32 * q + 4].bitcast(I32), in_=rows[4 * q : 4 * q + 4])
 
         def load_x(a, *planes):
             rows = xT[512 * a : 512 * a + 512, :].rearrange("(p i) c -> p i c", i=4)
@@ -82,7 +80,7 @@ def tile_list_hlora_none_kernel(tc, xT, w4_words, w4_scales, down, up, wgt, offs
                 nc.sync.dma_start(out=d_raw[a, m0][:], in_=rows.rearrange("(p i) r -> p i r", i=4))
 
         def load_w(group, a0, a1):
-            piece = keep.tile([P, a1 - a0, 2 * P * EARLY], U8, name=f"wcodes{group}{a0}", align_bytes=ALIGN)
+            piece = sbuf([P, a1 - a0, 2 * P * EARLY], U8, f"wcodes{group}{a0}")
             for a in range(a0, a1):
                 w_codes[group, a] = piece[:, a - a0, :]
             per_group = 2 * P * EARLY // 4
@@ -94,6 +92,9 @@ def tile_list_hlora_none_kernel(tc, xT, w4_words, w4_scales, down, up, wgt, offs
             for c in quarters:
                 nc.sync.dma_start(out=u_raw[c][:], in_=rows[:, :, U_COLS * c : U_COLS * c + U_COLS])
 
+        nc.sync.dma_start(offsets[:], offs)
+        nc.gpsimd.memset(w_scales[:].bitcast(I32), 0)
+        load_scales()
         load_x(0, 0)
         for c0 in (0, HALF):
             nc.sync.dma_start(weights[:, c0 : c0 + HALF], wgt[:, c0 : c0 + HALF])
@@ -126,7 +127,6 @@ def tile_list_hlora_none_kernel(tc, xT, w4_words, w4_scales, down, up, wgt, offs
             nc.vector.quantize_mx(out=codes.bitcast(E4M3), scales=scales, in_=grouped)
 
         def quantize_x(a):
-            x_codes[a] = keep.tile([P, S], U32, name=f"xcodes{a}", align_bytes=ALIGN)
             quantize(x_codes[a][:], x_scales[a][:], x_grouped[a][:].rearrange("p c i -> p (c i)"))
 
         def interleave_d(a):
@@ -141,12 +141,12 @@ def tile_list_hlora_none_kernel(tc, xT, w4_words, w4_scales, down, up, wgt, offs
             cols = slice(P * t0, P * t1)
             quantize(d_codes[a][:, cols], d_scales[a][:, cols], d_grouped[a][:, 4 * P * t0 : 4 * P * t1])
 
-        def interleave_u(c, copy, buffer):
-            u_grouped[c] = keep.tile([P, U_COLS, 4], BF16, name=buffer, align_bytes=ALIGN)
-            interleave(copy, u_grouped[c], u_raw[c], 0, U_COLS)
+        def interleave_u(c, c0, c1, copy, buffer):
+            u_grouped[c, c0] = sbuf([P, c1 - c0, 4], BF16, buffer)
+            interleave(copy, u_grouped[c, c0], u_raw[c][:, :, c0:c1], 0, c1 - c0)
 
-        def quantize_u(c):
-            quantize(u_codes[c][:], u_scales[c][:], u_grouped[c][:].rearrange("p c i -> p (c i)"))
+        def quantize_u(c, c0, c1):
+            quantize(u_codes[c][:, c0:c1], u_scales[c][:, c0:c1], u_grouped[c, c0][:].rearrange("p c i -> p (c i)"))
 
         h_bank = [psum.tile([P, 4, CHUNK], F32, name=f"bank{q}") for q in range(CHUNKS)]
 
@@ -163,38 +163,45 @@ def tile_list_hlora_none_kernel(tc, xT, w4_words, w4_scales, down, up, wgt, offs
                     stop=(a == LAST and t == 3),
                 )
 
-        out_bank = [f"acc{n}" for n in range(EARLY)] + [f"bank{q}" for q in range(TILES - EARLY - 1)] + [f"acc{EARLY - 1}"]
+        parts = [(0, 2, 0, HALF), (0, 2, HALF, HALF)] + [(n, 1, 0, S) for n in range(2, TILES - 1)] + [(TILES - 1, 1, 0, HALF), (TILES - 1, 1, HALF, HALF)]
+        part_bank = [f"acc{b}" for b in range(EARLY)] + [f"bank{q}" for q in range(CHUNKS - 1)] + [f"acc{EARLY - 1}", f"bank{CHUNKS - 1}"]
         acc = {}
 
-        def multiply_w4(n, a):
+        def multiply_w4(b, a):
+            n0, tiles, c0, width = parts[b]
             if a == 0:
-                acc[n] = psum.tile([P, S], F32, name=out_bank[n])
-            group, m = divmod(n, EARLY)
-            nc.tensor.matmul_mx(
-                out=acc[n][:],
-                lhsT=w_codes[group, a][:, 2 * P * m : 2 * P * (m + 1)].bitcast(E2M1),
-                lhsT_scale=w_scales[:, a, P * n : P * n + P],
-                rhs=x_codes[a][:].bitcast(E4M3),
-                rhs_scale=x_scales[a][:],
-                start=(a == 0),
-                stop=False,
-            )
+                acc[b] = psum.tile([P, tiles, width], F32, name=part_bank[b])
+            for n in range(n0, n0 + tiles):
+                group, m = divmod(n, EARLY)
+                nc.tensor.matmul_mx(
+                    out=acc[b][:, n - n0, :],
+                    lhsT=w_codes[group, a][:, 2 * P * m : 2 * P * (m + 1)].bitcast(E2M1),
+                    lhsT_scale=w_scales[:, a, P * n : P * n + P],
+                    rhs=x_codes[a][:, c0 : c0 + width].bitcast(E4M3),
+                    rhs_scale=x_scales[a][:, c0 : c0 + width],
+                    start=(a == 0 and n == n0),
+                    stop=False,
+                )
 
-        def close_and_store(n, copy, width):
-            c, first = divmod(P * n, U_COLS)
-            nc.tensor.matmul_mx(
-                out=acc[n][:],
-                lhsT=u_codes[c][:, first : first + P].bitcast(E4M3),
-                lhsT_scale=u_scales[c][:, first : first + P],
-                rhs=h_codes[:].bitcast(E4M3),
-                rhs_scale=h_scales[:],
-                start=False,
-                stop=True,
-            )
-            staged = keep.tile([P, S], F32, name=f"staged{n}", align_bytes=ALIGN)
-            for c0 in range(0, S, width):
-                copy(out=staged[:, c0 : c0 + width], in_=acc[n][:, c0 : c0 + width])
-                nc.sync.dma_start(out=out[P * n : P * n + P, c0 : c0 + width], in_=staged[:, c0 : c0 + width])
+        def close_and_store(b, copy, pieces):
+            n0, tiles, c0, width = parts[b]
+            for n in range(n0, n0 + tiles):
+                c, first = divmod(P * n, U_COLS)
+                nc.tensor.matmul_mx(
+                    out=acc[b][:, n - n0, :],
+                    lhsT=u_codes[c][:, first : first + P].bitcast(E4M3),
+                    lhsT_scale=u_scales[c][:, first : first + P],
+                    rhs=h_codes[:, c0 : c0 + width].bitcast(E4M3),
+                    rhs_scale=h_scales[:, c0 : c0 + width],
+                    start=False,
+                    stop=(n == n0 + tiles - 1),
+                )
+            staged = sbuf([P, tiles, width], F32, f"staged{b}")
+            rows = out[P * n0 : P * (n0 + tiles), c0 : c0 + width].rearrange("(n p) c -> p n c", p=P)
+            step = width // pieces
+            for e0 in range(0, width, step):
+                copy(out=staged[:, :, e0 : e0 + step], in_=acc[b][:, :, e0 : e0 + step])
+                nc.sync.dma_start(out=rows[:, :, e0 : e0 + step], in_=staged[:, :, e0 : e0 + step])
 
         for a in range(PASSES):
             for i in range(4):
@@ -206,7 +213,6 @@ def tile_list_hlora_none_kernel(tc, xT, w4_words, w4_scales, down, up, wgt, offs
             if a < LAST:
                 for c0 in (0, HALF):
                     interleave(on_scalar, x_grouped[a], picked[a], c0, c0 + HALF)
-        x_grouped.append(keep.tile([P, S, 4], BF16, name=f"xgrouped{LAST}", align_bytes=ALIGN))
         interleave(on_scalar, x_grouped[LAST], picked[LAST], 0, X_ON_SCALAR)
         interleave(on_vector, x_grouped[LAST], picked[LAST], X_ON_SCALAR, HALF)
         interleave(on_vector, x_grouped[LAST], picked[LAST], HALF, S)
@@ -220,11 +226,10 @@ def tile_list_hlora_none_kernel(tc, xT, w4_words, w4_scales, down, up, wgt, offs
         interleave_d(LAST)
         quantize_d(LAST, 0, 2)
         quantize_d(LAST, 2, 4)
-        u_grouped[0] = keep.tile([P, U_COLS, 4], BF16, name="ugrouped", align_bytes=ALIGN)
-        interleave(on_scalar, u_grouped[0], u_raw[0], 0, P)
-        interleave(on_vector, u_grouped[0], u_raw[0], P, U_COLS)
-        quantize_u(0)
-        h_grouped = [keep.tile([P, HALF, 4], BF16, name=f"hgrouped{half}", align_bytes=ALIGN) for half in range(2)]
+        u_grouped[0, 0] = sbuf([P, U_COLS, 4], BF16, "ugrouped")
+        interleave(on_scalar, u_grouped[0, 0], u_raw[0], 0, P)
+        interleave(on_vector, u_grouped[0, 0], u_raw[0], P, U_COLS)
+        quantize_u(0, 0, U_COLS)
         for q in range(CHUNKS):
             multiply_down(q, LAST)
             half, first = divmod(CHUNK * q, HALF)
@@ -235,17 +240,21 @@ def tile_list_hlora_none_kernel(tc, xT, w4_words, w4_scales, down, up, wgt, offs
             quantize(h_codes[:, cols], h_scales[:, cols], h_grouped[half][:].rearrange("p c t -> p (c t)"))
 
         for a in range(PASSES):
-            for n in range(EARLY):
-                multiply_w4(n, a)
-        interleave_u(1, on_scalar, f"dcodes{LAST}")
-        interleave_u(2, on_vector, "hgrouped1")
-        quantize_u(1)
-        quantize_u(2)
-        interleave_u(3, on_vector, f"dcodes{LAST}")
-        quantize_u(3)
-        for n in range(TILES):
-            if n >= EARLY:
-                for a in range(PASSES):
-                    multiply_w4(n, a)
-            copy = on_vector if n >= EARLY and n % 2 == 0 else on_scalar
-            close_and_store(n, copy, HALF if n == TILES - 1 else S)
+            for b in range(EARLY):
+                multiply_w4(b, a)
+        interleave_u(1, 0, P, on_scalar, f"dcodes{LAST}")
+        quantize_u(1, 0, P)
+        interleave_u(1, P, U_COLS, on_vector, "hgrouped1")
+        close_and_store(0, on_scalar, 1)
+        close_and_store(1, on_scalar, 1)
+        close_and_store(2, on_scalar, 1)
+        interleave_u(2, 0, U_COLS, on_vector, "ugrouped")
+        quantize_u(1, P, U_COLS)
+        close_and_store(3, on_scalar, 1)
+        quantize_u(2, 0, U_COLS)
+        interleave_u(3, 0, U_COLS, on_vector, "hgrouped0")
+        quantize_u(3, 0, U_COLS)
+        for b in range(EARLY, len(parts)):
+            for a in range(PASSES):
+                multiply_w4(b, a)
+            close_and_store(b, on_vector if b % 2 else on_scalar, 1)

@@ -28,7 +28,8 @@ QUARTERS = M // U_COLS
 ALIGN = 256
 
 X_ON_SCALAR = 192
-D_ON_SCALAR = (80, 48, 32)
+D_ON_SCALAR = (80, 48, 64)
+D_LAST_ON_VECTOR = 20
 
 
 def tile_list_hlora_none_kernel(tc, xT, w4_words, w4_scales, down, up, wgt, offs, out):
@@ -56,7 +57,7 @@ def tile_list_hlora_none_kernel(tc, xT, w4_words, w4_scales, down, up, wgt, offs
         d_scales = [sbuf([P, R], U8, f"dscales{a}") for a in range(PASSES)]
         u_raw = [sbuf([P, 4, U_COLS], F32, f"uraw{c}") for c in range(QUARTERS)]
         u_grouped = {}
-        u_codes = [sbuf([P, U_COLS], U32, f"ucodes{c}") for c in range(QUARTERS)]
+        u_codes = {}
         u_scales = [sbuf([P, U_COLS], U8, f"uscales{c}") for c in range(QUARTERS)]
         w_codes = {}
         w_scales = sbuf([P, PASSES, M], U8, "wscales")
@@ -109,9 +110,8 @@ def tile_list_hlora_none_kernel(tc, xT, w4_words, w4_scales, down, up, wgt, offs
         load_w(0, LAST, PASSES)
         load_d(LAST, *halves)
         load_u(0)
-        load_w(1, 0, LAST)
+        load_w(1, 0, PASSES)
         load_u(1, 2, 3)
-        load_w(1, LAST, PASSES)
 
         def gather(a, i, c0, c1):
             window = x_plane[a][i][:].indirect(offsets[:, c0 // 16 : c1 // 16])
@@ -134,7 +134,11 @@ def tile_list_hlora_none_kernel(tc, xT, w4_words, w4_scales, down, up, wgt, offs
                 target = d_grouped[a][:].rearrange("p (t m i) -> p m i t", t=4, i=4)[:, m0:m1]
                 source = d_raw[a, m0][:].rearrange("p i (m t) -> p m i t", t=4)
                 cut = D_ON_SCALAR[a] * (m1 - m0) // P
-                for copy, first, end, t0 in ((on_scalar, 0, m1 - m0, 2), (on_scalar, 0, cut, 0), (on_vector, cut, m1 - m0, 0)):
+                shares = [(on_scalar, 0, m1 - m0, 2), (on_scalar, 0, cut, 0), (on_vector, cut, m1 - m0, 0)]
+                if (a, m1) == (LAST, P):
+                    cut = m1 - m0 - D_LAST_ON_VECTOR
+                    shares = [(on_vector, 0, m1 - m0, 0), (on_scalar, 0, cut, 2), (on_vector, cut, m1 - m0, 2)]
+                for copy, first, end, t0 in shares:
                     copy(out=target[:, first:end, :, t0 : t0 + 2], in_=source[:, first:end, :, t0 : t0 + 2])
 
         def quantize_d(a, t0, t1):
@@ -164,7 +168,7 @@ def tile_list_hlora_none_kernel(tc, xT, w4_words, w4_scales, down, up, wgt, offs
                 )
 
         parts = [(0, 2, 0, HALF), (0, 2, HALF, HALF)] + [(n, 1, 0, S) for n in range(2, TILES - 1)] + [(TILES - 1, 1, 0, HALF), (TILES - 1, 1, HALF, HALF)]
-        part_bank = [f"acc{b}" for b in range(EARLY)] + [f"bank{q}" for q in range(CHUNKS - 1)] + [f"acc{EARLY - 1}", f"bank{CHUNKS - 1}"]
+        part_bank = [f"acc{b}" for b in range(EARLY)] + ["bank0", "bank3", "acc2", "acc3", "acc1"]
         acc = {}
 
         def multiply_w4(b, a):
@@ -226,15 +230,16 @@ def tile_list_hlora_none_kernel(tc, xT, w4_words, w4_scales, down, up, wgt, offs
         interleave_d(LAST)
         quantize_d(LAST, 0, 2)
         quantize_d(LAST, 2, 4)
-        u_grouped[0, 0] = sbuf([P, U_COLS, 4], BF16, "ugrouped")
-        interleave(on_scalar, u_grouped[0, 0], u_raw[0], 0, P)
-        interleave(on_vector, u_grouped[0, 0], u_raw[0], P, U_COLS)
-        quantize_u(0, 0, U_COLS)
+        interleave_u(0, 0, U_COLS, on_vector, "ugrouped")
         for q in range(CHUNKS):
             multiply_down(q, LAST)
             half, first = divmod(CHUNK * q, HALF)
-            copy = on_scalar if q % 2 else on_vector
+            copy = on_vector if q == 1 else on_scalar
             copy(out=h_grouped[half][:, first : first + CHUNK, :], in_=h_bank[q][:].rearrange("p t c -> p c t"))
+        u_codes[0] = sbuf([P, U_COLS], U32, f"dcodes{LAST}")
+        quantize_u(0, 0, U_COLS)
+        for c in range(1, QUARTERS):
+            u_codes[c] = sbuf([P, U_COLS], U32, f"ucodes{c}")
         for half in range(2):
             cols = slice(HALF * half, HALF * half + HALF)
             quantize(h_codes[:, cols], h_scales[:, cols], h_grouped[half][:].rearrange("p c t -> p (c t)"))
@@ -242,18 +247,13 @@ def tile_list_hlora_none_kernel(tc, xT, w4_words, w4_scales, down, up, wgt, offs
         for a in range(PASSES):
             for b in range(EARLY):
                 multiply_w4(b, a)
-        interleave_u(1, 0, P, on_scalar, f"dcodes{LAST}")
-        quantize_u(1, 0, P)
-        interleave_u(1, P, U_COLS, on_vector, "hgrouped1")
-        close_and_store(0, on_scalar, 1)
-        close_and_store(1, on_scalar, 1)
-        close_and_store(2, on_scalar, 1)
-        interleave_u(2, 0, U_COLS, on_vector, "ugrouped")
-        quantize_u(1, P, U_COLS)
-        close_and_store(3, on_scalar, 1)
-        quantize_u(2, 0, U_COLS)
-        interleave_u(3, 0, U_COLS, on_vector, "hgrouped0")
-        quantize_u(3, 0, U_COLS)
+        for c in range(1, QUARTERS):
+            for c0 in (0, P):
+                interleave_u(c, c0, c0 + P, on_vector, f"ugrouped{c}{c0}")
+            for c0 in (0, P):
+                quantize_u(c, c0, c0 + P)
+        for b in range(EARLY):
+            close_and_store(b, on_scalar, 1)
         for b in range(EARLY, len(parts)):
             for a in range(PASSES):
                 multiply_w4(b, a)

@@ -27,6 +27,8 @@ U_COLS = 256
 QUARTERS = M // U_COLS
 ALIGN = 256
 
+GROUP = 16
+BLOCK = 32
 X_ON_SCALAR = 192
 D_ON_SCALAR = (80, 48, 64)
 D_LAST_ON_VECTOR = 20
@@ -96,10 +98,9 @@ def tile_list_hlora_none_kernel(tc, xT, w4_words, w4_scales, down, up, wgt, offs
         nc.sync.dma_start(offsets[:], offs)
         nc.gpsimd.memset(w_scales[:].bitcast(I32), 0)
         load_scales()
-        load_x(0, 0)
-        for c0 in (0, HALF):
-            nc.sync.dma_start(weights[:, c0 : c0 + HALF], wgt[:, c0 : c0 + HALF])
-        load_x(0, 1, 2, 3)
+        w_part = sbuf([P, BLOCK], F32, "wpart")
+        nc.sync.dma_start(w_part[:], wgt.rearrange("(g r) (s c) -> g r s c", r=GROUP, c=BLOCK)[:, 0])
+        load_x(0, 0, 1, 2, 3)
         load_x(1, 0, 1, 2, 3)
         load_x(LAST, 0, 1)
         load_d(0, *whole)
@@ -168,7 +169,7 @@ def tile_list_hlora_none_kernel(tc, xT, w4_words, w4_scales, down, up, wgt, offs
                 )
 
         parts = [(0, 2, 0, HALF), (0, 2, HALF, HALF)] + [(n, 1, 0, S) for n in range(2, TILES - 1)] + [(TILES - 1, 1, 0, HALF), (TILES - 1, 1, HALF, HALF)]
-        part_bank = [f"acc{b}" for b in range(EARLY)] + ["bank0", "bank3", "acc2", "acc3", "acc1"]
+        part_bank = [f"acc{b}" for b in range(EARLY)] + ["bank0", "bank3", "acc2", "acc3", "acc0"]
         acc = {}
 
         def multiply_w4(b, a):
@@ -206,6 +207,17 @@ def tile_list_hlora_none_kernel(tc, xT, w4_words, w4_scales, down, up, wgt, offs
             for e0 in range(0, width, step):
                 copy(out=staged[:, :, e0 : e0 + step], in_=acc[b][:, :, e0 : e0 + step])
                 nc.sync.dma_start(out=rows[:, :, e0 : e0 + step], in_=staged[:, :, e0 : e0 + step])
+
+        w_turned = sbuf([P, BLOCK], F32, "wturned")
+        nc.vector.transpose(w_turned[:], w_part[:])
+        w_repeated = sbuf([P, S], F32, "wrepeated")
+        runs = HALF // BLOCK
+        for half in range(2):
+            source = w_turned[:].rearrange("p (g s) -> p s g", g=2)[:, runs * half : runs * (half + 1)]
+            target = w_repeated[:, HALF * half : HALF * (half + 1)].rearrange("p (s g r) -> p s g r", g=2, r=GROUP)
+            on_vector(out=target, in_=source.unsqueeze(3).to_broadcast([P, runs, 2, GROUP]))
+        for c0 in (0, HALF):
+            nc.vector.transpose(weights[:, c0 : c0 + HALF], w_repeated[:, c0 : c0 + HALF])
 
         for a in range(PASSES):
             for i in range(4):

@@ -29,9 +29,8 @@ ALIGN = 256
 
 GROUP = 16
 BLOCK = 32
-X_ON_SCALAR = 192
-D_ON_SCALAR = (80, 48, 64)
-D_LAST_ON_VECTOR = 20
+X_ON_SCALAR = 96
+D_ON_SCALAR = (80, 64)
 
 
 def tile_list_hlora_none_kernel(tc, xT, w4_words, w4_scales, down, up, wgt, offs, out):
@@ -127,20 +126,14 @@ def tile_list_hlora_none_kernel(tc, xT, w4_words, w4_scales, down, up, wgt, offs
         def quantize(codes, scales, grouped):
             nc.vector.quantize_mx(out=codes.bitcast(E4M3), scales=scales, in_=grouped)
 
-        def quantize_x(a):
-            quantize(x_codes[a][:], x_scales[a][:], x_grouped[a][:].rearrange("p c i -> p (c i)"))
+        def quantize_x(a, c0, c1):
+            quantize(x_codes[a][:, c0:c1], x_scales[a][:, c0:c1], x_grouped[a][:, c0:c1, :].rearrange("p c i -> p (c i)"))
 
-        def interleave_d(a):
-            for m0, m1 in d_pieces[a]:
-                target = d_grouped[a][:].rearrange("p (t m i) -> p m i t", t=4, i=4)[:, m0:m1]
-                source = d_raw[a, m0][:].rearrange("p i (m t) -> p m i t", t=4)
-                cut = D_ON_SCALAR[a] * (m1 - m0) // P
-                shares = [(on_scalar, 0, m1 - m0, 2), (on_scalar, 0, cut, 0), (on_vector, cut, m1 - m0, 0)]
-                if (a, m1) == (LAST, P):
-                    cut = m1 - m0 - D_LAST_ON_VECTOR
-                    shares = [(on_vector, 0, m1 - m0, 0), (on_scalar, 0, cut, 2), (on_vector, cut, m1 - m0, 2)]
-                for copy, first, end, t0 in shares:
-                    copy(out=target[:, first:end, :, t0 : t0 + 2], in_=source[:, first:end, :, t0 : t0 + 2])
+        def interleave_d(a, piece, copy, first, end, t0):
+            m0, m1 = piece
+            target = d_grouped[a][:].rearrange("p (t m i) -> p m i t", t=4, i=4)[:, m0:m1]
+            source = d_raw[a, m0][:].rearrange("p i (m t) -> p m i t", t=4)
+            copy(out=target[:, first:end, :, t0 : t0 + 2], in_=source[:, first:end, :, t0 : t0 + 2])
 
         def quantize_d(a, t0, t1):
             cols = slice(P * t0, P * t1)
@@ -157,14 +150,14 @@ def tile_list_hlora_none_kernel(tc, xT, w4_words, w4_scales, down, up, wgt, offs
 
         def multiply_down(q, a):
             cols = slice(CHUNK * q, CHUNK * q + CHUNK)
-            for t in range(4):
+            for t in (0, 1, 2, 3) if a == LAST else (2, 3, 0, 1):
                 nc.tensor.matmul_mx(
                     out=h_bank[q][:, t, :],
                     lhsT=d_codes[a][:, P * t : P * t + P].bitcast(E4M3),
                     lhsT_scale=d_scales[a][:, P * t : P * t + P],
                     rhs=x_codes[a][:, cols].bitcast(E4M3),
                     rhs_scale=x_scales[a][:, cols],
-                    start=(a == 0 and t == 0),
+                    start=(a == 0 and t == 2),
                     stop=(a == LAST and t == 3),
                 )
 
@@ -225,23 +218,29 @@ def tile_list_hlora_none_kernel(tc, xT, w4_words, w4_scales, down, up, wgt, offs
                 for c0 in range(0, S, width):
                     gather(a, i, c0, c0 + width)
                 if a > 0 and i == 0:
-                    quantize_x(a - 1)
+                    quantize_x(a - 1, 0, S)
             if a < LAST:
                 for c0 in (0, HALF):
                     interleave(on_scalar, x_grouped[a], picked[a], c0, c0 + HALF)
         interleave(on_scalar, x_grouped[LAST], picked[LAST], 0, X_ON_SCALAR)
         interleave(on_vector, x_grouped[LAST], picked[LAST], X_ON_SCALAR, HALF)
         interleave(on_vector, x_grouped[LAST], picked[LAST], HALF, S)
-        quantize_x(LAST)
+        for c0 in (0, HALF):
+            quantize_x(LAST, c0, c0 + HALF)
 
         for a in range(LAST):
-            interleave_d(a)
-            quantize_d(a, 0, 4)
+            interleave_d(a, whole[0], on_scalar, 0, P, 2)
+            interleave_d(a, whole[0], on_scalar, 0, D_ON_SCALAR[a], 0)
+            interleave_d(a, whole[0], on_vector, D_ON_SCALAR[a], P, 0)
+            for t0, t1 in ((0, 4),) if a == 0 else ((2, 4), (0, 2)):
+                quantize_d(a, t0, t1)
             for q in range(CHUNKS):
                 multiply_down(q, a)
-        interleave_d(LAST)
-        quantize_d(LAST, 0, 2)
-        quantize_d(LAST, 2, 4)
+        for piece, copy in zip(halves, (on_scalar, on_vector)):
+            for t0 in (0, 2):
+                interleave_d(LAST, piece, copy, 0, P // 2, t0)
+        for t in range(4):
+            quantize_d(LAST, t, t + 1)
         interleave_u(0, 0, U_COLS, on_vector, "ugrouped")
         for q in range(CHUNKS):
             multiply_down(q, LAST)

@@ -68,8 +68,8 @@ def tile_list_hlora_none_kernel(tc, xT, w4_words, w4_scales, down, up, wgt, offs
 
         def load_scales():
             rows = w4_scales.bitcast(I32).rearrange("a q c -> q a c")
-            for q in range(4):
-                nc.gpsimd.dma_start(out=w_scales[32 * q : 32 * q + 4].bitcast(I32), in_=rows[4 * q : 4 * q + 4])
+            for q in (0, 2, 1, 3):
+                nc.scalar.dma_start(out=w_scales[32 * q : 32 * q + 4].bitcast(I32), in_=rows[4 * q : 4 * q + 4])
 
         def load_x(a, *planes):
             rows = xT[512 * a : 512 * a + 512, :].rearrange("(p i) c -> p i c", i=4)
@@ -95,7 +95,6 @@ def tile_list_hlora_none_kernel(tc, xT, w4_words, w4_scales, down, up, wgt, offs
                 nc.sync.dma_start(out=u_raw[c][:], in_=rows[:, :, U_COLS * c : U_COLS * c + U_COLS])
 
         nc.sync.dma_start(offsets[:], offs)
-        nc.gpsimd.memset(w_scales[:].bitcast(I32), 0)
         load_scales()
         w_part = sbuf([P, BLOCK], F32, "wpart")
         nc.sync.dma_start(w_part[:], wgt.rearrange("(g r) (s c) -> g r s c", r=GROUP, c=BLOCK)[:, 0])

@@ -23,14 +23,14 @@ EARLY = 4
 CHUNK = 128
 CHUNKS = S // CHUNK
 HALF = S // 2
-U_COLS = 256
-QUARTERS = M // U_COLS
 ALIGN = 256
-
 GROUP = 16
 BLOCK = 32
-X_ON_SCALAR = 96
-D_ON_SCALAR = (80, 64)
+
+U_PIECES = ((0, 2), (2, 4), (4, 6), (6, 8))
+X_ON_SCALAR = 176
+D_ON_SCALAR = ((80, 128), (32, 128))
+D_LAST_CUT = 96
 
 
 def tile_list_hlora_none_kernel(tc, xT, w4_words, w4_scales, down, up, wgt, offs, out):
@@ -44,22 +44,20 @@ def tile_list_hlora_none_kernel(tc, xT, w4_words, w4_scales, down, up, wgt, offs
             return keep.tile(shape, dtype, name=name, align_bytes=ALIGN)
 
         offsets = keep.tile([P, S // 16], U16, name="offsets")
+        w_part = sbuf([P, BLOCK], F32, "wpart")
         weights = sbuf([P, S], F32, "weights")
         x_plane = [[sbuf([P, T], F32, f"x{a}{i}") for i in range(4)] for a in range(PASSES)]
         picked = [sbuf([P, 4, S], F32, f"picked{a}") for a in range(PASSES)]
         x_grouped = [sbuf([P, S, 4], BF16, f"xgrouped{a}") for a in range(PASSES)]
         x_codes = [sbuf([P, S], U32, f"xcodes{a}") for a in range(PASSES)]
         x_scales = [sbuf([P, S], U8, f"xscales{a}") for a in range(PASSES)]
-        whole, halves = [(0, P)], [(0, P // 2), (P // 2, P)]
-        d_pieces = [whole] * LAST + [halves]
-        d_raw = {(a, m0): sbuf([P, 4, 4 * (m1 - m0)], F32, f"draw{a}{m0}") for a in range(PASSES) for m0, m1 in d_pieces[a]}
-        d_grouped = [sbuf([P, R * 4], BF16, f"dgrouped{a}") for a in range(PASSES)]
+        d_pieces = [(a, 0, P) for a in range(LAST)] + [(LAST, 0, P // 2), (LAST, P // 2, P)]
+        d_raw = {(a, m0): sbuf([P, 4, 4 * (m1 - m0)], F32, f"draw{a}{m0}") for a, m0, m1 in d_pieces}
+        d_grouped = [sbuf([P, 4, P, 4], BF16, f"dgrouped{a}") for a in range(PASSES)]
         d_codes = [sbuf([P, R], U32, f"dcodes{a}") for a in range(PASSES)]
         d_scales = [sbuf([P, R], U8, f"dscales{a}") for a in range(PASSES)]
-        u_raw = [sbuf([P, 4, U_COLS], F32, f"uraw{c}") for c in range(QUARTERS)]
-        u_grouped = {}
-        u_codes = {}
-        u_scales = [sbuf([P, U_COLS], U8, f"uscales{c}") for c in range(QUARTERS)]
+        u_raw = {n0: sbuf([P, 4, P * (n1 - n0)], F32, f"uraw{n0}") for n0, n1 in U_PIECES}
+        u_grouped, u_codes, u_scales = {}, {}, {}
         w_codes = {}
         w_scales = sbuf([P, PASSES, M], U8, "wscales")
         h_grouped = [sbuf([P, HALF, 4], BF16, f"hgrouped{half}") for half in range(2)]
@@ -67,101 +65,111 @@ def tile_list_hlora_none_kernel(tc, xT, w4_words, w4_scales, down, up, wgt, offs
         h_scales = sbuf([P, S], U8, "hscales")
 
         def load_scales():
-            rows = w4_scales.bitcast(I32).rearrange("a q c -> q a c")
-            for q in (0, 2, 1, 3):
-                nc.scalar.dma_start(out=w_scales[32 * q : 32 * q + 4].bitcast(I32), in_=rows[4 * q : 4 * q + 4])
+            rows = w4_scales.bitcast(I32).rearrange("a (q r) c -> r q a c", r=4)
+            for r in range(4):
+                nc.scalar.dma_start(out=w_scales[r:P:32].bitcast(I32), in_=rows[r])
 
         def load_x(a, *planes):
             rows = xT[512 * a : 512 * a + 512, :].rearrange("(p i) c -> p i c", i=4)
             for i in planes:
                 nc.sync.dma_start(out=x_plane[a][i][:], in_=rows[:, i, :])
 
-        def load_d(a, *pieces):
-            for m0, m1 in pieces:
-                rows = down[512 * a : 512 * a + 512, 4 * m0 : 4 * m1]
-                nc.sync.dma_start(out=d_raw[a, m0][:], in_=rows.rearrange("(p i) r -> p i r", i=4))
+        def load_d(a, m0, m1):
+            rows = down[512 * a : 512 * a + 512, 4 * m0 : 4 * m1]
+            nc.sync.dma_start(out=d_raw[a, m0][:], in_=rows.rearrange("(p i) r -> p i r", i=4))
 
-        def load_w(group, a0, a1):
-            piece = sbuf([P, a1 - a0, 2 * P * EARLY], U8, f"wcodes{group}{a0}")
+        def load_w(n0, n1, a0, a1):
+            piece = sbuf([P, a1 - a0, 2 * P * (n1 - n0)], U8, f"wcodes{n0}{a0}")
             for a in range(a0, a1):
-                w_codes[group, a] = piece[:, a - a0, :]
-            per_group = 2 * P * EARLY // 4
+                for n in range(n0, n1):
+                    w_codes[n, a] = piece[:, a - a0, 2 * P * (n - n0) : 2 * P * (n - n0 + 1)]
+            per_tile = 2 * P // 4
             words = w4_words.bitcast(I32).rearrange("a p c -> p a c")
-            nc.sync.dma_start(out=piece[:].bitcast(I32), in_=words[:, a0:a1, per_group * group : per_group * (group + 1)])
+            nc.sync.dma_start(out=piece[:].bitcast(I32), in_=words[:, a0:a1, per_tile * n0 : per_tile * n1])
 
-        def load_u(*quarters):
-            rows = up.rearrange("(p i) n -> p i n", i=4)
-            for c in quarters:
-                nc.sync.dma_start(out=u_raw[c][:], in_=rows[:, :, U_COLS * c : U_COLS * c + U_COLS])
+        def load_u(n0, n1):
+            nc.sync.dma_start(out=u_raw[n0][:], in_=up.rearrange("(p i) n -> p i n", i=4)[:, :, P * n0 : P * n1])
 
         nc.sync.dma_start(offsets[:], offs)
         load_scales()
-        w_part = sbuf([P, BLOCK], F32, "wpart")
         nc.sync.dma_start(w_part[:], wgt.rearrange("(g r) (s c) -> g r s c", r=GROUP, c=BLOCK)[:, 0])
         load_x(0, 0, 1, 2, 3)
         load_x(1, 0, 1, 2, 3)
         load_x(LAST, 0, 1)
-        load_d(0, *whole)
+        load_d(*d_pieces[0])
         load_x(LAST, 2)
-        load_w(0, 0, LAST)
+        load_w(0, EARLY, 0, LAST)
         load_x(LAST, 3)
-        load_d(1, *whole)
-        load_w(0, LAST, PASSES)
-        load_d(LAST, *halves)
-        load_u(0)
-        load_w(1, 0, PASSES)
-        load_u(1, 2, 3)
+        load_d(*d_pieces[1])
+        load_w(0, EARLY, LAST, PASSES)
+        load_d(*d_pieces[2])
+        load_d(*d_pieces[3])
+        load_u(0, 2)
+        load_w(4, 6, 0, PASSES)
+        load_u(2, 4)
+        load_u(4, 6)
+        load_u(6, 8)
+        load_w(6, 8, 0, PASSES)
 
         def gather(a, i, c0, c1):
             window = x_plane[a][i][:].indirect(offsets[:, c0 // 16 : c1 // 16])
             nc.vector.tensor_tensor(picked[a][:, i, c0:c1], window, weights[:, c0:c1], MULT)
 
-        def interleave(copy, grouped, planes, c0, c1):
+        def interleave(copy, grouped, planes):
             copy(
-                out=grouped[:, c0:c1, :].rearrange("p (c e) i -> p c i e", e=4),
-                in_=planes[:, :, c0:c1].rearrange("p i (c e) -> p c i e", e=4),
+                out=grouped.rearrange("p (c e) i -> p c i e", e=4),
+                in_=planes.rearrange("p i (c e) -> p c i e", e=4),
             )
 
         def quantize(codes, scales, grouped):
             nc.vector.quantize_mx(out=codes.bitcast(E4M3), scales=scales, in_=grouped)
 
+        def interleave_x(copy, a, c0, c1):
+            interleave(copy, x_grouped[a][:, c0:c1, :], picked[a][:, :, c0:c1])
+
         def quantize_x(a, c0, c1):
             quantize(x_codes[a][:, c0:c1], x_scales[a][:, c0:c1], x_grouped[a][:, c0:c1, :].rearrange("p c i -> p (c i)"))
 
-        def interleave_d(a, piece, copy, first, end, t0):
-            m0, m1 = piece
-            target = d_grouped[a][:].rearrange("p (t m i) -> p m i t", t=4, i=4)[:, m0:m1]
-            source = d_raw[a, m0][:].rearrange("p i (m t) -> p m i t", t=4)
-            copy(out=target[:, first:end, :, t0 : t0 + 2], in_=source[:, first:end, :, t0 : t0 + 2])
+        def interleave_d(copy, a, t0, m0, m1):
+            first = max(start for b, start, end in d_pieces if b == a and start <= m0)
+            target = d_grouped[a][:].rearrange("p t m i -> p m i t")
+            source = d_raw[a, first][:].rearrange("p i (m t) -> p m i t", t=4)
+            copy(out=target[:, m0:m1, :, t0 : t0 + 2], in_=source[:, m0 - first : m1 - first, :, t0 : t0 + 2])
 
         def quantize_d(a, t0, t1):
             cols = slice(P * t0, P * t1)
-            quantize(d_codes[a][:, cols], d_scales[a][:, cols], d_grouped[a][:, 4 * P * t0 : 4 * P * t1])
+            quantize(d_codes[a][:, cols], d_scales[a][:, cols], d_grouped[a][:, t0:t1].rearrange("p t m i -> p (t m i)"))
 
-        def interleave_u(c, c0, c1, copy, buffer):
-            u_grouped[c, c0] = sbuf([P, c1 - c0, 4], BF16, buffer)
-            interleave(copy, u_grouped[c, c0], u_raw[c][:, :, c0:c1], 0, c1 - c0)
+        def interleave_u(copy, n0, n1):
+            first = max(start for start, end in U_PIECES if start <= n0)
+            u_grouped[n0] = sbuf([P, P * (n1 - n0), 4], BF16, f"ugrouped{n0}")
+            interleave(copy, u_grouped[n0][:], u_raw[first][:, :, P * (n0 - first) : P * (n1 - first)])
 
-        def quantize_u(c, c0, c1):
-            quantize(u_codes[c][:, c0:c1], u_scales[c][:, c0:c1], u_grouped[c, c0][:].rearrange("p c i -> p (c i)"))
+        def quantize_u(n0, n1, buffer):
+            codes = sbuf([P, P * (n1 - n0)], U32, buffer)
+            scales = sbuf([P, P * (n1 - n0)], U8, f"uscales{n0}")
+            quantize(codes[:], scales[:], u_grouped[n0][:].rearrange("p c i -> p (c i)"))
+            for n in range(n0, n1):
+                u_codes[n] = codes[:, P * (n - n0) : P * (n - n0 + 1)]
+                u_scales[n] = scales[:, P * (n - n0) : P * (n - n0 + 1)]
 
         h_bank = [psum.tile([P, 4, CHUNK], F32, name=f"bank{q}") for q in range(CHUNKS)]
 
-        def multiply_down(q, a):
+        def multiply_down(q, a, order):
             cols = slice(CHUNK * q, CHUNK * q + CHUNK)
-            for t in (0, 1, 2, 3) if a == LAST else (2, 3, 0, 1):
+            for t in order:
                 nc.tensor.matmul_mx(
                     out=h_bank[q][:, t, :],
                     lhsT=d_codes[a][:, P * t : P * t + P].bitcast(E4M3),
                     lhsT_scale=d_scales[a][:, P * t : P * t + P],
                     rhs=x_codes[a][:, cols].bitcast(E4M3),
                     rhs_scale=x_scales[a][:, cols],
-                    start=(a == 0 and t == 2),
-                    stop=(a == LAST and t == 3),
+                    start=(a == 0 and t == order[0]),
+                    stop=(a == LAST and t == order[-1]),
                 )
 
         parts = [(0, 2, 0, HALF), (0, 2, HALF, HALF)] + [(n, 1, 0, S) for n in range(2, TILES - 1)] + [(TILES - 1, 1, 0, HALF), (TILES - 1, 1, HALF, HALF)]
-        part_bank = [f"acc{b}" for b in range(EARLY)] + ["bank0", "bank3", "acc2", "acc3", "acc0"]
+        part_bank = [f"acc{b}" for b in range(EARLY)] + ["bank1", "bank3", "bank0", "bank2", "acc0"]
         acc = {}
 
         def multiply_w4(b, a):
@@ -169,10 +177,9 @@ def tile_list_hlora_none_kernel(tc, xT, w4_words, w4_scales, down, up, wgt, offs
             if a == 0:
                 acc[b] = psum.tile([P, tiles, width], F32, name=part_bank[b])
             for n in range(n0, n0 + tiles):
-                group, m = divmod(n, EARLY)
                 nc.tensor.matmul_mx(
                     out=acc[b][:, n - n0, :],
-                    lhsT=w_codes[group, a][:, 2 * P * m : 2 * P * (m + 1)].bitcast(E2M1),
+                    lhsT=w_codes[n, a].bitcast(E2M1),
                     lhsT_scale=w_scales[:, a, P * n : P * n + P],
                     rhs=x_codes[a][:, c0 : c0 + width].bitcast(E4M3),
                     rhs_scale=x_scales[a][:, c0 : c0 + width],
@@ -180,14 +187,13 @@ def tile_list_hlora_none_kernel(tc, xT, w4_words, w4_scales, down, up, wgt, offs
                     stop=False,
                 )
 
-        def close_and_store(b, copy, pieces):
+        def close_and_store(b, copy):
             n0, tiles, c0, width = parts[b]
             for n in range(n0, n0 + tiles):
-                c, first = divmod(P * n, U_COLS)
                 nc.tensor.matmul_mx(
                     out=acc[b][:, n - n0, :],
-                    lhsT=u_codes[c][:, first : first + P].bitcast(E4M3),
-                    lhsT_scale=u_scales[c][:, first : first + P],
+                    lhsT=u_codes[n].bitcast(E4M3),
+                    lhsT_scale=u_scales[n],
                     rhs=h_codes[:, c0 : c0 + width].bitcast(E4M3),
                     rhs_scale=h_scales[:, c0 : c0 + width],
                     start=False,
@@ -195,10 +201,8 @@ def tile_list_hlora_none_kernel(tc, xT, w4_words, w4_scales, down, up, wgt, offs
                 )
             staged = sbuf([P, tiles, width], F32, f"staged{b}")
             rows = out[P * n0 : P * (n0 + tiles), c0 : c0 + width].rearrange("(n p) c -> p n c", p=P)
-            step = width // pieces
-            for e0 in range(0, width, step):
-                copy(out=staged[:, :, e0 : e0 + step], in_=acc[b][:, :, e0 : e0 + step])
-                nc.sync.dma_start(out=rows[:, :, e0 : e0 + step], in_=staged[:, :, e0 : e0 + step])
+            copy(out=staged[:], in_=acc[b][:])
+            nc.sync.dma_start(out=rows, in_=staged[:])
 
         w_turned = sbuf([P, BLOCK], F32, "wturned")
         nc.vector.transpose(w_turned[:], w_part[:])
@@ -213,43 +217,44 @@ def tile_list_hlora_none_kernel(tc, xT, w4_words, w4_scales, down, up, wgt, offs
 
         for a in range(PASSES):
             for i in range(4):
-                width = HALF if (a, i) == (0, 0) or i == 3 else S
+                width = CHUNK if (a, i) == (LAST, 3) else HALF if (a, i) == (0, 0) or i == 3 else S
                 for c0 in range(0, S, width):
                     gather(a, i, c0, c0 + width)
                 if a > 0 and i == 0:
                     quantize_x(a - 1, 0, S)
             if a < LAST:
                 for c0 in (0, HALF):
-                    interleave(on_scalar, x_grouped[a], picked[a], c0, c0 + HALF)
-        interleave(on_scalar, x_grouped[LAST], picked[LAST], 0, X_ON_SCALAR)
-        interleave(on_vector, x_grouped[LAST], picked[LAST], X_ON_SCALAR, HALF)
-        interleave(on_vector, x_grouped[LAST], picked[LAST], HALF, S)
+                    interleave_x(on_scalar, a, c0, c0 + HALF)
+        interleave_x(on_scalar, LAST, 0, CHUNK)
+        interleave_x(on_scalar, LAST, CHUNK, X_ON_SCALAR)
+        interleave_x(on_vector, LAST, X_ON_SCALAR, HALF)
+        interleave_x(on_vector, LAST, HALF, S)
         for c0 in (0, HALF):
             quantize_x(LAST, c0, c0 + HALF)
 
         for a in range(LAST):
-            interleave_d(a, whole[0], on_scalar, 0, P, 2)
-            interleave_d(a, whole[0], on_scalar, 0, D_ON_SCALAR[a], 0)
-            interleave_d(a, whole[0], on_vector, D_ON_SCALAR[a], P, 0)
+            low, high = D_ON_SCALAR[a]
+            interleave_d(on_scalar, a, 2, 0, high)
+            interleave_d(on_scalar, a, 0, 0, low)
+            interleave_d(on_vector, a, 0, low, P)
             for t0, t1 in ((0, 4),) if a == 0 else ((2, 4), (0, 2)):
                 quantize_d(a, t0, t1)
             for q in range(CHUNKS):
-                multiply_down(q, a)
-        for piece, copy in zip(halves, (on_scalar, on_vector)):
-            for t0 in (0, 2):
-                interleave_d(LAST, piece, copy, 0, P // 2, t0)
+                multiply_down(q, a, (2, 3, 0, 1))
+        for t0 in (0, 2):
+            interleave_d(on_scalar, LAST, t0, 0, P // 2)
+        interleave_d(on_vector, LAST, 0, P // 2, P)
+        interleave_d(on_vector, LAST, 2, P // 2, D_LAST_CUT)
+        interleave_d(on_scalar, LAST, 2, D_LAST_CUT, P)
         for t in range(4):
             quantize_d(LAST, t, t + 1)
-        interleave_u(0, 0, U_COLS, on_vector, "ugrouped")
+        interleave_u(on_vector, 0, 2)
         for q in range(CHUNKS):
-            multiply_down(q, LAST)
+            multiply_down(q, LAST, (0, 1, 2, 3))
             half, first = divmod(CHUNK * q, HALF)
             copy = on_vector if q == 1 else on_scalar
             copy(out=h_grouped[half][:, first : first + CHUNK, :], in_=h_bank[q][:].rearrange("p t c -> p c t"))
-        u_codes[0] = sbuf([P, U_COLS], U32, f"dcodes{LAST}")
-        quantize_u(0, 0, U_COLS)
-        for c in range(1, QUARTERS):
-            u_codes[c] = sbuf([P, U_COLS], U32, f"ucodes{c}")
+        quantize_u(0, 2, f"dcodes{LAST}")
         for half in range(2):
             cols = slice(HALF * half, HALF * half + HALF)
             quantize(h_codes[:, cols], h_scales[:, cols], h_grouped[half][:].rearrange("p c t -> p (c t)"))
@@ -257,14 +262,14 @@ def tile_list_hlora_none_kernel(tc, xT, w4_words, w4_scales, down, up, wgt, offs
         for a in range(PASSES):
             for b in range(EARLY):
                 multiply_w4(b, a)
-        for c in range(1, QUARTERS):
-            for c0 in (0, P):
-                interleave_u(c, c0, c0 + P, on_vector, f"ugrouped{c}{c0}")
-            for c0 in (0, P):
-                quantize_u(c, c0, c0 + P)
+        interleave_u(on_vector, 2, 3)
+        for n in range(2, TILES):
+            if n + 1 < TILES:
+                interleave_u(on_scalar if n + 1 == 3 else on_vector, n + 1, n + 2)
+            quantize_u(n, n + 1, f"ucodes{n}")
         for b in range(EARLY):
-            close_and_store(b, on_scalar, 1)
+            close_and_store(b, on_scalar)
         for b in range(EARLY, len(parts)):
             for a in range(PASSES):
                 multiply_w4(b, a)
-            close_and_store(b, on_vector if b % 2 else on_scalar, 1)
+            close_and_store(b, on_vector if b in (5, 8) else on_scalar)

@@ -233,6 +233,10 @@ def tile_list_hlora_none_kernel(tc, xT, w4_words, w4_scales, down, up, wgt, offs
             quantize_x(LAST, c0, c0 + HALF)
 
         for a in range(LAST):
+            for b in range(EARLY):
+                multiply_w4(b, a)
+
+        for a in range(LAST):
             low, high = D_ON_SCALAR[a]
             interleave_d(on_scalar, a, 2, 0, high)
             interleave_d(on_scalar, a, 0, 0, low)
@@ -259,9 +263,8 @@ def tile_list_hlora_none_kernel(tc, xT, w4_words, w4_scales, down, up, wgt, offs
             cols = slice(HALF * half, HALF * half + HALF)
             quantize(h_codes[:, cols], h_scales[:, cols], h_grouped[half][:].rearrange("p c t -> p (c t)"))
 
-        for a in range(PASSES):
-            for b in range(EARLY):
-                multiply_w4(b, a)
+        for b in range(EARLY):
+            multiply_w4(b, LAST)
         interleave_u(on_vector, 2, 3)
         for n in range(2, TILES):
             if n + 1 < TILES:

@@ -29,7 +29,7 @@ BLOCK = 32
 
 U_PIECES = ((0, 2), (2, 4), (4, 6), (6, 8))
 X_ON_SCALAR = 176
-D_ON_SCALAR = ((80, 128), (32, 128))
+D_ON_SCALAR = ((128, 128), (32, 128))
 D_LAST_CUT = 96
 
 
@@ -97,8 +97,8 @@ def tile_list_hlora_none_kernel(tc, xT, w4_words, w4_scales, down, up, wgt, offs
         load_x(1, 0, 1, 2, 3)
         load_x(LAST, 0, 1)
         load_d(*d_pieces[0])
-        load_x(LAST, 2)
         load_w(0, EARLY, 0, LAST)
+        load_x(LAST, 2)
         load_x(LAST, 3)
         load_d(*d_pieces[1])
         load_w(0, EARLY, LAST, PASSES)
@@ -240,7 +240,8 @@ def tile_list_hlora_none_kernel(tc, xT, w4_words, w4_scales, down, up, wgt, offs
             low, high = D_ON_SCALAR[a]
             interleave_d(on_scalar, a, 2, 0, high)
             interleave_d(on_scalar, a, 0, 0, low)
-            interleave_d(on_vector, a, 0, low, P)
+            if low < P:
+                interleave_d(on_vector, a, 0, low, P)
             for t0, t1 in ((0, 4),) if a == 0 else ((2, 4), (0, 2)):
                 quantize_d(a, t0, t1)
             for q in range(CHUNKS):

from contextlib import ExitStack

import concourse.mybir as mybir

K, R, M, T, S = 1536, 512, 1024, 1024, 512
FLOPS = 2 * S * (K * R + K * M + R * M)

F32 = mybir.dt.float32
BF16 = mybir.dt.bfloat16
U32 = mybir.dt.uint32
I32 = mybir.dt.int32
U16 = mybir.dt.uint16
U8 = mybir.dt.uint8
E4M3 = mybir.dt.float8_e4m3fn_x4
E2M1 = mybir.dt.float4_e2m1fn_x4
MULT = mybir.AluOpType.mult

P = 128
PASSES = K // 512
LAST = PASSES - 1
TILES = M // P
EARLY = 4
CHUNK = 128
CHUNKS = S // CHUNK
HALF = S // 2
ALIGN = 256
GROUP = 16
BLOCK = 32

U_PIECES = ((0, 2), (2, 4), (4, 6), (6, 8))
X_ON_SCALAR = 176
D_ON_SCALAR = ((128, 128), (32, 128))
D_LAST_CUT = 96


def tile_list_hlora_none_kernel(tc, xT, w4_words, w4_scales, down, up, wgt, offs, out):
    nc = tc.nc
    on_scalar, on_vector = nc.scalar.copy, nc.vector.tensor_copy
    with ExitStack() as ctx:
        keep = ctx.enter_context(tc.tile_pool(name="keep", bufs=1))
        psum = ctx.enter_context(tc.psum_pool(name="psum", bufs=1))

        def sbuf(shape, dtype, name):
            return keep.tile(shape, dtype, name=name, align_bytes=ALIGN)

        offsets = keep.tile([P, S // 16], U16, name="offsets")
        w_part = sbuf([P, BLOCK], F32, "wpart")
        weights = sbuf([P, S], F32, "weights")
        x_plane = [[sbuf([P, T], F32, f"x{a}{i}") for i in range(4)] for a in range(PASSES)]
        picked = [sbuf([P, 4, S], F32, f"picked{a}") for a in range(PASSES)]
        x_grouped = [sbuf([P, S, 4], BF16, f"xgrouped{a}") for a in range(PASSES)]
        x_codes = [sbuf([P, S], U32, f"xcodes{a}") for a in range(PASSES)]
        x_scales = [sbuf([P, S], U8, f"xscales{a}") for a in range(PASSES)]
        d_pieces = [(a, 0, P) for a in range(LAST)] + [(LAST, 0, P // 2), (LAST, P // 2, P)]
        d_raw = {(a, m0): sbuf([P, 4, 4 * (m1 - m0)], F32, f"draw{a}{m0}") for a, m0, m1 in d_pieces}
        d_grouped = [sbuf([P, 4, P, 4], BF16, f"dgrouped{a}") for a in range(PASSES)]
        d_codes = [sbuf([P, R], U32, f"dcodes{a}") for a in range(PASSES)]
        d_scales = [sbuf([P, R], U8, f"dscales{a}") for a in range(PASSES)]
        u_raw = {n0: sbuf([P, 4, P * (n1 - n0)], F32, f"uraw{n0}") for n0, n1 in U_PIECES}
        u_grouped, u_codes, u_scales = {}, {}, {}
        w_codes = {}
        w_scales = sbuf([P, PASSES, M], U8, "wscales")
        h_grouped = [sbuf([P, HALF, 4], BF16, f"hgrouped{half}") for half in range(2)]
        h_codes = sbuf([P, S], U32, "hcodes")
        h_scales = sbuf([P, S], U8, "hscales")

        def load_scales():
            rows = w4_scales.bitcast(I32).rearrange("a (q r) c -> r q a c", r=4)
            for r in range(4):
                nc.scalar.dma_start(out=w_scales[r:P:32].bitcast(I32), in_=rows[r])

        def load_x(a, *planes):
            rows = xT[512 * a : 512 * a + 512, :].rearrange("(p i) c -> p i c", i=4)
            for i in planes:
                nc.sync.dma_start(out=x_plane[a][i][:], in_=rows[:, i, :])

        def load_d(a, m0, m1):
            rows = down[512 * a : 512 * a + 512, 4 * m0 : 4 * m1]
            nc.sync.dma_start(out=d_raw[a, m0][:], in_=rows.rearrange("(p i) r -> p i r", i=4))

        def load_w(n0, n1, a0, a1):
            piece = sbuf([P, a1 - a0, 2 * P * (n1 - n0)], U8, f"wcodes{n0}{a0}")
            for a in range(a0, a1):
                for n in range(n0, n1):
                    w_codes[n, a] = piece[:, a - a0, 2 * P * (n - n0) : 2 * P * (n - n0 + 1)]
            per_tile = 2 * P // 4
            words = w4_words.bitcast(I32).rearrange("a p c -> p a c")
            nc.sync.dma_start(out=piece[:].bitcast(I32), in_=words[:, a0:a1, per_tile * n0 : per_tile * n1])

        def load_u(n0, n1):
            nc.sync.dma_start(out=u_raw[n0][:], in_=up.rearrange("(p i) n -> p i n", i=4)[:, :, P * n0 : P * n1])

        nc.sync.dma_start(offsets[:], offs)
        load_scales()
        nc.sync.dma_start(w_part[:], wgt.rearrange("(g r) (s c) -> g r s c", r=GROUP, c=BLOCK)[:, 0])
        load_x(0, 0, 1, 2, 3)
        load_x(1, 0, 1, 2, 3)
        load_x(LAST, 0, 1)
        load_d(*d_pieces[0])
        load_w(0, EARLY, 0, LAST)
        load_x(LAST, 2)
        load_x(LAST, 3)
        load_d(*d_pieces[1])
        load_w(0, EARLY, LAST, PASSES)
        load_d(*d_pieces[2])
        load_d(*d_pieces[3])
        load_u(0, 2)
        load_w(4, 6, 0, PASSES)
        load_u(2, 4)
        load_u(4, 6)
        load_u(6, 8)
        load_w(6, 8, 0, PASSES)

        def gather(a, i, c0, c1):
            window = x_plane[a][i][:].indirect(offsets[:, c0 // 16 : c1 // 16])
            nc.vector.tensor_tensor(picked[a][:, i, c0:c1], window, weights[:, c0:c1], MULT)

        def interleave(copy, grouped, planes):
            copy(
                out=grouped.rearrange("p (c e) i -> p c i e", e=4),
                in_=planes.rearrange("p i (c e) -> p c i e", e=4),
            )

        def quantize(codes, scales, grouped):
            nc.vector.quantize_mx(out=codes.bitcast(E4M3), scales=scales, in_=grouped)

        def interleave_x(copy, a, c0, c1):
            interleave(copy, x_grouped[a][:, c0:c1, :], picked[a][:, :, c0:c1])

        def quantize_x(a, c0, c1):
            quantize(x_codes[a][:, c0:c1], x_scales[a][:, c0:c1], x_grouped[a][:, c0:c1, :].rearrange("p c i -> p (c i)"))

        def interleave_d(copy, a, t0, m0, m1):
            first = max(start for b, start, end in d_pieces if b == a and start <= m0)
            target = d_grouped[a][:].rearrange("p t m i -> p m i t")
            source = d_raw[a, first][:].rearrange("p i (m t) -> p m i t", t=4)
            copy(out=target[:, m0:m1, :, t0 : t0 + 2], in_=source[:, m0 - first : m1 - first, :, t0 : t0 + 2])

        def quantize_d(a, t0, t1):
            cols = slice(P * t0, P * t1)
            quantize(d_codes[a][:, cols], d_scales[a][:, cols], d_grouped[a][:, t0:t1].rearrange("p t m i -> p (t m i)"))

        def interleave_u(copy, n0, n1):
            first = max(start for start, end in U_PIECES if start <= n0)
            u_grouped[n0] = sbuf([P, P * (n1 - n0), 4], BF16, f"ugrouped{n0}")
            interleave(copy, u_grouped[n0][:], u_raw[first][:, :, P * (n0 - first) : P * (n1 - first)])

        def quantize_u(n0, n1, buffer):
            codes = sbuf([P, P * (n1 - n0)], U32, buffer)
            scales = sbuf([P, P * (n1 - n0)], U8, f"uscales{n0}")
            quantize(codes[:], scales[:], u_grouped[n0][:].rearrange("p c i -> p (c i)"))
            for n in range(n0, n1):
                u_codes[n] = codes[:, P * (n - n0) : P * (n - n0 + 1)]
                u_scales[n] = scales[:, P * (n - n0) : P * (n - n0 + 1)]

        h_bank = [psum.tile([P, 4, CHUNK], F32, name=f"bank{q}") for q in range(CHUNKS)]

        def multiply_down(q, a, order):
            cols = slice(CHUNK * q, CHUNK * q + CHUNK)
            for t in order:
                nc.tensor.matmul_mx(
                    out=h_bank[q][:, t, :],
                    lhsT=d_codes[a][:, P * t : P * t + P].bitcast(E4M3),
                    lhsT_scale=d_scales[a][:, P * t : P * t + P],
                    rhs=x_codes[a][:, cols].bitcast(E4M3),
                    rhs_scale=x_scales[a][:, cols],
                    start=(a == 0 and t == order[0]),
                    stop=(a == LAST and t == order[-1]),
                )

        parts = [(0, 2, 0, HALF), (0, 2, HALF, HALF)] + [(n, 1, 0, S) for n in range(2, TILES - 1)] + [(TILES - 1, 1, 0, HALF), (TILES - 1, 1, HALF, HALF)]
        part_bank = [f"acc{b}" for b in range(EARLY)] + ["bank1", "bank3", "bank0", "bank2", "acc0"]
        acc = {}

        def multiply_w4(b, a):
            n0, tiles, c0, width = parts[b]
            if a == 0:
                acc[b] = psum.tile([P, tiles, width], F32, name=part_bank[b])
            for n in range(n0, n0 + tiles):
                nc.tensor.matmul_mx(
                    out=acc[b][:, n - n0, :],
                    lhsT=w_codes[n, a].bitcast(E2M1),
                    lhsT_scale=w_scales[:, a, P * n : P * n + P],
                    rhs=x_codes[a][:, c0 : c0 + width].bitcast(E4M3),
                    rhs_scale=x_scales[a][:, c0 : c0 + width],
                    start=(a == 0 and n == n0),
                    stop=False,
                )

        def close_and_store(b, copy):
            n0, tiles, c0, width = parts[b]
            for n in range(n0, n0 + tiles):
                nc.tensor.matmul_mx(
                    out=acc[b][:, n - n0, :],
                    lhsT=u_codes[n].bitcast(E4M3),
                    lhsT_scale=u_scales[n],
                    rhs=h_codes[:, c0 : c0 + width].bitcast(E4M3),
                    rhs_scale=h_scales[:, c0 : c0 + width],
                    start=False,
                    stop=(n == n0 + tiles - 1),
                )
            staged = sbuf([P, tiles, width], F32, f"staged{b}")
            rows = out[P * n0 : P * (n0 + tiles), c0 : c0 + width].rearrange("(n p) c -> p n c", p=P)
            copy(out=staged[:], in_=acc[b][:])
            nc.sync.dma_start(out=rows, in_=staged[:])

        w_turned = sbuf([P, BLOCK], F32, "wturned")
        nc.vector.transpose(w_turned[:], w_part[:])
        w_repeated = sbuf([P, S], F32, "wrepeated")
        runs = HALF // BLOCK
        for half in range(2):
            source = w_turned[:].rearrange("p (g s) -> p s g", g=2)[:, runs * half : runs * (half + 1)]
            target = w_repeated[:, HALF * half : HALF * (half + 1)].rearrange("p (s g r) -> p s g r", g=2, r=GROUP)
            on_vector(out=target, in_=source.unsqueeze(3).to_broadcast([P, runs, 2, GROUP]))
        for c0 in (0, HALF):
            nc.vector.transpose(weights[:, c0 : c0 + HALF], w_repeated[:, c0 : c0 + HALF])

        for a in range(PASSES):
            for i in range(4):
                width = CHUNK if (a, i) == (LAST, 3) else HALF if (a, i) == (0, 0) or i == 3 else S
                for c0 in range(0, S, width):
                    gather(a, i, c0, c0 + width)
                if a > 0 and i == 0:
                    quantize_x(a - 1, 0, S)
            if a < LAST:
                for c0 in (0, HALF):
                    interleave_x(on_scalar, a, c0, c0 + HALF)
        interleave_x(on_scalar, LAST, 0, CHUNK)
        interleave_x(on_scalar, LAST, CHUNK, X_ON_SCALAR)
        interleave_x(on_vector, LAST, X_ON_SCALAR, HALF)
        interleave_x(on_vector, LAST, HALF, S)
        for c0 in (0, HALF):
            quantize_x(LAST, c0, c0 + HALF)

        for a in range(LAST):
            for b in range(EARLY):
                multiply_w4(b, a)

        for a in range(LAST):
            low, high = D_ON_SCALAR[a]
            interleave_d(on_scalar, a, 2, 0, high)
            interleave_d(on_scalar, a, 0, 0, low)
            if low < P:
                interleave_d(on_vector, a, 0, low, P)
            for t0, t1 in ((0, 4),) if a == 0 else ((2, 4), (0, 2)):
                quantize_d(a, t0, t1)
            for q in range(CHUNKS):
                multiply_down(q, a, (2, 3, 0, 1))
        for t0 in (0, 2):
            interleave_d(on_scalar, LAST, t0, 0, P // 2)
        interleave_d(on_vector, LAST, 0, P // 2, P)
        interleave_d(on_vector, LAST, 2, P // 2, D_LAST_CUT)
        interleave_d(on_scalar, LAST, 2, D_LAST_CUT, P)
        for t in range(4):
            quantize_d(LAST, t, t + 1)
        interleave_u(on_vector, 0, 2)
        for q in range(CHUNKS):
            multiply_down(q, LAST, (0, 1, 2, 3))
            half, first = divmod(CHUNK * q, HALF)
            copy = on_vector if q == 1 else on_scalar
            copy(out=h_grouped[half][:, first : first + CHUNK, :], in_=h_bank[q][:].rearrange("p t c -> p c t"))
        quantize_u(0, 2, f"dcodes{LAST}")
        for half in range(2):
            cols = slice(HALF * half, HALF * half + HALF)
            quantize(h_codes[:, cols], h_scales[:, cols], h_grouped[half][:].rearrange("p c t -> p (c t)"))

        for b in range(EARLY):
            multiply_w4(b, LAST)
        interleave_u(on_vector, 2, 3)
        for n in range(2, TILES):
            if n + 1 < TILES:
                interleave_u(on_scalar if n + 1 == 3 else on_vector, n + 1, n + 2)
            quantize_u(n, n + 1, f"ucodes{n}")
        for b in range(EARLY):
            close_and_store(b, on_scalar)
        for b in range(EARLY, len(parts)):
            for a in range(PASSES):
                multiply_w4(b, a)
            close_and_store(b, on_vector if b in (5, 8) else on_scalar)
